import numpy as np
import ml_dtypes


def mxq(x, axis, fmt="e4m3"):
    dtype, down = {"e4m3": (ml_dtypes.float8_e4m3fn, 7), "e5m2": (ml_dtypes.float8_e5m2, 14)}[fmt]
    v = np.moveaxis(np.asarray(x, np.float32).astype(ml_dtypes.bfloat16).astype(np.float64), axis, -1)
    blocks = v.reshape(v.shape[:-1] + (-1, 32))
    amax = np.abs(blocks).max(-1, keepdims=True)
    byte = np.maximum(np.where(amax > 0, np.frexp(amax)[1] - 1 + 127, 0) - down, 1)
    scale = np.exp2(byte - 127.0)
    codes = (blocks / scale).astype(np.float32).astype(dtype).astype(np.float64)
    return np.moveaxis((codes * scale).reshape(v.shape), -1, axis)


WIDE = False


def mx_kscale(k):
    if not WIDE:
        return np.ones(k)
    levels = np.array([10, -10, 5, -5, 0])
    if k % 512:
        return np.exp2(np.random.permutation(np.resize(levels, k // 32))).repeat(32)
    a = np.empty((k // 512, 16))
    for p in range(k // 512):
        a[p, :8] = np.random.permutation(np.resize(levels, 8))
        for g in range(8):
            far = levels[np.abs(levels - a[p, g]) >= 10]
            a[p, g + 8] = far[np.random.randint(len(far))]
    return np.exp2(a.ravel()).repeat(32)


def f64(x):
    return np.asarray(x).astype(np.float64)


def striped(idx):
    return np.tile(np.asarray(idx).reshape(-1, 16).T, (8, 1)).astype(np.uint16)


def unstriped(offs):
    return offs[:16].T.reshape(-1).astype(np.int64)


E2M1 = np.array([0.0, 0.5, 1.0, 1.5, 2.0, 3.0, 4.0, 6.0, -0.0, -0.5, -1.0, -1.5, -2.0, -3.0, -4.0, -6.0])


def pack_weight(w, fmt):
    k, n = w.shape
    w = f64(np.asarray(w, np.float32).astype(ml_dtypes.bfloat16)).reshape(k // 32, 32, n)
    amax = np.abs(w).max(1)
    if fmt == "e4m3":
        byte = np.frexp(amax)[1] - 1 + 127 - 7
    else:
        mant, ex = np.frexp(amax / 6.0)
        byte = np.where(mant > 0.5, ex, ex - 1) + 127
    byte = np.clip(np.where(amax > 0, byte, 1), 1, 254)
    scaled = (w * np.exp2(127.0 - byte)[:, None, :]).reshape(k, n).astype(np.float32)
    by_word = np.ascontiguousarray(scaled.reshape(k // 512, 128, 4, n).transpose(0, 1, 3, 2))
    if fmt == "e4m3":
        words = by_word.astype(ml_dtypes.float8_e4m3fn).view(np.uint8)
    else:
        c = by_word.astype(ml_dtypes.float4_e2m1fn).view(np.uint8) & 0xF
        words = (c[..., 0::2] | (c[..., 1::2] << 4)).reshape(k // 512, 128, 2 * n)
    return np.ascontiguousarray(words), np.ascontiguousarray(byte.astype(np.uint8).reshape(k // 512, 16, n))


def unpack_weight(words, scales, fmt):
    g, _, n = scales.shape
    words = np.ascontiguousarray(words).reshape(g, 128, n, -1)
    if fmt == "e4m3":
        vals = words.view(ml_dtypes.float8_e4m3fn).astype(np.float64)
    else:
        nib = np.empty((g, 128, n, 4), np.uint8)
        nib[..., 0::2] = words & 0xF
        nib[..., 1::2] = words >> 4
        vals = E2M1[nib]
    vals = vals * np.repeat(np.exp2(scales.astype(np.float64) - 127.0), 8, axis=1)[..., None]
    return vals.transpose(0, 1, 3, 2).reshape(g * 512, n)


B, N, T, D, DV, NQ = 2, 512, 2048, 512, 256, 128


def setup_inputs():
    n = np.random.standard_normal
    seg = T // B
    idx = np.concatenate([b * seg + np.random.permutation(seg)[:N] for b in range(B)])
    s = mx_kscale(D)[:, None]
    u = np.ones(T)
    u[idx] = mx_kscale(B * N)
    r = np.random.uniform(0.5, 2.0, T)
    k = n((D, T)) / s
    v = n((DV, T)) / (u * r)
    kp = pack_weight(k, "e4m3")
    return {
        "qT": (n((B, D, NQ)) * s * (1.00 / np.sqrt(D))).astype(np.float32),
        "k_words": kp[0],
        "k_scales": kp[1],
        "vT": v.astype(np.float32),
        "vs": np.tile(u * r, (128, 1)).astype(np.float32),
        "offs": striped(idx),
    }


def reference(qT, k_words, k_scales, vT, vs, offs):
    idx = unstriped(offs)
    k = unpack_weight(k_words, k_scales, "e4m3")
    v = f64(vT)
    pick = lambda x: x[:, idx].reshape(x.shape[0], B, N).transpose(1, 0, 2)
    q = f64(qT)
    score = mxq(q, 1, "e4m3").transpose(0, 2, 1) @ pick(k)
    p = score / (1.0 + np.exp(-score))
    w = p * pick(f64(vs))[:, :1, :]
    y = mxq(w, 2, "e4m3") @ mxq(pick(v).transpose(0, 2, 1), 1, "e4m3")
    y = y / 16.0
    return y

@@ -1,0 +1,191 @@
+from contextlib import ExitStack
+
+import concourse.mybir as mybir
+from concourse.masks import make_identity
+
+B, N, T, D, DV, NQ = 2, 512, 2048, 512, 256, 128
+FLOPS = 2 * B * NQ * N * (D + DV)
+BYTES = 4 * B * D * NQ + 4 * 128 * T + 16 * T + 4 * DV * T + 4 * T + 2 * 128 * 64 + 4 * B * NQ * DV
+
+F32 = mybir.dt.float32
+BF16 = mybir.dt.bfloat16
+I32 = mybir.dt.int32
+U32 = mybir.dt.uint32
+U16 = mybir.dt.uint16
+U8 = mybir.dt.uint8
+FP8X4 = mybir.dt.float8_e4m3fn_x4
+ACT = mybir.ActivationFunctionType
+MULT = mybir.AluOpType.mult
+
+P = 128
+PACK = 4
+SEG = T // B
+COLS = N // 16
+CHUNK = 512
+
+
+def by_slot(t):
+    return t.rearrange("x t (j r) -> x j t r", r=8)
+
+
+def tile_attend_silu_seg_kernel(tc, qT, k_words, k_scales, vT, vs, offs, out):
+    nc = tc.nc
+    with ExitStack() as ctx:
+        sb = ctx.enter_context(tc.tile_pool(name="sb", bufs=1))
+        ps = ctx.enter_context(tc.psum_pool(name="ps", bufs=1))
+
+        offsets = sb.tile([P, B * COLS], U16, name="offsets")
+        kw = sb.tile([P, T], I32, name="kw", align_bytes=64)
+        ksc = sb.tile([P, T], U8, name="ksc", align_bytes=64)
+        vsw = sb.tile([P, T], F32, name="vsw", align_bytes=64)
+        vb = sb.tile([P, T, 2], BF16, name="vb", align_bytes=64)
+        qraw = sb.tile([P, B, PACK, NQ], F32, name="qraw", align_bytes=64)
+        ident = sb.tile([P, P], F32, name="ident", align_bytes=64)
+        warm = sb.tile([P, 8], F32, name="warm")
+        warm2 = sb.tile([P, 8], F32, name="warm2")
+
+        nc.vector.memset(vsw[:], 0.0)
+        nc.gpsimd.memset(warm[:], 0.0)
+        make_identity(nc, ident[:])
+
+        words = k_words[0].rearrange("p n t -> p (n t)").bitcast(I32)
+        vpairs = vT.rearrange("(p j) t -> p j t", j=2)
+        nc.sync.dma_start(offsets[:], offs)
+        nc.sync.dma_start(out=kw[:, 0:SEG], in_=words[:, 0:SEG])
+        scale_rows = k_scales[0].bitcast(I32)
+        for quad in range(4):
+            rows = scale_rows[4 * quad : 4 * quad + 4, :].unsqueeze(0).to_broadcast([8, 4, T // 4])
+            nc.sync.dma_start(out=ksc[32 * quad : 32 * quad + 32, :].bitcast(I32), in_=rows)
+        nc.scalar.activation(warm2[:], warm[:], ACT.Silu)
+        nc.sync.dma_start(out=qraw[:], in_=qT.rearrange("b (p j) n -> p b j n", j=PACK))
+        vraw = []
+        for c in range(T // CHUNK):
+            vr = sb.tile([P, 2, CHUNK], F32, name="vraw%d" % c, align_bytes=64)
+            vraw.append(vr)
+        for c in range(2):
+            nc.sync.dma_start(out=vraw[c][:], in_=vpairs[:, :, c * CHUNK : (c + 1) * CHUNK])
+            if c == 0:
+                nc.sync.dma_start(out=vsw[0:1, :], in_=vs[0:1, :])
+        nc.sync.dma_start(out=kw[:, SEG:T], in_=words[:, SEG:T])
+        for c in range(2, 4):
+            nc.sync.dma_start(out=vraw[c][:], in_=vpairs[:, :, c * CHUNK : (c + 1) * CHUNK])
+
+        def lst(b):
+            return offsets[:, b * COLS : (b + 1) * COLS]
+
+        def end(b):
+            return (b + 1) * SEG
+
+        kg, ksg, vsg, vg = {}, {}, {}, {}
+        z, vst, vt, pw, wq, vq = {}, {}, {}, {}, {}, {}
+        wc, wsc, vc, vsc = {}, {}, {}, {}
+
+        def gather_k(b):
+            kg[b] = sb.tile([P, PACK, P], U32, name="kg%d" % b, align_bytes=64)
+            nc.vector.tensor_copy(by_slot(kg[b][:]), kw[:, 0 : end(b)].bitcast(U32).indirect(lst(b)))
+
+        def gather_ks(b):
+            listed = sb.tile([P, N], U8, name="kslisted%d" % b, align_bytes=64)
+            nc.vector.tensor_copy(listed[:], ksc[:, 0 : end(b)].indirect(lst(b)))
+            ksg[b] = sb.tile([P, PACK, P], U8, name="ksg%d" % b, align_bytes=64)
+            nc.vector.tensor_copy(
+                ksg[b][:].bitcast(I32).rearrange("x t (j r) -> x t j r", r=2),
+                listed[:].bitcast(I32).rearrange("x (j t r) -> x t j r", t=PACK, r=2),
+            )
+
+        def gather_vs(b):
+            vsg[b] = sb.tile([P, PACK, P], U32, name="vsg%d" % b, align_bytes=64)
+            nc.vector.tensor_copy(by_slot(vsg[b][:]), vsw[:, 0 : end(b)].bitcast(U32).indirect(lst(b)))
+            vst[b] = ps.tile([P, PACK, P], F32, name="vst%d" % b)
+            for t in range(PACK):
+                nc.tensor.transpose(vst[b][:, t, :], vsg[b][:, t, :].bitcast(F32), ident[:])
+
+        def cast_v(c):
+            nc.scalar.activation(vb[:, c * CHUNK : (c + 1) * CHUNK, :], vraw[c][:].rearrange("p j t -> p t j"), ACT.Copy)
+
+        def gather_v(b):
+            vg[b] = sb.tile([P, PACK, P], U32, name="vg%d" % b, align_bytes=64)
+            window = vb[:, 0 : end(b), :].rearrange("p t j -> p (t j)").bitcast(U32)
+            nc.vector.tensor_copy(by_slot(vg[b][:]), window.indirect(lst(b)))
+            vt[b] = ps.tile([P, PACK, P], F32, name="vt%d" % b)
+            for t in range(PACK):
+                nc.tensor.transpose(vt[b][:, t, :], vg[b][:, t, :].bitcast(F32), ident[:])
+            vq[b] = sb.tile([P, DV, PACK], BF16, name="vq%d" % b, align_bytes=64)
+            nc.scalar.activation(vq[b][:], vt[b][:].bitcast(BF16).rearrange("p t e -> p e t"), ACT.Copy)
+
+        def quant_v(b):
+            vc[b] = sb.tile([P, DV], U32, name="vc%d" % b, align_bytes=64)
+            vsc[b] = sb.tile([P, DV], U8, name="vsc%d" % b, align_bytes=64)
+            nc.vector.quantize_mx(out=vc[b][:].bitcast(FP8X4), scales=vsc[b][:], in_=vq[b][:].rearrange("p e t -> p (e t)"))
+
+        qb = sb.tile([P, B, NQ, PACK], BF16, name="qb", align_bytes=64)
+        qc = sb.tile([P, B * NQ], U32, name="qc", align_bytes=64)
+        qsc = sb.tile([P, B * NQ], U8, name="qsc", align_bytes=64)
+
+        def quant_q():
+            nc.scalar.activation(qb[:], qraw[:].rearrange("p b j n -> p b n j"), ACT.Copy)
+            nc.vector.quantize_mx(out=qc[:].bitcast(FP8X4), scales=qsc[:], in_=qb[:].rearrange("p b n j -> p (b n j)"))
+
+        def scores(b):
+            z[b] = ps.tile([P, PACK, NQ], F32, name="z%d" % b)
+            for t in range(PACK):
+                nc.tensor.matmul_mx(
+                    out=z[b][:, t, :],
+                    lhsT=kg[b][:, t, :].bitcast(FP8X4),
+                    lhsT_scale=ksg[b][:, t, :],
+                    rhs=qc[:, b * NQ : (b + 1) * NQ].bitcast(FP8X4),
+                    rhs_scale=qsc[:, b * NQ : (b + 1) * NQ],
+                    start=True,
+                    stop=True,
+                )
+            pw[b] = sb.tile([P, NQ, PACK], F32, name="pw%d" % b, align_bytes=64)
+            nc.scalar.activation(pw[b][:], z[b][:].rearrange("p t q -> p q t"), ACT.Silu)
+
+        def weigh(b):
+            wq[b] = sb.tile([P, NQ, PACK], BF16, name="wq%d" % b, align_bytes=64)
+            scale = vst[b][:, :, 0:1].rearrange("p t o -> p o t").to_broadcast([P, NQ, PACK])
+            nc.vector.tensor_tensor(wq[b][:], pw[b][:], scale, MULT)
+
+        def quant_w(b):
+            wc[b] = sb.tile([P, NQ], U32, name="wc%d" % b, align_bytes=64)
+            wsc[b] = sb.tile([P, NQ], U8, name="wsc%d" % b, align_bytes=64)
+            nc.vector.quantize_mx(out=wc[b][:].bitcast(FP8X4), scales=wsc[b][:], in_=wq[b][:].rearrange("p q t -> p (q t)"))
+
+        def finish(b):
+            y = ps.tile([P, DV], F32, name="y%d" % b)
+            nc.tensor.matmul_mx(
+                out=y[:],
+                lhsT=wc[b][:].bitcast(FP8X4),
+                lhsT_scale=wsc[b][:],
+                rhs=vc[b][:].bitcast(FP8X4),
+                rhs_scale=vsc[b][:],
+                start=True,
+                stop=True,
+            )
+            res = sb.tile([P, DV], F32, name="res%d" % b, align_bytes=64)
+            nc.scalar.activation(res[:], y[:], ACT.Copy, scale=1.0 / 16.0)
+            nc.sync.dma_start(out=out[b], in_=res[:])
+
+        gather_k(0)
+        gather_ks(0)
+        quant_q()
+        scores(0)
+        gather_ks(1)
+        cast_v(0)
+        cast_v(1)
+        gather_vs(0)
+        gather_v(0)
+        gather_k(1)
+        weigh(0)
+        cast_v(2)
+        cast_v(3)
+        scores(1)
+        quant_w(0)
+        quant_v(0)
+        finish(0)
+        gather_v(1)
+        gather_vs(1)
+        weigh(1)
+        quant_v(1)
+        quant_w(1)
+        finish(1)

@@ -35,15 +35,16 @@ def tile_attend_silu_seg_kernel(tc, qT, k_words, k_scales, vT, vs, offs, out):
         ps = ctx.enter_context(tc.psum_pool(name="ps", bufs=1))
 
         offsets = sb.tile([P, B * COLS], U16, name="offsets")
-        kw = sb.tile([P, T], I32, name="kw", align_bytes=64)
+        kw = sb.tile([P, T], I32, name="kw", tag="keys", align_bytes=64)
         ksc = sb.tile([P, T], U8, name="ksc", align_bytes=64)
         vsw = sb.tile([P, T], F32, name="vsw", align_bytes=64)
         vb = sb.tile([P, T, 2], BF16, name="vb", align_bytes=64)
-        qraw = sb.tile([P, B, PACK, NQ], F32, name="qraw", align_bytes=64)
+        qraw = sb.tile([P, B, PACK, NQ], F32, name="qraw", tag="queries", align_bytes=64)
         ident = sb.tile([P, P], F32, name="ident", align_bytes=64)
         warm = sb.tile([P, 8], F32, name="warm")
         warm2 = sb.tile([P, 8], F32, name="warm2")
 
+        nc.gpsimd.memset(ksc[:].bitcast(I32), 0)
         nc.vector.memset(vsw[:], 0.0)
         nc.gpsimd.memset(warm[:], 0.0)
         make_identity(nc, ident[:])
@@ -51,24 +52,22 @@ def tile_attend_silu_seg_kernel(tc, qT, k_words, k_scales, vT, vs, offs, out):
         words = k_words[0].rearrange("p n t -> p (n t)").bitcast(I32)
         vpairs = vT.rearrange("(p j) t -> p j t", j=2)
         nc.sync.dma_start(offsets[:], offs)
-        nc.sync.dma_start(out=kw[:, 0:SEG], in_=words[:, 0:SEG])
         scale_rows = k_scales[0].bitcast(I32)
         for quad in range(4):
-            rows = scale_rows[4 * quad : 4 * quad + 4, :].unsqueeze(0).to_broadcast([8, 4, T // 4])
-            nc.sync.dma_start(out=ksc[32 * quad : 32 * quad + 32, :].bitcast(I32), in_=rows)
+            nc.sync.dma_start(
+                out=ksc[32 * quad : 32 * quad + 4, :].bitcast(I32), in_=scale_rows[4 * quad : 4 * quad + 4, :]
+            )
         nc.scalar.activation(warm2[:], warm[:], ACT.Silu)
-        nc.sync.dma_start(out=qraw[:], in_=qT.rearrange("b (p j) n -> p b j n", j=PACK))
         vraw = []
         for c in range(T // CHUNK):
             vr = sb.tile([P, 2, CHUNK], F32, name="vraw%d" % c, align_bytes=64)
             vraw.append(vr)
-        for c in range(2):
-            nc.sync.dma_start(out=vraw[c][:], in_=vpairs[:, :, c * CHUNK : (c + 1) * CHUNK])
+            nc.sync.dma_start(out=vr[:], in_=vpairs[:, :, c * CHUNK : (c + 1) * CHUNK])
             if c == 0:
                 nc.sync.dma_start(out=vsw[0:1, :], in_=vs[0:1, :])
-        nc.sync.dma_start(out=kw[:, SEG:T], in_=words[:, SEG:T])
-        for c in range(2, 4):
-            nc.sync.dma_start(out=vraw[c][:], in_=vpairs[:, :, c * CHUNK : (c + 1) * CHUNK])
+        nc.sync.dma_start(out=qraw[:], in_=qT.rearrange("b (p j) n -> p b j n", j=PACK))
+        for b in range(B):
+            nc.sync.dma_start(out=kw[:, b * SEG : (b + 1) * SEG], in_=words[:, b * SEG : (b + 1) * SEG])
 
         def lst(b):
             return offsets[:, b * COLS : (b + 1) * COLS]
@@ -76,29 +75,32 @@ def tile_attend_silu_seg_kernel(tc, qT, k_words, k_scales, vT, vs, offs, out):
         def end(b):
             return (b + 1) * SEG
 
-        kg, ksg, vsg, vg = {}, {}, {}, {}
-        z, vst, vt, pw, wq, vq = {}, {}, {}, {}, {}, {}
+        kg, ksg, vg = {}, {}, {}
+        z, vst, vt, pw, wq = {}, {}, {}, {}, {}
         wc, wsc, vc, vsc = {}, {}, {}, {}
 
         def gather_k(b):
             kg[b] = sb.tile([P, PACK, P], U32, name="kg%d" % b, align_bytes=64)
             nc.vector.tensor_copy(by_slot(kg[b][:]), kw[:, 0 : end(b)].bitcast(U32).indirect(lst(b)))
 
-        def gather_ks(b):
-            listed = sb.tile([P, N], U8, name="kslisted%d" % b, align_bytes=64)
-            nc.vector.tensor_copy(listed[:], ksc[:, 0 : end(b)].indirect(lst(b)))
-            ksg[b] = sb.tile([P, PACK, P], U8, name="ksg%d" % b, align_bytes=64)
+        def gather_ks():
+            listed = sb.tile([P, B * N], U8, name="kslisted", align_bytes=64)
+            nc.vector.tensor_copy(listed[:], ksc[:].indirect(offsets[:]))
+            both = sb.tile([P, PACK, B * P], U8, name="ksg", align_bytes=64)
             nc.vector.tensor_copy(
-                ksg[b][:].bitcast(I32).rearrange("x t (j r) -> x t j r", r=2),
+                both[:].bitcast(I32).rearrange("x t (j r) -> x t j r", r=2),
                 listed[:].bitcast(I32).rearrange("x (j t r) -> x t j r", t=PACK, r=2),
             )
+            for b in range(B):
+                ksg[b] = both[:, :, b * P : (b + 1) * P]
 
-        def gather_vs(b):
-            vsg[b] = sb.tile([P, PACK, P], U32, name="vsg%d" % b, align_bytes=64)
-            nc.vector.tensor_copy(by_slot(vsg[b][:]), vsw[:, 0 : end(b)].bitcast(U32).indirect(lst(b)))
-            vst[b] = ps.tile([P, PACK, P], F32, name="vst%d" % b)
-            for t in range(PACK):
-                nc.tensor.transpose(vst[b][:, t, :], vsg[b][:, t, :].bitcast(F32), ident[:])
+        def gather_vs():
+            both = sb.tile([P, PACK, B * P], U32, name="vsg", align_bytes=64)
+            nc.vector.tensor_copy(by_slot(both[:]), vsw[:].bitcast(U32).indirect(offsets[:]))
+            for b in range(B):
+                vst[b] = ps.tile([P, PACK, P], F32, name="vst%d" % b)
+                for t in range(PACK):
+                    nc.tensor.transpose(vst[b][:, t, :], both[:, t, b * P : (b + 1) * P].bitcast(F32), ident[:])
 
         def cast_v(c):
             nc.scalar.activation(vb[:, c * CHUNK : (c + 1) * CHUNK, :], vraw[c][:].rearrange("p j t -> p t j"), ACT.Copy)
@@ -110,13 +112,17 @@ def tile_attend_silu_seg_kernel(tc, qT, k_words, k_scales, vT, vs, offs, out):
             vt[b] = ps.tile([P, PACK, P], F32, name="vt%d" % b)
             for t in range(PACK):
                 nc.tensor.transpose(vt[b][:, t, :], vg[b][:, t, :].bitcast(F32), ident[:])
-            vq[b] = sb.tile([P, DV, PACK], BF16, name="vq%d" % b, align_bytes=64)
-            nc.scalar.activation(vq[b][:], vt[b][:].bitcast(BF16).rearrange("p t e -> p e t"), ACT.Copy)
 
-        def quant_v(b):
-            vc[b] = sb.tile([P, DV], U32, name="vc%d" % b, align_bytes=64)
-            vsc[b] = sb.tile([P, DV], U8, name="vsc%d" % b, align_bytes=64)
-            nc.vector.quantize_mx(out=vc[b][:].bitcast(FP8X4), scales=vsc[b][:], in_=vq[b][:].rearrange("p e t -> p (e t)"))
+        def quant_v():
+            vq = sb.tile([P, B, DV, PACK], BF16, name="vq", tag="queries", align_bytes=64)
+            for b in range(B):
+                nc.scalar.activation(vq[:, b], vt[b][:].bitcast(BF16).rearrange("p t e -> p e t"), ACT.Copy)
+            codes = sb.tile([P, B * DV], U32, name="vc", tag="keys", align_bytes=64)
+            scales = sb.tile([P, B * DV], U8, name="vsc", align_bytes=64)
+            nc.vector.quantize_mx(out=codes[:].bitcast(FP8X4), scales=scales[:], in_=vq[:].rearrange("p b e t -> p (b e t)"))
+            for b in range(B):
+                vc[b] = codes[:, b * DV : (b + 1) * DV]
+                vsc[b] = scales[:, b * DV : (b + 1) * DV]
 
         qb = sb.tile([P, B, NQ, PACK], BF16, name="qb", align_bytes=64)
         qc = sb.tile([P, B * NQ], U32, name="qc", align_bytes=64)
@@ -157,8 +163,8 @@ def tile_attend_silu_seg_kernel(tc, qT, k_words, k_scales, vT, vs, offs, out):
                 out=y[:],
                 lhsT=wc[b][:].bitcast(FP8X4),
                 lhsT_scale=wsc[b][:],
-                rhs=vc[b][:].bitcast(FP8X4),
-                rhs_scale=vsc[b][:],
+                rhs=vc[b].bitcast(FP8X4),
+                rhs_scale=vsc[b],
                 start=True,
                 stop=True,
             )
@@ -166,26 +172,21 @@ def tile_attend_silu_seg_kernel(tc, qT, k_words, k_scales, vT, vs, offs, out):
             nc.scalar.activation(res[:], y[:], ACT.Copy, scale=1.0 / 16.0)
             nc.sync.dma_start(out=out[b], in_=res[:])
 
-        gather_k(0)
-        gather_ks(0)
-        quant_q()
-        scores(0)
-        gather_ks(1)
-        cast_v(0)
-        cast_v(1)
-        gather_vs(0)
+        gather_ks()
+        for c in range(T // CHUNK):
+            cast_v(c)
+        gather_vs()
         gather_v(0)
-        gather_k(1)
-        weigh(0)
-        cast_v(2)
-        cast_v(3)
-        scores(1)
-        quant_w(0)
-        quant_v(0)
-        finish(0)
         gather_v(1)
-        gather_vs(1)
+        quant_q()
+        gather_k(0)
+        gather_k(1)
+        scores(0)
+        scores(1)
+        quant_v()
+        weigh(0)
         weigh(1)
-        quant_v(1)
+        quant_w(0)
+        finish(0)
         quant_w(1)
         finish(1)

@@ -21,7 +21,7 @@ P = 128
 PACK = 4
 SEG = T // B
 COLS = N // 16
-CHUNK = 512
+CUTS = [0, 256, 640, 1024, 1536, 2048]
 
 
 def by_slot(t):
@@ -32,10 +32,11 @@ def tile_attend_silu_seg_kernel(tc, qT, k_words, k_scales, vT, vs, offs, out):
     nc = tc.nc
     with ExitStack() as ctx:
         sb = ctx.enter_context(tc.tile_pool(name="sb", bufs=1))
+        shared = ctx.enter_context(tc.tile_pool(name="shared", bufs=1))
         ps = ctx.enter_context(tc.psum_pool(name="ps", bufs=1))
 
         offsets = sb.tile([P, B * COLS], U16, name="offsets")
-        kw = sb.tile([P, T], I32, name="kw", tag="keys", align_bytes=64)
+        kw = shared.tile([P, T], I32, name="kw", offset=0, align_bytes=64)
         ksc = sb.tile([P, T], U8, name="ksc", align_bytes=64)
         vsw = sb.tile([P, T], F32, name="vsw", align_bytes=64)
         vb = sb.tile([P, T, 2], BF16, name="vb", align_bytes=64)
@@ -44,7 +45,7 @@ def tile_attend_silu_seg_kernel(tc, qT, k_words, k_scales, vT, vs, offs, out):
         warm = sb.tile([P, 8], F32, name="warm")
         warm2 = sb.tile([P, 8], F32, name="warm2")
 
-        nc.gpsimd.memset(ksc[:].bitcast(I32), 0)
+        nc.vector.memset(ksc[:].bitcast(I32), 0)
         nc.vector.memset(vsw[:], 0.0)
         nc.gpsimd.memset(warm[:], 0.0)
         make_identity(nc, ident[:])
@@ -53,21 +54,25 @@ def tile_attend_silu_seg_kernel(tc, qT, k_words, k_scales, vT, vs, offs, out):
         vpairs = vT.rearrange("(p j) t -> p j t", j=2)
         nc.sync.dma_start(offsets[:], offs)
         scale_rows = k_scales[0].bitcast(I32)
-        for quad in range(4):
-            nc.sync.dma_start(
-                out=ksc[32 * quad : 32 * quad + 4, :].bitcast(I32), in_=scale_rows[4 * quad : 4 * quad + 4, :]
-            )
         nc.scalar.activation(warm2[:], warm[:], ACT.Silu)
         vraw = []
-        for c in range(T // CHUNK):
-            vr = sb.tile([P, 2, CHUNK], F32, name="vraw%d" % c, align_bytes=64)
+        for c in range(len(CUTS) - 1):
+            vr = sb.tile([P, 2, CUTS[c + 1] - CUTS[c]], F32, name="vraw%d" % c, align_bytes=64)
             vraw.append(vr)
-            nc.sync.dma_start(out=vr[:], in_=vpairs[:, :, c * CHUNK : (c + 1) * CHUNK])
+            nc.sync.dma_start(out=vr[:], in_=vpairs[:, :, CUTS[c] : CUTS[c + 1]])
             if c == 0:
+                for quad in range(4):
+                    nc.sync.dma_start(
+                        out=ksc[32 * quad : 32 * quad + 4, :].bitcast(I32), in_=scale_rows[4 * quad : 4 * quad + 4, :]
+                    )
+            if c == 1:
                 nc.sync.dma_start(out=vsw[0:1, :], in_=vs[0:1, :])
         nc.sync.dma_start(out=qraw[:], in_=qT.rearrange("b (p j) n -> p b j n", j=PACK))
         for b in range(B):
             nc.sync.dma_start(out=kw[:, b * SEG : (b + 1) * SEG], in_=words[:, b * SEG : (b + 1) * SEG])
+
+        def parts(b):
+            return [slice(0, NQ)] if b == 0 else [slice(0, NQ // 2), slice(NQ // 2, NQ)]
 
         def lst(b):
             return offsets[:, b * COLS : (b + 1) * COLS]
@@ -86,7 +91,10 @@ def tile_attend_silu_seg_kernel(tc, qT, k_words, k_scales, vT, vs, offs, out):
         def gather_ks():
             listed = sb.tile([P, B * N], U8, name="kslisted", align_bytes=64)
             nc.vector.tensor_copy(listed[:], ksc[:].indirect(offsets[:]))
-            both = sb.tile([P, PACK, B * P], U8, name="ksg", align_bytes=64)
+            return listed
+
+        def order_ks(listed):
+            both = sb.tile([P, PACK, B * P], U8, name="ksg", tag="vraw2", align_bytes=64)
             nc.vector.tensor_copy(
                 both[:].bitcast(I32).rearrange("x t (j r) -> x t j r", r=2),
                 listed[:].bitcast(I32).rearrange("x (j t r) -> x t j r", t=PACK, r=2),
@@ -103,7 +111,7 @@ def tile_attend_silu_seg_kernel(tc, qT, k_words, k_scales, vT, vs, offs, out):
                     nc.tensor.transpose(vst[b][:, t, :], both[:, t, b * P : (b + 1) * P].bitcast(F32), ident[:])
 
         def cast_v(c):
-            nc.scalar.activation(vb[:, c * CHUNK : (c + 1) * CHUNK, :], vraw[c][:].rearrange("p j t -> p t j"), ACT.Copy)
+            nc.scalar.activation(vb[:, CUTS[c] : CUTS[c + 1], :], vraw[c][:].rearrange("p j t -> p t j"), ACT.Copy)
 
         def gather_v(b):
             vg[b] = sb.tile([P, PACK, P], U32, name="vg%d" % b, align_bytes=64)
@@ -117,7 +125,7 @@ def tile_attend_silu_seg_kernel(tc, qT, k_words, k_scales, vT, vs, offs, out):
             vq = sb.tile([P, B, DV, PACK], BF16, name="vq", tag="queries", align_bytes=64)
             for b in range(B):
                 nc.scalar.activation(vq[:, b], vt[b][:].bitcast(BF16).rearrange("p t e -> p e t"), ACT.Copy)
-            codes = sb.tile([P, B * DV], U32, name="vc", tag="keys", align_bytes=64)
+            codes = shared.tile([P, B * DV], U32, name="vc", offset=0, align_bytes=64)
             scales = sb.tile([P, B * DV], U8, name="vsc", align_bytes=64)
             nc.vector.quantize_mx(out=codes[:].bitcast(FP8X4), scales=scales[:], in_=vq[:].rearrange("p b e t -> p (b e t)"))
             for b in range(B):
@@ -145,37 +153,50 @@ def tile_attend_silu_seg_kernel(tc, qT, k_words, k_scales, vT, vs, offs, out):
                     stop=True,
                 )
             pw[b] = sb.tile([P, NQ, PACK], F32, name="pw%d" % b, align_bytes=64)
-            nc.scalar.activation(pw[b][:], z[b][:].rearrange("p t q -> p q t"), ACT.Silu)
+            for rows in parts(b):
+                nc.scalar.activation(pw[b][:, rows, :], z[b][:, :, rows].rearrange("p t q -> p q t"), ACT.Silu)
 
         def weigh(b):
-            wq[b] = sb.tile([P, NQ, PACK], BF16, name="wq%d" % b, align_bytes=64)
-            scale = vst[b][:, :, 0:1].rearrange("p t o -> p o t").to_broadcast([P, NQ, PACK])
-            nc.vector.tensor_tensor(wq[b][:], pw[b][:], scale, MULT)
+            wq[b] = shared.tile([P, NQ, PACK], BF16, name="wq%d" % b, offset=2048 + 1024 * b, align_bytes=64)
+            for rows in parts(b):
+                scale = vst[b][:, :, 0:1].rearrange("p t o -> p o t").to_broadcast([P, rows.stop - rows.start, PACK])
+                nc.vector.tensor_tensor(wq[b][:, rows, :], pw[b][:, rows, :], scale, MULT)
 
         def quant_w(b):
             wc[b] = sb.tile([P, NQ], U32, name="wc%d" % b, align_bytes=64)
             wsc[b] = sb.tile([P, NQ], U8, name="wsc%d" % b, align_bytes=64)
-            nc.vector.quantize_mx(out=wc[b][:].bitcast(FP8X4), scales=wsc[b][:], in_=wq[b][:].rearrange("p q t -> p (q t)"))
+            for rows in parts(b):
+                nc.vector.quantize_mx(
+                    out=wc[b][:, rows].bitcast(FP8X4),
+                    scales=wsc[b][:, rows],
+                    in_=wq[b][:, rows, :].rearrange("p q t -> p (q t)"),
+                )
 
         def finish(b):
-            y = ps.tile([P, DV], F32, name="y%d" % b)
-            nc.tensor.matmul_mx(
-                out=y[:],
-                lhsT=wc[b][:].bitcast(FP8X4),
-                lhsT_scale=wsc[b][:],
-                rhs=vc[b].bitcast(FP8X4),
-                rhs_scale=vsc[b],
-                start=True,
-                stop=True,
-            )
             res = sb.tile([P, DV], F32, name="res%d" % b, align_bytes=64)
-            nc.scalar.activation(res[:], y[:], ACT.Copy, scale=1.0 / 16.0)
+            halves = [slice(0, DV)] if b == 0 else [slice(0, DV // 2), slice(DV // 2, DV)]
+            for h, cols in enumerate(halves):
+                y = ps.tile([P, cols.stop - cols.start], F32, name="y%d%d" % (b, h), tag="y%d" % b if h == 0 else "vt0")
+                nc.tensor.matmul_mx(
+                    out=y[:],
+                    lhsT=wc[b][:].bitcast(FP8X4),
+                    lhsT_scale=wsc[b][:],
+                    rhs=vc[b][:, cols].bitcast(FP8X4),
+                    rhs_scale=vsc[b][:, cols],
+                    start=True,
+                    stop=True,
+                )
+                if h == 0:
+                    nc.scalar.activation(res[:, cols], y[:], ACT.Copy, scale=1.0 / 16.0)
+                else:
+                    nc.vector.tensor_scalar(res[:, cols], y[:], 1.0 / 16.0, None, MULT)
             nc.sync.dma_start(out=out[b], in_=res[:])
 
-        gather_ks()
-        for c in range(T // CHUNK):
+        listed_scales = gather_ks()
+        for c in range(len(CUTS) - 1):
             cast_v(c)
         gather_vs()
+        order_ks(listed_scales)
         gather_v(0)
         gather_v(1)
         quant_q()
@@ -183,10 +204,10 @@ def tile_attend_silu_seg_kernel(tc, qT, k_words, k_scales, vT, vs, offs, out):
         gather_k(1)
         scores(0)
         scores(1)
-        quant_v()
         weigh(0)
-        weigh(1)
+        quant_v()
         quant_w(0)
+        weigh(1)
         finish(0)
         quant_w(1)
         finish(1)

@@ -46,13 +46,14 @@ def tile_attend_silu_seg_kernel(tc, qT, k_words, k_scales, vT, vs, offs, out):
         warm2 = sb.tile([P, 8], F32, name="warm2")
 
         nc.vector.memset(ksc[:].bitcast(I32), 0)
-        nc.vector.memset(vsw[:], 0.0)
+        nc.vector.memset(vsw[0 : P - 1, :], 0.0)
         nc.gpsimd.memset(warm[:], 0.0)
         make_identity(nc, ident[:])
 
         words = k_words[0].rearrange("p n t -> p (n t)").bitcast(I32)
         vpairs = vT.rearrange("(p j) t -> p j t", j=2)
         nc.sync.dma_start(offsets[:], offs)
+        nc.sync.dma_start(out=vsw[P - 1 : P, :], in_=vs[0:1, :])
         scale_rows = k_scales[0].bitcast(I32)
         nc.scalar.activation(warm2[:], warm[:], ACT.Silu)
         vraw = []
@@ -65,8 +66,6 @@ def tile_attend_silu_seg_kernel(tc, qT, k_words, k_scales, vT, vs, offs, out):
                     nc.sync.dma_start(
                         out=ksc[32 * quad : 32 * quad + 4, :].bitcast(I32), in_=scale_rows[4 * quad : 4 * quad + 4, :]
                     )
-            if c == 1:
-                nc.sync.dma_start(out=vsw[0:1, :], in_=vs[0:1, :])
         nc.sync.dma_start(out=qraw[:], in_=qT.rearrange("b (p j) n -> p b j n", j=PACK))
         for b in range(B):
             nc.sync.dma_start(out=kw[:, b * SEG : (b + 1) * SEG], in_=words[:, b * SEG : (b + 1) * SEG])
@@ -159,7 +158,7 @@ def tile_attend_silu_seg_kernel(tc, qT, k_words, k_scales, vT, vs, offs, out):
         def weigh(b):
             wq[b] = shared.tile([P, NQ, PACK], BF16, name="wq%d" % b, offset=2048 + 1024 * b, align_bytes=64)
             for rows in parts(b):
-                scale = vst[b][:, :, 0:1].rearrange("p t o -> p o t").to_broadcast([P, rows.stop - rows.start, PACK])
+                scale = vst[b][:, :, P - 1 : P].rearrange("p t o -> p o t").to_broadcast([P, rows.stop - rows.start, PACK])
                 nc.vector.tensor_tensor(wq[b][:, rows, :], pw[b][:, rows, :], scale, MULT)
 
         def quant_w(b):
@@ -192,12 +191,12 @@ def tile_attend_silu_seg_kernel(tc, qT, k_words, k_scales, vT, vs, offs, out):
                     nc.vector.tensor_scalar(res[:, cols], y[:], 1.0 / 16.0, None, MULT)
             nc.sync.dma_start(out=out[b], in_=res[:])
 
+        gather_vs()
         listed_scales = gather_ks()
         for c in range(len(CUTS) - 1):
             cast_v(c)
-        gather_vs()
-        order_ks(listed_scales)
         gather_v(0)
+        order_ks(listed_scales)
         gather_v(1)
         quant_q()
         gather_k(0)

@@ -21,7 +21,8 @@ P = 128
 PACK = 4
 SEG = T // B
 COLS = N // 16
-CUTS = [0, 256, 640, 1024, 1536, 2048]
+PLANES = DV // P
+HALF = SEG // 2
 
 
 def by_slot(t):
@@ -36,39 +37,63 @@ def tile_attend_silu_seg_kernel(tc, qT, k_words, k_scales, vT, vs, offs, out):
         ps = ctx.enter_context(tc.psum_pool(name="ps", bufs=1))
 
         offsets = sb.tile([P, B * COLS], U16, name="offsets")
-        kw = shared.tile([P, T], I32, name="kw", offset=0, align_bytes=64)
+        kw = sb.tile([P, T], I32, name="kw", align_bytes=64)
         ksc = sb.tile([P, T], U8, name="ksc", align_bytes=64)
         vsw = sb.tile([P, T], F32, name="vsw", align_bytes=64)
-        vb = sb.tile([P, T, 2], BF16, name="vb", align_bytes=64)
-        qraw = sb.tile([P, B, PACK, NQ], F32, name="qraw", tag="queries", align_bytes=64)
+        vb = [sb.tile([P, T], BF16, name="vb%d" % j, align_bytes=64) for j in range(PLANES)]
+        qraw = [sb.tile([P, PACK, NQ], F32, name="qraw%d" % b, align_bytes=64) for b in range(B)]
         ident = sb.tile([P, P], F32, name="ident", align_bytes=64)
         warm = sb.tile([P, 8], F32, name="warm")
         warm2 = sb.tile([P, 8], F32, name="warm2")
 
-        nc.vector.memset(ksc[:].bitcast(I32), 0)
+        nc.vector.memset(ksc[:, 0:SEG].bitcast(I32), 0)
+        nc.gpsimd.memset(ksc[:, SEG:T].bitcast(I32), 0)
         nc.vector.memset(vsw[0 : P - 1, :], 0.0)
         nc.gpsimd.memset(warm[:], 0.0)
         make_identity(nc, ident[:])
 
         words = k_words[0].rearrange("p n t -> p (n t)").bitcast(I32)
-        vpairs = vT.rearrange("(p j) t -> p j t", j=2)
+        scale_rows = k_scales[0].bitcast(I32)
+        vraw = {}
+
+        def seg(b):
+            return slice(b * SEG, (b + 1) * SEG)
+
+        def pieces(b, j):
+            if (b, j) == (0, 1):
+                return [seg(b)]
+            return [slice(b * SEG + h * HALF, b * SEG + (h + 1) * HALF) for h in range(2)]
+
+        def load_v(b, j):
+            for h, cols in enumerate(pieces(b, j)):
+                name = "vraw%d%d%d" % (b, j, h)
+                if (b, j, h) == (1, 1, 1):
+                    vraw[b, j, h] = shared.tile([P, HALF], F32, name=name, offset=0, align_bytes=64)
+                else:
+                    vraw[b, j, h] = sb.tile([P, cols.stop - cols.start], F32, name=name, align_bytes=64)
+                nc.sync.dma_start(out=vraw[b, j, h][:], in_=vT[j * P : (j + 1) * P, cols])
+
+        def load_k(b):
+            nc.sync.dma_start(out=kw[:, seg(b)], in_=words[:, seg(b)])
+
+        def load_q(b):
+            nc.sync.dma_start(out=qraw[b][:], in_=qT[b].rearrange("(p j) n -> p j n", j=PACK))
+
         nc.sync.dma_start(offsets[:], offs)
         nc.sync.dma_start(out=vsw[P - 1 : P, :], in_=vs[0:1, :])
-        scale_rows = k_scales[0].bitcast(I32)
         nc.scalar.activation(warm2[:], warm[:], ACT.Silu)
-        vraw = []
-        for c in range(len(CUTS) - 1):
-            vr = sb.tile([P, 2, CUTS[c + 1] - CUTS[c]], F32, name="vraw%d" % c, align_bytes=64)
-            vraw.append(vr)
-            nc.sync.dma_start(out=vr[:], in_=vpairs[:, :, CUTS[c] : CUTS[c + 1]])
-            if c == 0:
-                for quad in range(4):
-                    nc.sync.dma_start(
-                        out=ksc[32 * quad : 32 * quad + 4, :].bitcast(I32), in_=scale_rows[4 * quad : 4 * quad + 4, :]
-                    )
-        nc.sync.dma_start(out=qraw[:], in_=qT.rearrange("b (p j) n -> p b j n", j=PACK))
-        for b in range(B):
-            nc.sync.dma_start(out=kw[:, b * SEG : (b + 1) * SEG], in_=words[:, b * SEG : (b + 1) * SEG])
+        load_v(0, 0)
+        load_v(0, 1)
+        for quad in range(4):
+            nc.sync.dma_start(
+                out=ksc[32 * quad : 32 * quad + 4, :].bitcast(I32), in_=scale_rows[4 * quad : 4 * quad + 4, :]
+            )
+        load_q(0)
+        load_v(1, 0)
+        load_k(0)
+        load_v(1, 1)
+        load_q(1)
+        load_k(1)
 
         def parts(b):
             return [slice(0, NQ)] if b == 0 else [slice(0, NQ // 2), slice(NQ // 2, NQ)]
@@ -79,9 +104,9 @@ def tile_attend_silu_seg_kernel(tc, qT, k_words, k_scales, vT, vs, offs, out):
         def end(b):
             return (b + 1) * SEG
 
-        kg, ksg, vg = {}, {}, {}
+        kg, ksg = {}, {}
         z, vst, vt, pw, wq = {}, {}, {}, {}, {}
-        wc, wsc, vc, vsc = {}, {}, {}, {}
+        wc, wsc, vc, vsc, qc, qsc = {}, {}, {}, {}, {}, {}
 
         def gather_k(b):
             kg[b] = sb.tile([P, PACK, P], U32, name="kg%d" % b, align_bytes=64)
@@ -93,7 +118,7 @@ def tile_attend_silu_seg_kernel(tc, qT, k_words, k_scales, vT, vs, offs, out):
             return listed
 
         def order_ks(listed):
-            both = sb.tile([P, PACK, B * P], U8, name="ksg", tag="vraw2", align_bytes=64)
+            both = sb.tile([P, PACK, B * P], U8, name="ksg", tag="qraw0", align_bytes=64)
             nc.vector.tensor_copy(
                 both[:].bitcast(I32).rearrange("x t (j r) -> x t j r", r=2),
                 listed[:].bitcast(I32).rearrange("x (j t r) -> x t j r", t=PACK, r=2),
@@ -109,35 +134,44 @@ def tile_attend_silu_seg_kernel(tc, qT, k_words, k_scales, vT, vs, offs, out):
                 for t in range(PACK):
                     nc.tensor.transpose(vst[b][:, t, :], both[:, t, b * P : (b + 1) * P].bitcast(F32), ident[:])
 
-        def cast_v(c):
-            nc.scalar.activation(vb[:, CUTS[c] : CUTS[c + 1], :], vraw[c][:].rearrange("p j t -> p t j"), ACT.Copy)
+        def gather_v(b, j):
+            for h, cols in enumerate(pieces(b, j)):
+                if (b, j, h) == (0, 0, 0):
+                    nc.scalar.activation(vb[j][:, cols], vraw[b, j, h][:], ACT.Copy)
+                else:
+                    nc.gpsimd.tensor_copy(vb[j][:, cols], vraw[b, j, h][:])
+            vg = sb.tile([P, N], BF16, name="vg%d%d" % (b, j), align_bytes=64)
+            nc.scalar.activation(
+                vg[:].rearrange("x (g r t) -> x g t r", r=8, t=PACK), vb[j][:, 0 : end(b)].indirect(lst(b)), ACT.Copy
+            )
+            if j == 0:
+                vt[b] = ps.tile([P, PLANES, 2, P], F32, name="vt%d" % b)
+            pairs = vg[:].bitcast(F32)
+            for u in range(2):
+                nc.tensor.transpose(vt[b][:, j, u, :], pairs[:, u : N // 2 : 2], ident[:])
 
-        def gather_v(b):
-            vg[b] = sb.tile([P, PACK, P], U32, name="vg%d" % b, align_bytes=64)
-            window = vb[:, 0 : end(b), :].rearrange("p t j -> p (t j)").bitcast(U32)
-            nc.vector.tensor_copy(by_slot(vg[b][:]), window.indirect(lst(b)))
-            vt[b] = ps.tile([P, PACK, P], F32, name="vt%d" % b)
-            for t in range(PACK):
-                nc.tensor.transpose(vt[b][:, t, :], vg[b][:, t, :].bitcast(F32), ident[:])
+        def quant_v(b):
+            vq = sb.tile([P, DV * PACK], BF16, name="vq%d" % b, tag="vraw101" if b == 0 else "vq1", align_bytes=64)
+            nc.scalar.copy(
+                vq[:].bitcast(F32).rearrange("p (j e u) -> p j e u", j=PLANES, u=2),
+                vt[b][:].rearrange("p j u e -> p j e u"),
+            )
+            vc[b] = sb.tile([P, DV], U32, name="vc%d" % b, align_bytes=64)
+            if b == 0:
+                vsc[b] = shared.tile([P, DV], U8, name="vsc0", offset=0, align_bytes=64)
+            else:
+                vsc[b] = sb.tile([P, DV], U8, name="vsc1", align_bytes=64)
+            nc.vector.quantize_mx(out=vc[b][:].bitcast(FP8X4), scales=vsc[b][:], in_=vq[:])
 
-        def quant_v():
-            vq = sb.tile([P, B, DV, PACK], BF16, name="vq", tag="queries", align_bytes=64)
-            for b in range(B):
-                nc.scalar.activation(vq[:, b], vt[b][:].bitcast(BF16).rearrange("p t e -> p e t"), ACT.Copy)
-            codes = shared.tile([P, B * DV], U32, name="vc", offset=0, align_bytes=64)
-            scales = sb.tile([P, B * DV], U8, name="vsc", align_bytes=64)
-            nc.vector.quantize_mx(out=codes[:].bitcast(FP8X4), scales=scales[:], in_=vq[:].rearrange("p b e t -> p (b e t)"))
-            for b in range(B):
-                vc[b] = codes[:, b * DV : (b + 1) * DV]
-                vsc[b] = scales[:, b * DV : (b + 1) * DV]
-
-        qb = sb.tile([P, B, NQ, PACK], BF16, name="qb", align_bytes=64)
-        qc = sb.tile([P, B * NQ], U32, name="qc", align_bytes=64)
-        qsc = sb.tile([P, B * NQ], U8, name="qsc", align_bytes=64)
-
-        def quant_q():
-            nc.scalar.activation(qb[:], qraw[:].rearrange("p b j n -> p b n j"), ACT.Copy)
-            nc.vector.quantize_mx(out=qc[:].bitcast(FP8X4), scales=qsc[:], in_=qb[:].rearrange("p b n j -> p (b n j)"))
+        def quant_q(b):
+            qb = sb.tile([P, NQ, PACK], BF16, name="qb%d" % b, align_bytes=64)
+            qc[b] = sb.tile([P, NQ], U32, name="qc%d" % b, align_bytes=64)
+            qsc[b] = sb.tile([P, NQ], U8, name="qsc%d" % b, align_bytes=64)
+            if b == 0:
+                nc.scalar.activation(qb[:], qraw[b][:].rearrange("p j n -> p n j"), ACT.Copy)
+            else:
+                nc.vector.tensor_copy(qb[:], qraw[b][:].rearrange("p j n -> p n j"))
+            nc.vector.quantize_mx(out=qc[b][:].bitcast(FP8X4), scales=qsc[b][:], in_=qb[:].rearrange("p n j -> p (n j)"))
 
         def scores(b):
             z[b] = ps.tile([P, PACK, NQ], F32, name="z%d" % b)
@@ -146,17 +180,20 @@ def tile_attend_silu_seg_kernel(tc, qT, k_words, k_scales, vT, vs, offs, out):
                     out=z[b][:, t, :],
                     lhsT=kg[b][:, t, :].bitcast(FP8X4),
                     lhsT_scale=ksg[b][:, t, :],
-                    rhs=qc[:, b * NQ : (b + 1) * NQ].bitcast(FP8X4),
-                    rhs_scale=qsc[:, b * NQ : (b + 1) * NQ],
+                    rhs=qc[b][:].bitcast(FP8X4),
+                    rhs_scale=qsc[b][:],
                     start=True,
                     stop=True,
                 )
-            pw[b] = sb.tile([P, NQ, PACK], F32, name="pw%d" % b, align_bytes=64)
+            if b == 0:
+                pw[b] = shared.tile([P, NQ, PACK], F32, name="pw0", offset=1024, align_bytes=64)
+            else:
+                pw[b] = sb.tile([P, NQ, PACK], F32, name="pw1", align_bytes=64)
             for rows in parts(b):
                 nc.scalar.activation(pw[b][:, rows, :], z[b][:, :, rows].rearrange("p t q -> p q t"), ACT.Silu)
 
         def weigh(b):
-            wq[b] = shared.tile([P, NQ, PACK], BF16, name="wq%d" % b, offset=2048 + 1024 * b, align_bytes=64)
+            wq[b] = sb.tile([P, NQ, PACK], BF16, name="wq%d" % b, tag="kw" if b == 0 else "wq1", align_bytes=64)
             for rows in parts(b):
                 scale = vst[b][:, :, P - 1 : P].rearrange("p t o -> p o t").to_broadcast([P, rows.stop - rows.start, PACK])
                 nc.vector.tensor_tensor(wq[b][:, rows, :], pw[b][:, rows, :], scale, MULT)
@@ -193,20 +230,22 @@ def tile_attend_silu_seg_kernel(tc, qT, k_words, k_scales, vT, vs, offs, out):
 
         gather_vs()
         listed_scales = gather_ks()
-        for c in range(len(CUTS) - 1):
-            cast_v(c)
-        gather_v(0)
+        gather_v(0, 0)
+        quant_q(0)
         order_ks(listed_scales)
-        gather_v(1)
-        quant_q()
+        gather_v(0, 1)
+        gather_v(1, 0)
         gather_k(0)
+        gather_v(1, 1)
+        quant_q(1)
+        quant_v(0)
         gather_k(1)
         scores(0)
-        scores(1)
         weigh(0)
-        quant_v()
+        quant_v(1)
+        scores(1)
         quant_w(0)
-        weigh(1)
         finish(0)
+        weigh(1)
         quant_w(1)
         finish(1)

@@ -23,6 +23,7 @@ SEG = T // B
 COLS = N // 16
 PLANES = DV // P
 HALF = SEG // 2
+LAST = 4 * T
 
 
 def by_slot(t):
@@ -37,7 +38,7 @@ def tile_attend_silu_seg_kernel(tc, qT, k_words, k_scales, vT, vs, offs, out):
         ps = ctx.enter_context(tc.psum_pool(name="ps", bufs=1))
 
         offsets = sb.tile([P, B * COLS], U16, name="offsets")
-        kw = sb.tile([P, T], I32, name="kw", align_bytes=64)
+        kw = shared.tile([P, T], I32, name="kw", offset=0, align_bytes=64)
         ksc = sb.tile([P, T], U8, name="ksc", align_bytes=64)
         vsw = sb.tile([P, T], F32, name="vsw", align_bytes=64)
         vb = [sb.tile([P, T], BF16, name="vb%d" % j, align_bytes=64) for j in range(PLANES)]
@@ -59,19 +60,12 @@ def tile_attend_silu_seg_kernel(tc, qT, k_words, k_scales, vT, vs, offs, out):
         def seg(b):
             return slice(b * SEG, (b + 1) * SEG)
 
-        def pieces(b, j):
-            if (b, j) == (0, 1):
-                return [seg(b)]
-            return [slice(b * SEG + h * HALF, b * SEG + (h + 1) * HALF) for h in range(2)]
-
         def load_v(b, j):
-            for h, cols in enumerate(pieces(b, j)):
-                name = "vraw%d%d%d" % (b, j, h)
-                if (b, j, h) == (1, 1, 1):
-                    vraw[b, j, h] = shared.tile([P, HALF], F32, name=name, offset=0, align_bytes=64)
-                else:
-                    vraw[b, j, h] = sb.tile([P, cols.stop - cols.start], F32, name=name, align_bytes=64)
-                nc.sync.dma_start(out=vraw[b, j, h][:], in_=vT[j * P : (j + 1) * P, cols])
+            if (b, j) == (1, 1):
+                vraw[b, j] = shared.tile([P, SEG], F32, name="vraw11", offset=LAST, align_bytes=64)
+            else:
+                vraw[b, j] = sb.tile([P, SEG], F32, name="vraw%d%d" % (b, j), align_bytes=64)
+            nc.sync.dma_start(out=vraw[b, j][:], in_=vT[j * P : (j + 1) * P, seg(b)])
 
         def load_k(b):
             nc.sync.dma_start(out=kw[:, seg(b)], in_=words[:, seg(b)])
@@ -88,9 +82,9 @@ def tile_attend_silu_seg_kernel(tc, qT, k_words, k_scales, vT, vs, offs, out):
             nc.sync.dma_start(
                 out=ksc[32 * quad : 32 * quad + 4, :].bitcast(I32), in_=scale_rows[4 * quad : 4 * quad + 4, :]
             )
-        load_q(0)
         load_v(1, 0)
         load_k(0)
+        load_q(0)
         load_v(1, 1)
         load_q(1)
         load_k(1)
@@ -118,7 +112,7 @@ def tile_attend_silu_seg_kernel(tc, qT, k_words, k_scales, vT, vs, offs, out):
             return listed
 
         def order_ks(listed):
-            both = sb.tile([P, PACK, B * P], U8, name="ksg", tag="qraw0", align_bytes=64)
+            both = sb.tile([P, PACK, B * P], U8, name="ksg", tag="vraw10", align_bytes=64)
             nc.vector.tensor_copy(
                 both[:].bitcast(I32).rearrange("x t (j r) -> x t j r", r=2),
                 listed[:].bitcast(I32).rearrange("x (j t r) -> x t j r", t=PACK, r=2),
@@ -135,11 +129,13 @@ def tile_attend_silu_seg_kernel(tc, qT, k_words, k_scales, vT, vs, offs, out):
                     nc.tensor.transpose(vst[b][:, t, :], both[:, t, b * P : (b + 1) * P].bitcast(F32), ident[:])
 
         def gather_v(b, j):
-            for h, cols in enumerate(pieces(b, j)):
-                if (b, j, h) == (0, 0, 0):
-                    nc.scalar.activation(vb[j][:, cols], vraw[b, j, h][:], ACT.Copy)
-                else:
-                    nc.gpsimd.tensor_copy(vb[j][:, cols], vraw[b, j, h][:])
+            if (b, j) == (0, 0):
+                nc.scalar.activation(vb[j][:, 0:HALF], vraw[b, j][:, 0:HALF], ACT.Copy)
+                nc.gpsimd.tensor_copy(vb[j][:, HALF:SEG], vraw[b, j][:, HALF:SEG])
+            elif (b, j) == (1, 1):
+                nc.vector.tensor_copy(vb[j][:, seg(b)], vraw[b, j][:])
+            else:
+                nc.gpsimd.tensor_copy(vb[j][:, seg(b)], vraw[b, j][:])
             vg = sb.tile([P, N], BF16, name="vg%d%d" % (b, j), align_bytes=64)
             nc.scalar.activation(
                 vg[:].rearrange("x (g r t) -> x g t r", r=8, t=PACK), vb[j][:, 0 : end(b)].indirect(lst(b)), ACT.Copy
@@ -151,21 +147,25 @@ def tile_attend_silu_seg_kernel(tc, qT, k_words, k_scales, vT, vs, offs, out):
                 nc.tensor.transpose(vt[b][:, j, u, :], pairs[:, u : N // 2 : 2], ident[:])
 
         def quant_v(b):
-            vq = sb.tile([P, DV * PACK], BF16, name="vq%d" % b, tag="vraw101" if b == 0 else "vq1", align_bytes=64)
+            if b == 0:
+                vq = shared.tile([P, DV * PACK], BF16, name="vq0", offset=LAST, align_bytes=64)
+                vc[b] = shared.tile([P, DV], U32, name="vc0", offset=0, align_bytes=64)
+            else:
+                vq = sb.tile([P, DV * PACK], BF16, name="vq1", align_bytes=64)
+                vc[b] = sb.tile([P, DV], U32, name="vc1", align_bytes=64)
             nc.scalar.copy(
                 vq[:].bitcast(F32).rearrange("p (j e u) -> p j e u", j=PLANES, u=2),
                 vt[b][:].rearrange("p j u e -> p j e u"),
             )
-            vc[b] = sb.tile([P, DV], U32, name="vc%d" % b, align_bytes=64)
-            if b == 0:
-                vsc[b] = shared.tile([P, DV], U8, name="vsc0", offset=0, align_bytes=64)
-            else:
-                vsc[b] = sb.tile([P, DV], U8, name="vsc1", align_bytes=64)
+            vsc[b] = sb.tile([P, DV], U8, name="vsc%d" % b, align_bytes=64)
             nc.vector.quantize_mx(out=vc[b][:].bitcast(FP8X4), scales=vsc[b][:], in_=vq[:])
 
         def quant_q(b):
             qb = sb.tile([P, NQ, PACK], BF16, name="qb%d" % b, align_bytes=64)
-            qc[b] = sb.tile([P, NQ], U32, name="qc%d" % b, align_bytes=64)
+            if b == 0:
+                qc[b] = shared.tile([P, NQ], U32, name="qc0", offset=LAST + 2048, align_bytes=64)
+            else:
+                qc[b] = sb.tile([P, NQ], U32, name="qc1", align_bytes=64)
             qsc[b] = sb.tile([P, NQ], U8, name="qsc%d" % b, align_bytes=64)
             if b == 0:
                 nc.scalar.activation(qb[:], qraw[b][:].rearrange("p j n -> p n j"), ACT.Copy)
@@ -185,15 +185,15 @@ def tile_attend_silu_seg_kernel(tc, qT, k_words, k_scales, vT, vs, offs, out):
                     start=True,
                     stop=True,
                 )
-            if b == 0:
-                pw[b] = shared.tile([P, NQ, PACK], F32, name="pw0", offset=1024, align_bytes=64)
-            else:
-                pw[b] = sb.tile([P, NQ, PACK], F32, name="pw1", align_bytes=64)
+            pw[b] = sb.tile([P, NQ, PACK], F32, name="pw%d" % b, align_bytes=64)
             for rows in parts(b):
                 nc.scalar.activation(pw[b][:, rows, :], z[b][:, :, rows].rearrange("p t q -> p q t"), ACT.Silu)
 
         def weigh(b):
-            wq[b] = sb.tile([P, NQ, PACK], BF16, name="wq%d" % b, tag="kw" if b == 0 else "wq1", align_bytes=64)
+            if b == 0:
+                wq[b] = shared.tile([P, NQ, PACK], BF16, name="wq0", offset=1024, align_bytes=64)
+            else:
+                wq[b] = sb.tile([P, NQ, PACK], BF16, name="wq1", align_bytes=64)
             for rows in parts(b):
                 scale = vst[b][:, :, P - 1 : P].rearrange("p t o -> p o t").to_broadcast([P, rows.stop - rows.start, PACK])
                 nc.vector.tensor_tensor(wq[b][:, rows, :], pw[b][:, rows, :], scale, MULT)
@@ -231,15 +231,15 @@ def tile_attend_silu_seg_kernel(tc, qT, k_words, k_scales, vT, vs, offs, out):
         gather_vs()
         listed_scales = gather_ks()
         gather_v(0, 0)
-        quant_q(0)
-        order_ks(listed_scales)
         gather_v(0, 1)
         gather_v(1, 0)
+        order_ks(listed_scales)
         gather_k(0)
         gather_v(1, 1)
+        quant_q(0)
         quant_q(1)
-        quant_v(0)
         gather_k(1)
+        quant_v(0)
         scores(0)
         weigh(0)
         quant_v(1)

@@ -24,6 +24,7 @@ COLS = N // 16
 PLANES = DV // P
 HALF = SEG // 2
 LAST = 4 * T
+THIRD = LAST + 2048
 
 
 def by_slot(t):
@@ -42,15 +43,19 @@ def tile_attend_silu_seg_kernel(tc, qT, k_words, k_scales, vT, vs, offs, out):
         ksc = sb.tile([P, T], U8, name="ksc", align_bytes=64)
         vsw = sb.tile([P, T], F32, name="vsw", align_bytes=64)
         vb = [sb.tile([P, T], BF16, name="vb%d" % j, align_bytes=64) for j in range(PLANES)]
-        qraw = [sb.tile([P, PACK, NQ], F32, name="qraw%d" % b, align_bytes=64) for b in range(B)]
+        qraw = [
+            sb.tile([P, PACK, NQ], F32, name="qraw0", align_bytes=64),
+            shared.tile([P, PACK, NQ], F32, name="qraw1", offset=LAST, align_bytes=64),
+        ]
         ident = sb.tile([P, P], F32, name="ident", align_bytes=64)
         warm = sb.tile([P, 8], F32, name="warm")
         warm2 = sb.tile([P, 8], F32, name="warm2")
 
+        nc.gpsimd.memset(warm[:], 0.0)
         nc.vector.memset(ksc[:, 0:SEG].bitcast(I32), 0)
         nc.gpsimd.memset(ksc[:, SEG:T].bitcast(I32), 0)
-        nc.vector.memset(vsw[0 : P - 1, :], 0.0)
-        nc.gpsimd.memset(warm[:], 0.0)
+        nc.vector.memset(vsw[0 : P - 1, 0:SEG], 0.0)
+        nc.gpsimd.memset(vsw[0 : P - 1, SEG:T], 0.0)
         make_identity(nc, ident[:])
 
         words = k_words[0].rearrange("p n t -> p (n t)").bitcast(I32)
@@ -61,8 +66,8 @@ def tile_attend_silu_seg_kernel(tc, qT, k_words, k_scales, vT, vs, offs, out):
             return slice(b * SEG, (b + 1) * SEG)
 
         def load_v(b, j):
-            if (b, j) == (1, 1):
-                vraw[b, j] = shared.tile([P, SEG], F32, name="vraw11", offset=LAST, align_bytes=64)
+            if (b, j) == (1, 0):
+                vraw[b, j] = shared.tile([P, SEG], F32, name="vraw10", offset=THIRD, align_bytes=64)
             else:
                 vraw[b, j] = sb.tile([P, SEG], F32, name="vraw%d%d" % (b, j), align_bytes=64)
             nc.sync.dma_start(out=vraw[b, j][:], in_=vT[j * P : (j + 1) * P, seg(b)])
@@ -98,7 +103,7 @@ def tile_attend_silu_seg_kernel(tc, qT, k_words, k_scales, vT, vs, offs, out):
         def end(b):
             return (b + 1) * SEG
 
-        kg, ksg = {}, {}
+        kg, ksg, qb, vq = {}, {}, {}, {}
         z, vst, vt, pw, wq = {}, {}, {}, {}, {}
         wc, wsc, vc, vsc, qc, qsc = {}, {}, {}, {}, {}, {}
 
@@ -112,7 +117,7 @@ def tile_attend_silu_seg_kernel(tc, qT, k_words, k_scales, vT, vs, offs, out):
             return listed
 
         def order_ks(listed):
-            both = sb.tile([P, PACK, B * P], U8, name="ksg", tag="vraw10", align_bytes=64)
+            both = shared.tile([P, PACK, B * P], U8, name="ksg", offset=THIRD + 2048, align_bytes=64)
             nc.vector.tensor_copy(
                 both[:].bitcast(I32).rearrange("x t (j r) -> x t j r", r=2),
                 listed[:].bitcast(I32).rearrange("x (j t r) -> x t j r", t=PACK, r=2),
@@ -128,7 +133,7 @@ def tile_attend_silu_seg_kernel(tc, qT, k_words, k_scales, vT, vs, offs, out):
                 for t in range(PACK):
                     nc.tensor.transpose(vst[b][:, t, :], both[:, t, b * P : (b + 1) * P].bitcast(F32), ident[:])
 
-        def gather_v(b, j):
+        def cast_v(b, j):
             if (b, j) == (0, 0):
                 nc.scalar.activation(vb[j][:, 0:HALF], vraw[b, j][:, 0:HALF], ACT.Copy)
                 nc.gpsimd.tensor_copy(vb[j][:, HALF:SEG], vraw[b, j][:, HALF:SEG])
@@ -136,7 +141,12 @@ def tile_attend_silu_seg_kernel(tc, qT, k_words, k_scales, vT, vs, offs, out):
                 nc.vector.tensor_copy(vb[j][:, seg(b)], vraw[b, j][:])
             else:
                 nc.gpsimd.tensor_copy(vb[j][:, seg(b)], vraw[b, j][:])
-            vg = sb.tile([P, N], BF16, name="vg%d%d" % (b, j), align_bytes=64)
+
+        def gather_v(b, j):
+            if (b, j) == (1, 1):
+                vg = shared.tile([P, N], BF16, name="vg11", offset=LAST, align_bytes=64)
+            else:
+                vg = sb.tile([P, N], BF16, name="vg%d%d" % (b, j), align_bytes=64)
             nc.scalar.activation(
                 vg[:].rearrange("x (g r t) -> x g t r", r=8, t=PACK), vb[j][:, 0 : end(b)].indirect(lst(b)), ACT.Copy
             )
@@ -146,32 +156,38 @@ def tile_attend_silu_seg_kernel(tc, qT, k_words, k_scales, vT, vs, offs, out):
             for u in range(2):
                 nc.tensor.transpose(vt[b][:, j, u, :], pairs[:, u : N // 2 : 2], ident[:])
 
-        def quant_v(b):
+        def empty_v(b):
             if b == 0:
-                vq = shared.tile([P, DV * PACK], BF16, name="vq0", offset=LAST, align_bytes=64)
-                vc[b] = shared.tile([P, DV], U32, name="vc0", offset=0, align_bytes=64)
+                vq[b] = shared.tile([P, DV * PACK], BF16, name="vq0", offset=THIRD, align_bytes=64)
             else:
-                vq = sb.tile([P, DV * PACK], BF16, name="vq1", align_bytes=64)
-                vc[b] = sb.tile([P, DV], U32, name="vc1", align_bytes=64)
+                vq[b] = sb.tile([P, DV * PACK], BF16, name="vq1", align_bytes=64)
             nc.scalar.copy(
-                vq[:].bitcast(F32).rearrange("p (j e u) -> p j e u", j=PLANES, u=2),
+                vq[b][:].bitcast(F32).rearrange("p (j e u) -> p j e u", j=PLANES, u=2),
                 vt[b][:].rearrange("p j u e -> p j e u"),
             )
+
+        def quant_v(b):
+            if b == 0:
+                vc[b] = shared.tile([P, DV], U32, name="vc0", offset=0, align_bytes=64)
+            else:
+                vc[b] = sb.tile([P, DV], U32, name="vc1", align_bytes=64)
             vsc[b] = sb.tile([P, DV], U8, name="vsc%d" % b, align_bytes=64)
-            nc.vector.quantize_mx(out=vc[b][:].bitcast(FP8X4), scales=vsc[b][:], in_=vq[:])
+            nc.vector.quantize_mx(out=vc[b][:].bitcast(FP8X4), scales=vsc[b][:], in_=vq[b][:])
+
+        def cast_q(b):
+            qb[b] = sb.tile([P, NQ, PACK], BF16, name="qb%d" % b, align_bytes=64)
+            if b == 0:
+                nc.scalar.activation(qb[b][:], qraw[b][:].rearrange("p j n -> p n j"), ACT.Copy)
+            else:
+                nc.vector.tensor_copy(qb[b][:], qraw[b][:].rearrange("p j n -> p n j"))
 
         def quant_q(b):
-            qb = sb.tile([P, NQ, PACK], BF16, name="qb%d" % b, align_bytes=64)
             if b == 0:
-                qc[b] = shared.tile([P, NQ], U32, name="qc0", offset=LAST + 2048, align_bytes=64)
+                qc[b] = shared.tile([P, NQ], U32, name="qc0", offset=LAST + 1024, align_bytes=64)
             else:
                 qc[b] = sb.tile([P, NQ], U32, name="qc1", align_bytes=64)
             qsc[b] = sb.tile([P, NQ], U8, name="qsc%d" % b, align_bytes=64)
-            if b == 0:
-                nc.scalar.activation(qb[:], qraw[b][:].rearrange("p j n -> p n j"), ACT.Copy)
-            else:
-                nc.vector.tensor_copy(qb[:], qraw[b][:].rearrange("p j n -> p n j"))
-            nc.vector.quantize_mx(out=qc[b][:].bitcast(FP8X4), scales=qsc[b][:], in_=qb[:].rearrange("p n j -> p (n j)"))
+            nc.vector.quantize_mx(out=qc[b][:].bitcast(FP8X4), scales=qsc[b][:], in_=qb[b][:].rearrange("p n j -> p (n j)"))
 
         def scores(b):
             z[b] = ps.tile([P, PACK, NQ], F32, name="z%d" % b)
@@ -230,21 +246,26 @@ def tile_attend_silu_seg_kernel(tc, qT, k_words, k_scales, vT, vs, offs, out):
 
         gather_vs()
         listed_scales = gather_ks()
-        gather_v(0, 0)
-        gather_v(0, 1)
-        gather_v(1, 0)
+        for b, j in ((0, 0), (0, 1), (1, 0)):
+            cast_v(b, j)
+            gather_v(b, j)
         order_ks(listed_scales)
         gather_k(0)
-        gather_v(1, 1)
+        empty_v(0)
+        cast_q(0)
+        cast_v(1, 1)
+        cast_q(1)
         quant_q(0)
         quant_q(1)
+        scores(0)
+        gather_v(1, 1)
         gather_k(1)
         quant_v(0)
-        scores(0)
         weigh(0)
+        empty_v(1)
+        quant_w(0)
         quant_v(1)
         scores(1)
-        quant_w(0)
         finish(0)
         weigh(1)
         quant_w(1)

@@ -83,10 +83,8 @@ def tile_attend_silu_seg_kernel(tc, qT, k_words, k_scales, vT, vs, offs, out):
         nc.scalar.activation(warm2[:], warm[:], ACT.Silu)
         load_v(0, 0)
         load_v(0, 1)
-        for quad in range(4):
-            nc.sync.dma_start(
-                out=ksc[32 * quad : 32 * quad + 4, :].bitcast(I32), in_=scale_rows[4 * quad : 4 * quad + 4, :]
-            )
+        for r in range(4):
+            nc.sync.dma_start(out=ksc[r:P:32, :].bitcast(I32), in_=scale_rows[r:16:4, :])
         load_v(1, 0)
         load_k(0)
         load_q(0)

@@ -28,7 +28,7 @@ THIRD = LAST + 2048
 
 
 def by_slot(t):
-    return t.rearrange("x t (j r) -> x j t r", r=8)
+    return t.rearrange("x t (j r) -> x j t r", r=4)
 
 
 def tile_attend_silu_seg_kernel(tc, qT, k_words, k_scales, vT, vs, offs, out):
@@ -117,8 +117,8 @@ def tile_attend_silu_seg_kernel(tc, qT, k_words, k_scales, vT, vs, offs, out):
         def order_ks(listed):
             both = shared.tile([P, PACK, B * P], U8, name="ksg", offset=THIRD + 2048, align_bytes=64)
             nc.vector.tensor_copy(
-                both[:].bitcast(I32).rearrange("x t (j r) -> x t j r", r=2),
-                listed[:].bitcast(I32).rearrange("x (j t r) -> x t j r", t=PACK, r=2),
+                both[:].bitcast(I32).rearrange("x t (a i) -> x a t i", i=4),
+                listed[:].bitcast(I32).rearrange("x (a i t) -> x a t i", i=4, t=PACK),
             )
             for b in range(B):
                 ksg[b] = both[:, :, b * P : (b + 1) * P]
@@ -146,7 +146,7 @@ def tile_attend_silu_seg_kernel(tc, qT, k_words, k_scales, vT, vs, offs, out):
             else:
                 vg = sb.tile([P, N], BF16, name="vg%d%d" % (b, j), align_bytes=64)
             nc.scalar.activation(
-                vg[:].rearrange("x (g r t) -> x g t r", r=8, t=PACK), vb[j][:, 0 : end(b)].indirect(lst(b)), ACT.Copy
+                vg[:].rearrange("x (g r t) -> x g t r", r=4, t=PACK), vb[j][:, 0 : end(b)].indirect(lst(b)), ACT.Copy
             )
             if j == 0:
                 vt[b] = ps.tile([P, PLANES, 2, P], F32, name="vt%d" % b)
@@ -174,10 +174,12 @@ def tile_attend_silu_seg_kernel(tc, qT, k_words, k_scales, vT, vs, offs, out):
 
         def cast_q(b):
             qb[b] = sb.tile([P, NQ, PACK], BF16, name="qb%d" % b, align_bytes=64)
+            dst = qb[b][:].rearrange("p (c i) j -> p c j i", i=4)
+            src = qraw[b][:].rearrange("p j (c i) -> p c j i", i=4)
             if b == 0:
-                nc.scalar.activation(qb[b][:], qraw[b][:].rearrange("p j n -> p n j"), ACT.Copy)
+                nc.scalar.activation(dst, src, ACT.Copy)
             else:
-                nc.vector.tensor_copy(qb[b][:], qraw[b][:].rearrange("p j n -> p n j"))
+                nc.vector.tensor_copy(dst, src)
 
         def quant_q(b):
             if b == 0:

@@ -23,8 +23,8 @@ SEG = T // B
 COLS = N // 16
 PLANES = DV // P
 HALF = SEG // 2
-LAST = 4 * T
-THIRD = LAST + 2048
+QRAW = [0, 2048]
+QCODE = 4096
 
 
 def by_slot(t):
@@ -39,14 +39,12 @@ def tile_attend_silu_seg_kernel(tc, qT, k_words, k_scales, vT, vs, offs, out):
         ps = ctx.enter_context(tc.psum_pool(name="ps", bufs=1))
 
         offsets = sb.tile([P, B * COLS], U16, name="offsets")
-        kw = shared.tile([P, T], I32, name="kw", offset=0, align_bytes=64)
+        kw = sb.tile([P, T], I32, name="kw", align_bytes=64)
         ksc = sb.tile([P, T], U8, name="ksc", align_bytes=64)
         vsw = sb.tile([P, T], F32, name="vsw", align_bytes=64)
-        vb = [sb.tile([P, T], BF16, name="vb%d" % j, align_bytes=64) for j in range(PLANES)]
-        qraw = [
-            sb.tile([P, PACK, NQ], F32, name="qraw0", align_bytes=64),
-            shared.tile([P, PACK, NQ], F32, name="qraw1", offset=LAST, align_bytes=64),
-        ]
+        vb = [sb.tile([P, T // (j + 1)], BF16, name="vb%d" % j, align_bytes=64) for j in range(PLANES)]
+        vf = [sb.tile([P, T], F32, name="vf%d" % j, align_bytes=64) for j in range(PLANES)]
+        qraw = [shared.tile([P, PACK, NQ], F32, name="qraw%d" % b, offset=QRAW[b], align_bytes=64) for b in range(B)]
         ident = sb.tile([P, P], F32, name="ident", align_bytes=64)
         warm = sb.tile([P, 8], F32, name="warm")
         warm2 = sb.tile([P, 8], F32, name="warm2")
@@ -66,11 +64,8 @@ def tile_attend_silu_seg_kernel(tc, qT, k_words, k_scales, vT, vs, offs, out):
             return slice(b * SEG, (b + 1) * SEG)
 
         def load_v(b, j):
-            if (b, j) == (1, 0):
-                vraw[b, j] = shared.tile([P, SEG], F32, name="vraw10", offset=THIRD, align_bytes=64)
-            else:
-                vraw[b, j] = sb.tile([P, SEG], F32, name="vraw%d%d" % (b, j), align_bytes=64)
-            nc.sync.dma_start(out=vraw[b, j][:], in_=vT[j * P : (j + 1) * P, seg(b)])
+            vraw[b, j] = vf[j][:, seg(b)]
+            nc.sync.dma_start(out=vraw[b, j], in_=vT[j * P : (j + 1) * P, seg(b)])
 
         def load_k(b):
             nc.sync.dma_start(out=kw[:, seg(b)], in_=words[:, seg(b)])
@@ -87,13 +82,10 @@ def tile_attend_silu_seg_kernel(tc, qT, k_words, k_scales, vT, vs, offs, out):
             nc.sync.dma_start(out=ksc[r:P:32, :].bitcast(I32), in_=scale_rows[r:16:4, :])
         load_v(1, 0)
         load_k(0)
-        load_q(0)
-        load_v(1, 1)
-        load_q(1)
         load_k(1)
-
-        def parts(b):
-            return [slice(0, NQ)] if b == 0 else [slice(0, NQ // 2), slice(NQ // 2, NQ)]
+        load_q(0)
+        load_q(1)
+        load_v(1, 1)
 
         def lst(b):
             return offsets[:, b * COLS : (b + 1) * COLS]
@@ -115,7 +107,7 @@ def tile_attend_silu_seg_kernel(tc, qT, k_words, k_scales, vT, vs, offs, out):
             return listed
 
         def order_ks(listed):
-            both = shared.tile([P, PACK, B * P], U8, name="ksg", offset=THIRD + 2048, align_bytes=64)
+            both = shared.tile([P, PACK, B * P], U8, name="ksg", offset=QRAW[0], align_bytes=64)
             nc.vector.tensor_copy(
                 both[:].bitcast(I32).rearrange("x t (a i) -> x a t i", i=4),
                 listed[:].bitcast(I32).rearrange("x (a i t) -> x a t i", i=4, t=PACK),
@@ -133,44 +125,42 @@ def tile_attend_silu_seg_kernel(tc, qT, k_words, k_scales, vT, vs, offs, out):
 
         def cast_v(b, j):
             if (b, j) == (0, 0):
-                nc.scalar.activation(vb[j][:, 0:HALF], vraw[b, j][:, 0:HALF], ACT.Copy)
-                nc.gpsimd.tensor_copy(vb[j][:, HALF:SEG], vraw[b, j][:, HALF:SEG])
-            elif (b, j) == (1, 1):
-                nc.vector.tensor_copy(vb[j][:, seg(b)], vraw[b, j][:])
+                nc.scalar.activation(vb[j][:, 0:HALF], vf[j][:, 0:HALF], ACT.Copy)
+                nc.gpsimd.tensor_copy(vb[j][:, HALF:SEG], vf[j][:, HALF:SEG])
             else:
-                nc.gpsimd.tensor_copy(vb[j][:, seg(b)], vraw[b, j][:])
+                nc.gpsimd.tensor_copy(vb[j][:, seg(b)], vraw[b, j])
 
         def gather_v(b, j):
+            vg = sb.tile([P, N], BF16, name="vg%d%d" % (b, j), align_bytes=64)
+            dealt = vg[:].rearrange("x (g r t) -> x g t r", r=4, t=PACK)
             if (b, j) == (1, 1):
-                vg = shared.tile([P, N], BF16, name="vg11", offset=LAST, align_bytes=64)
+                nc.vector.tensor_copy(dealt, vf[j][:].indirect(lst(b)))
             else:
-                vg = sb.tile([P, N], BF16, name="vg%d%d" % (b, j), align_bytes=64)
-            nc.scalar.activation(
-                vg[:].rearrange("x (g r t) -> x g t r", r=4, t=PACK), vb[j][:, 0 : end(b)].indirect(lst(b)), ACT.Copy
-            )
+                nc.scalar.activation(dealt, vb[j][:, 0 : end(b)].indirect(lst(b)), ACT.Copy)
             if j == 0:
                 vt[b] = ps.tile([P, PLANES, 2, P], F32, name="vt%d" % b)
             pairs = vg[:].bitcast(F32)
             for u in range(2):
                 nc.tensor.transpose(vt[b][:, j, u, :], pairs[:, u : N // 2 : 2], ident[:])
 
-        def empty_v(b):
-            if b == 0:
-                vq[b] = shared.tile([P, DV * PACK], BF16, name="vq0", offset=THIRD, align_bytes=64)
+        def empty_v(b, planes):
+            j = planes[0]
+            if (b, j) == (1, 1):
+                vq[b, j] = sb.tile([P, P * PACK], BF16, name="vq11", align_bytes=64)
             else:
-                vq[b] = sb.tile([P, DV * PACK], BF16, name="vq1", align_bytes=64)
+                at = 1024 if b == 0 else 3072
+                vq[b, j] = shared.tile([P, len(planes) * P * PACK], BF16, name="vq%d%d" % (b, j), offset=at, align_bytes=64)
             nc.scalar.copy(
-                vq[b][:].bitcast(F32).rearrange("p (j e u) -> p j e u", j=PLANES, u=2),
-                vt[b][:].rearrange("p j u e -> p j e u"),
+                vq[b, j][:].bitcast(F32).rearrange("p (j e u) -> p j e u", j=len(planes), u=2),
+                vt[b][:, planes[0] : planes[-1] + 1, :, :].rearrange("p j u e -> p j e u"),
             )
 
-        def quant_v(b):
-            if b == 0:
-                vc[b] = shared.tile([P, DV], U32, name="vc0", offset=0, align_bytes=64)
-            else:
-                vc[b] = sb.tile([P, DV], U32, name="vc1", align_bytes=64)
-            vsc[b] = sb.tile([P, DV], U8, name="vsc%d" % b, align_bytes=64)
-            nc.vector.quantize_mx(out=vc[b][:].bitcast(FP8X4), scales=vsc[b][:], in_=vq[b][:])
+        def quant_v(b, planes):
+            if planes[0] == 0:
+                vc[b] = shared.tile([P, DV], U32, name="vc%d" % b, offset=QCODE + 1024 * b, align_bytes=64)
+                vsc[b] = sb.tile([P, DV], U8, name="vsc%d" % b, align_bytes=64)
+            cols = slice(planes[0] * P, (planes[-1] + 1) * P)
+            nc.vector.quantize_mx(out=vc[b][:, cols].bitcast(FP8X4), scales=vsc[b][:, cols], in_=vq[b, planes[0]][:])
 
         def cast_q(b):
             qb[b] = sb.tile([P, NQ, PACK], BF16, name="qb%d" % b, align_bytes=64)
@@ -182,10 +172,7 @@ def tile_attend_silu_seg_kernel(tc, qT, k_words, k_scales, vT, vs, offs, out):
                 nc.vector.tensor_copy(dst, src)
 
         def quant_q(b):
-            if b == 0:
-                qc[b] = shared.tile([P, NQ], U32, name="qc0", offset=LAST + 1024, align_bytes=64)
-            else:
-                qc[b] = sb.tile([P, NQ], U32, name="qc1", align_bytes=64)
+            qc[b] = shared.tile([P, NQ], U32, name="qc%d" % b, offset=QCODE + 1024 * b, align_bytes=64)
             qsc[b] = sb.tile([P, NQ], U8, name="qsc%d" % b, align_bytes=64)
             nc.vector.quantize_mx(out=qc[b][:].bitcast(FP8X4), scales=qsc[b][:], in_=qb[b][:].rearrange("p n j -> p (n j)"))
 
@@ -202,27 +189,17 @@ def tile_attend_silu_seg_kernel(tc, qT, k_words, k_scales, vT, vs, offs, out):
                     stop=True,
                 )
             pw[b] = sb.tile([P, NQ, PACK], F32, name="pw%d" % b, align_bytes=64)
-            for rows in parts(b):
-                nc.scalar.activation(pw[b][:, rows, :], z[b][:, :, rows].rearrange("p t q -> p q t"), ACT.Silu)
+            nc.scalar.activation(pw[b][:], z[b][:].rearrange("p t q -> p q t"), ACT.Silu)
 
         def weigh(b):
-            if b == 0:
-                wq[b] = shared.tile([P, NQ, PACK], BF16, name="wq0", offset=1024, align_bytes=64)
-            else:
-                wq[b] = sb.tile([P, NQ, PACK], BF16, name="wq1", align_bytes=64)
-            for rows in parts(b):
-                scale = vst[b][:, :, P - 1 : P].rearrange("p t o -> p o t").to_broadcast([P, rows.stop - rows.start, PACK])
-                nc.vector.tensor_tensor(wq[b][:, rows, :], pw[b][:, rows, :], scale, MULT)
+            wq[b] = sb.tile([P, NQ, PACK], BF16, name="wq%d" % b, align_bytes=64)
+            scale = vst[b][:, :, P - 1 : P].rearrange("p t o -> p o t").to_broadcast([P, NQ, PACK])
+            nc.vector.tensor_tensor(wq[b][:], pw[b][:], scale, MULT)
 
         def quant_w(b):
             wc[b] = sb.tile([P, NQ], U32, name="wc%d" % b, align_bytes=64)
             wsc[b] = sb.tile([P, NQ], U8, name="wsc%d" % b, align_bytes=64)
-            for rows in parts(b):
-                nc.vector.quantize_mx(
-                    out=wc[b][:, rows].bitcast(FP8X4),
-                    scales=wsc[b][:, rows],
-                    in_=wq[b][:, rows, :].rearrange("p q t -> p (q t)"),
-                )
+            nc.vector.quantize_mx(out=wc[b][:].bitcast(FP8X4), scales=wsc[b][:], in_=wq[b][:].rearrange("p q t -> p (q t)"))
 
         def finish(b):
             res = sb.tile([P, DV], F32, name="res%d" % b, align_bytes=64)
@@ -249,24 +226,25 @@ def tile_attend_silu_seg_kernel(tc, qT, k_words, k_scales, vT, vs, offs, out):
         for b, j in ((0, 0), (0, 1), (1, 0)):
             cast_v(b, j)
             gather_v(b, j)
-        order_ks(listed_scales)
         gather_k(0)
-        empty_v(0)
+        gather_k(1)
         cast_q(0)
-        cast_v(1, 1)
         cast_q(1)
+        order_ks(listed_scales)
         quant_q(0)
         quant_q(1)
+        empty_v(0, [0, 1])
+        empty_v(1, [0])
         scores(0)
-        gather_v(1, 1)
-        gather_k(1)
-        quant_v(0)
-        weigh(0)
-        empty_v(1)
-        quant_w(0)
-        quant_v(1)
         scores(1)
-        finish(0)
+        gather_v(1, 1)
+        quant_v(0, [0, 1])
+        quant_v(1, [0])
+        empty_v(1, [1])
+        weigh(0)
         weigh(1)
+        quant_w(0)
+        quant_v(1, [1])
         quant_w(1)
+        finish(0)
         finish(1)

@@ -130,13 +130,24 @@ def tile_attend_silu_seg_kernel(tc, qT, k_words, k_scales, vT, vs, offs, out):
             else:
                 nc.gpsimd.tensor_copy(vb[j][:, seg(b)], vraw[b, j])
 
+        def gather_last():
+            vg = sb.tile([P, PACK, P], U32, name="vglast", align_bytes=64)
+            nc.vector.tensor_copy(by_slot(vg[:]), vf[1][:].bitcast(U32).indirect(lst(1)))
+            turned = ps.tile([P, PACK, P], F32, name="vtlast", tag="vt0")
+            for t in range(PACK):
+                nc.tensor.transpose(turned[:, t, :], vg[:, t, :].bitcast(F32), ident[:])
+            return turned
+
+        def empty_last(turned):
+            vq[1, 1] = sb.tile([P, P * PACK], BF16, name="vq11", align_bytes=64)
+            nc.scalar.activation(
+                vq[1, 1][:].rearrange("p (e t) -> p e t", t=PACK), turned[:].rearrange("p t e -> p e t"), ACT.Copy
+            )
+
         def gather_v(b, j):
             vg = sb.tile([P, N], BF16, name="vg%d%d" % (b, j), align_bytes=64)
             dealt = vg[:].rearrange("x (g r t) -> x g t r", r=4, t=PACK)
-            if (b, j) == (1, 1):
-                nc.vector.tensor_copy(dealt, vf[j][:].indirect(lst(b)))
-            else:
-                nc.scalar.activation(dealt, vb[j][:, 0 : end(b)].indirect(lst(b)), ACT.Copy)
+            nc.scalar.activation(dealt, vb[j][:, 0 : end(b)].indirect(lst(b)), ACT.Copy)
             if j == 0:
                 vt[b] = ps.tile([P, PLANES, 2, P], F32, name="vt%d" % b)
             pairs = vg[:].bitcast(F32)
@@ -145,11 +156,8 @@ def tile_attend_silu_seg_kernel(tc, qT, k_words, k_scales, vT, vs, offs, out):
 
         def empty_v(b, planes):
             j = planes[0]
-            if (b, j) == (1, 1):
-                vq[b, j] = sb.tile([P, P * PACK], BF16, name="vq11", align_bytes=64)
-            else:
-                at = 1024 if b == 0 else 3072
-                vq[b, j] = shared.tile([P, len(planes) * P * PACK], BF16, name="vq%d%d" % (b, j), offset=at, align_bytes=64)
+            at = 1024 if b == 0 else 3072
+            vq[b, j] = shared.tile([P, len(planes) * P * PACK], BF16, name="vq%d%d" % (b, j), offset=at, align_bytes=64)
             nc.scalar.copy(
                 vq[b, j][:].bitcast(F32).rearrange("p (j e u) -> p j e u", j=len(planes), u=2),
                 vt[b][:, planes[0] : planes[-1] + 1, :, :].rearrange("p j u e -> p j e u"),
@@ -205,7 +213,7 @@ def tile_attend_silu_seg_kernel(tc, qT, k_words, k_scales, vT, vs, offs, out):
             res = sb.tile([P, DV], F32, name="res%d" % b, align_bytes=64)
             halves = [slice(0, DV)] if b == 0 else [slice(0, DV // 2), slice(DV // 2, DV)]
             for h, cols in enumerate(halves):
-                y = ps.tile([P, cols.stop - cols.start], F32, name="y%d%d" % (b, h), tag="y%d" % b if h == 0 else "vt0")
+                y = ps.tile([P, cols.stop - cols.start], F32, name="y%d%d" % (b, h), tag="y%d" % b if h == 0 else "z0")
                 nc.tensor.matmul_mx(
                     out=y[:],
                     lhsT=wc[b][:].bitcast(FP8X4),
@@ -237,10 +245,10 @@ def tile_attend_silu_seg_kernel(tc, qT, k_words, k_scales, vT, vs, offs, out):
         empty_v(1, [0])
         scores(0)
         scores(1)
-        gather_v(1, 1)
+        turned_last = gather_last()
         quant_v(0, [0, 1])
         quant_v(1, [0])
-        empty_v(1, [1])
+        empty_last(turned_last)
         weigh(0)
         weigh(1)
         quant_w(0)

@@ -131,17 +131,18 @@ def tile_attend_silu_seg_kernel(tc, qT, k_words, k_scales, vT, vs, offs, out):
                 nc.gpsimd.tensor_copy(vb[j][:, seg(b)], vraw[b, j])
 
         def gather_last():
-            vg = sb.tile([P, PACK, P], U32, name="vglast", align_bytes=64)
-            nc.vector.tensor_copy(by_slot(vg[:]), vf[1][:].bitcast(U32).indirect(lst(1)))
-            turned = ps.tile([P, PACK, P], F32, name="vtlast", tag="vt0")
-            for t in range(PACK):
-                nc.tensor.transpose(turned[:, t, :], vg[:, t, :].bitcast(F32), ident[:])
+            vg = sb.tile([P, N], BF16, name="vglast", align_bytes=64)
+            nc.vector.tensor_copy(vg[:].rearrange("x (g r t) -> x g t r", r=4, t=PACK), vf[1][:].indirect(lst(1)))
+            turned = ps.tile([P, 2, P], F32, name="vtlast", tag="vt0")
+            pairs = vg[:].bitcast(F32)
+            for u in range(2):
+                nc.tensor.transpose(turned[:, u, :], pairs[:, u : N // 2 : 2], ident[:])
             return turned
 
         def empty_last(turned):
             vq[1, 1] = sb.tile([P, P * PACK], BF16, name="vq11", align_bytes=64)
-            nc.scalar.activation(
-                vq[1, 1][:].rearrange("p (e t) -> p e t", t=PACK), turned[:].rearrange("p t e -> p e t"), ACT.Copy
+            nc.scalar.copy(
+                vq[1, 1][:].bitcast(F32).rearrange("p (e u) -> p e u", u=2), turned[:].rearrange("p u e -> p e u")
             )
 
         def gather_v(b, j):
@@ -174,10 +175,7 @@ def tile_attend_silu_seg_kernel(tc, qT, k_words, k_scales, vT, vs, offs, out):
             qb[b] = sb.tile([P, NQ, PACK], BF16, name="qb%d" % b, align_bytes=64)
             dst = qb[b][:].rearrange("p (c i) j -> p c j i", i=4)
             src = qraw[b][:].rearrange("p j (c i) -> p c j i", i=4)
-            if b == 0:
-                nc.scalar.activation(dst, src, ACT.Copy)
-            else:
-                nc.vector.tensor_copy(dst, src)
+            nc.scalar.activation(dst, src, ACT.Copy)
 
         def quant_q(b):
             qc[b] = shared.tile([P, NQ], U32, name="qc%d" % b, offset=QCODE + 1024 * b, align_bytes=64)
@@ -200,7 +198,10 @@ def tile_attend_silu_seg_kernel(tc, qT, k_words, k_scales, vT, vs, offs, out):
             nc.scalar.activation(pw[b][:], z[b][:].rearrange("p t q -> p q t"), ACT.Silu)
 
         def weigh(b):
-            wq[b] = sb.tile([P, NQ, PACK], BF16, name="wq%d" % b, align_bytes=64)
+            if b == 0:
+                wq[b] = sb.tile([P, NQ, PACK], BF16, name="wq0", align_bytes=64)
+            else:
+                wq[b] = shared.tile([P, NQ, PACK], BF16, name="wq1", offset=3072, align_bytes=64)
             scale = vst[b][:, :, P - 1 : P].rearrange("p t o -> p o t").to_broadcast([P, NQ, PACK])
             nc.vector.tensor_tensor(wq[b][:], pw[b][:], scale, MULT)
 
@@ -247,11 +248,11 @@ def tile_attend_silu_seg_kernel(tc, qT, k_words, k_scales, vT, vs, offs, out):
         scores(1)
         turned_last = gather_last()
         quant_v(0, [0, 1])
-        quant_v(1, [0])
         empty_last(turned_last)
         weigh(0)
-        weigh(1)
+        quant_v(1, [0])
         quant_w(0)
+        weigh(1)
         quant_v(1, [1])
         quant_w(1)
         finish(0)

@@ -212,9 +212,9 @@ def tile_attend_silu_seg_kernel(tc, qT, k_words, k_scales, vT, vs, offs, out):
 
         def finish(b):
             res = sb.tile([P, DV], F32, name="res%d" % b, align_bytes=64)
-            halves = [slice(0, DV)] if b == 0 else [slice(0, DV // 2), slice(DV // 2, DV)]
-            for h, cols in enumerate(halves):
-                y = ps.tile([P, cols.stop - cols.start], F32, name="y%d%d" % (b, h), tag="y%d" % b if h == 0 else "z0")
+            for h in range(PLANES):
+                cols = slice(h * P, (h + 1) * P)
+                y = ps.tile([P, P], F32, name="y%d%d" % (b, h), tag="y%d" % b if h == 0 else "z%d" % b)
                 nc.tensor.matmul_mx(
                     out=y[:],
                     lhsT=wc[b][:].bitcast(FP8X4),
@@ -253,7 +253,7 @@ def tile_attend_silu_seg_kernel(tc, qT, k_words, k_scales, vT, vs, offs, out):
         quant_v(1, [0])
         quant_w(0)
         weigh(1)
-        quant_v(1, [1])
         quant_w(1)
+        quant_v(1, [1])
         finish(0)
         finish(1)

@@ -23,8 +23,12 @@ SEG = T // B
 COLS = N // 16
 PLANES = DV // P
 HALF = SEG // 2
-QRAW = [0, 2048]
-QCODE = 4096
+VB0 = 0
+VQ0 = VB0 + 1024
+QRAW = [4608, 7168]
+QB1 = 9216
+PW1 = 11008
+VC = [PW1 - 768, PW1 + 768]
 
 
 def by_slot(t):
@@ -42,7 +46,10 @@ def tile_attend_silu_seg_kernel(tc, qT, k_words, k_scales, vT, vs, offs, out):
         kw = sb.tile([P, T], I32, name="kw", align_bytes=64)
         ksc = sb.tile([P, T], U8, name="ksc", align_bytes=64)
         vsw = sb.tile([P, T], F32, name="vsw", align_bytes=64)
-        vb = [sb.tile([P, T // (j + 1)], BF16, name="vb%d" % j, align_bytes=64) for j in range(PLANES)]
+        vb = [
+            shared.tile([P, T], BF16, name="vb0", offset=VB0, align_bytes=64),
+            sb.tile([P, SEG], BF16, name="vb1", align_bytes=64),
+        ]
         vf = [sb.tile([P, T], F32, name="vf%d" % j, align_bytes=64) for j in range(PLANES)]
         qraw = [shared.tile([P, PACK, NQ], F32, name="qraw%d" % b, offset=QRAW[b], align_bytes=64) for b in range(B)]
         ident = sb.tile([P, P], F32, name="ident", align_bytes=64)
@@ -82,8 +89,8 @@ def tile_attend_silu_seg_kernel(tc, qT, k_words, k_scales, vT, vs, offs, out):
             nc.sync.dma_start(out=ksc[r:P:32, :].bitcast(I32), in_=scale_rows[r:16:4, :])
         load_v(1, 0)
         load_k(0)
-        load_k(1)
         load_q(0)
+        load_k(1)
         load_q(1)
         load_v(1, 1)
 
@@ -98,7 +105,10 @@ def tile_attend_silu_seg_kernel(tc, qT, k_words, k_scales, vT, vs, offs, out):
         wc, wsc, vc, vsc, qc, qsc = {}, {}, {}, {}, {}, {}
 
         def gather_k(b):
-            kg[b] = sb.tile([P, PACK, P], U32, name="kg%d" % b, align_bytes=64)
+            if b == 0:
+                kg[b] = sb.tile([P, PACK, P], U32, name="kg0", align_bytes=64)
+            else:
+                kg[b] = shared.tile([P, PACK, P], U32, name="kg1", offset=QRAW[0] + 512, align_bytes=64)
             nc.vector.tensor_copy(by_slot(kg[b][:]), kw[:, 0 : end(b)].bitcast(U32).indirect(lst(b)))
 
         def gather_ks():
@@ -107,7 +117,7 @@ def tile_attend_silu_seg_kernel(tc, qT, k_words, k_scales, vT, vs, offs, out):
             return listed
 
         def order_ks(listed):
-            both = shared.tile([P, PACK, B * P], U8, name="ksg", offset=QRAW[0], align_bytes=64)
+            both = shared.tile([P, PACK, B * P], U8, name="ksg", offset=QRAW[0] - 512, align_bytes=64)
             nc.vector.tensor_copy(
                 both[:].bitcast(I32).rearrange("x t (a i) -> x a t i", i=4),
                 listed[:].bitcast(I32).rearrange("x (a i t) -> x a t i", i=4, t=PACK),
@@ -131,12 +141,12 @@ def tile_attend_silu_seg_kernel(tc, qT, k_words, k_scales, vT, vs, offs, out):
                 nc.gpsimd.tensor_copy(vb[j][:, seg(b)], vraw[b, j])
 
         def gather_last():
-            vg = sb.tile([P, N], BF16, name="vglast", align_bytes=64)
-            nc.vector.tensor_copy(vg[:].rearrange("x (g r t) -> x g t r", r=4, t=PACK), vf[1][:].indirect(lst(1)))
+            vg = shared.tile([P, N], BF16, name="vglast", offset=QRAW[1], align_bytes=64)
+            nc.vector.tensor_copy(vg[:].rearrange("x (u g r e) -> x g u e r", u=2, r=4, e=2), vf[1][:].indirect(lst(1)))
             turned = ps.tile([P, 2, P], F32, name="vtlast", tag="vt0")
             pairs = vg[:].bitcast(F32)
             for u in range(2):
-                nc.tensor.transpose(turned[:, u, :], pairs[:, u : N // 2 : 2], ident[:])
+                nc.tensor.transpose(turned[:, u, :], pairs[:, u * P : (u + 1) * P], ident[:])
             return turned
 
         def empty_last(turned):
@@ -157,8 +167,10 @@ def tile_attend_silu_seg_kernel(tc, qT, k_words, k_scales, vT, vs, offs, out):
 
         def empty_v(b, planes):
             j = planes[0]
-            at = 1024 if b == 0 else 3072
-            vq[b, j] = shared.tile([P, len(planes) * P * PACK], BF16, name="vq%d%d" % (b, j), offset=at, align_bytes=64)
+            if b == 0:
+                vq[b, j] = shared.tile([P, len(planes) * P * PACK], BF16, name="vq00", offset=VQ0, align_bytes=64)
+            else:
+                vq[b, j] = sb.tile([P, len(planes) * P * PACK], BF16, name="vq10", align_bytes=64)
             nc.scalar.copy(
                 vq[b, j][:].bitcast(F32).rearrange("p (j e u) -> p j e u", j=len(planes), u=2),
                 vt[b][:, planes[0] : planes[-1] + 1, :, :].rearrange("p j u e -> p j e u"),
@@ -166,19 +178,20 @@ def tile_attend_silu_seg_kernel(tc, qT, k_words, k_scales, vT, vs, offs, out):
 
         def quant_v(b, planes):
             if planes[0] == 0:
-                vc[b] = shared.tile([P, DV], U32, name="vc%d" % b, offset=QCODE + 1024 * b, align_bytes=64)
+                vc[b] = shared.tile([P, DV], U32, name="vc%d" % b, offset=VC[b], align_bytes=64)
                 vsc[b] = sb.tile([P, DV], U8, name="vsc%d" % b, align_bytes=64)
             cols = slice(planes[0] * P, (planes[-1] + 1) * P)
             nc.vector.quantize_mx(out=vc[b][:, cols].bitcast(FP8X4), scales=vsc[b][:, cols], in_=vq[b, planes[0]][:])
 
         def cast_q(b):
-            qb[b] = sb.tile([P, NQ, PACK], BF16, name="qb%d" % b, align_bytes=64)
-            dst = qb[b][:].rearrange("p (c i) j -> p c j i", i=4)
-            src = qraw[b][:].rearrange("p j (c i) -> p c j i", i=4)
-            nc.scalar.activation(dst, src, ACT.Copy)
+            if b == 0:
+                qb[b] = sb.tile([P, NQ, PACK], BF16, name="qb0", align_bytes=64)
+            else:
+                qb[b] = shared.tile([P, NQ, PACK], BF16, name="qb1", offset=QB1, align_bytes=64)
+            nc.gpsimd.tensor_copy(qb[b][:], qraw[b][:].rearrange("p j n -> p n j"))
 
         def quant_q(b):
-            qc[b] = shared.tile([P, NQ], U32, name="qc%d" % b, offset=QCODE + 1024 * b, align_bytes=64)
+            qc[b] = sb.tile([P, NQ], U32, name="qc%d" % b, align_bytes=64)
             qsc[b] = sb.tile([P, NQ], U8, name="qsc%d" % b, align_bytes=64)
             nc.vector.quantize_mx(out=qc[b][:].bitcast(FP8X4), scales=qsc[b][:], in_=qb[b][:].rearrange("p n j -> p (n j)"))
 
@@ -194,27 +207,44 @@ def tile_attend_silu_seg_kernel(tc, qT, k_words, k_scales, vT, vs, offs, out):
                     start=True,
                     stop=True,
                 )
-            pw[b] = sb.tile([P, NQ, PACK], F32, name="pw%d" % b, align_bytes=64)
-            nc.scalar.activation(pw[b][:], z[b][:].rearrange("p t q -> p q t"), ACT.Silu)
+            width = NQ // (b + 1)
+            for h in range(b + 1):
+                if (b, h) == (1, 0):
+                    pw[b, h] = shared.tile([P, width, PACK], F32, name="pw10", offset=PW1, align_bytes=64)
+                else:
+                    pw[b, h] = sb.tile([P, width, PACK], F32, name="pw%d%d" % (b, h), align_bytes=64)
+                scored = z[b][:, :, h * width : (h + 1) * width]
+                nc.scalar.activation(pw[b, h][:], scored.rearrange("p t q -> p q t"), ACT.Silu)
+
+        def token_scales(b):
+            return vst[b][:, :, P - 1 : P].rearrange("p t o -> p o t")
+
+        held = shared.tile([P, 1, PACK], F32, name="held", offset=VQ0 + 2048, align_bytes=64)
 
         def weigh(b):
             if b == 0:
-                wq[b] = sb.tile([P, NQ, PACK], BF16, name="wq0", align_bytes=64)
+                wq[b] = shared.tile([P, NQ, PACK], BF16, name="wq0", offset=QB1, align_bytes=64)
+                nc.gpsimd.tensor_tensor(wq[b][:], pw[b, 0][:], held[:].to_broadcast([P, NQ, PACK]), MULT)
             else:
-                wq[b] = shared.tile([P, NQ, PACK], BF16, name="wq1", offset=3072, align_bytes=64)
-            scale = vst[b][:, :, P - 1 : P].rearrange("p t o -> p o t").to_broadcast([P, NQ, PACK])
-            nc.vector.tensor_tensor(wq[b][:], pw[b][:], scale, MULT)
+                wq[b] = sb.tile([P, NQ, PACK], BF16, name="wq1", align_bytes=64)
+                for h in range(2):
+                    scale = token_scales(b).to_broadcast([P, NQ // 2, PACK])
+                    nc.vector.tensor_tensor(wq[b][:, h * (NQ // 2) : (h + 1) * (NQ // 2), :], pw[b, h][:], scale, MULT)
 
         def quant_w(b):
-            wc[b] = sb.tile([P, NQ], U32, name="wc%d" % b, align_bytes=64)
+            if b == 0:
+                wc[b] = shared.tile([P, NQ], U32, name="wc0", offset=PW1 + 256, align_bytes=64)
+            else:
+                wc[b] = sb.tile([P, NQ], U32, name="wc1", align_bytes=64)
             wsc[b] = sb.tile([P, NQ], U8, name="wsc%d" % b, align_bytes=64)
             nc.vector.quantize_mx(out=wc[b][:].bitcast(FP8X4), scales=wsc[b][:], in_=wq[b][:].rearrange("p q t -> p (q t)"))
 
         def finish(b):
             res = sb.tile([P, DV], F32, name="res%d" % b, align_bytes=64)
-            for h in range(PLANES):
-                cols = slice(h * P, (h + 1) * P)
-                y = ps.tile([P, P], F32, name="y%d%d" % (b, h), tag="y%d" % b if h == 0 else "z%d" % b)
+            width = DV // (b + 1)
+            for h in range(b + 1):
+                cols = slice(h * width, (h + 1) * width)
+                y = ps.tile([P, width], F32, name="y%d%d" % (b, h), tag="y%d" % b if h == 0 else "z%d" % b)
                 nc.tensor.matmul_mx(
                     out=y[:],
                     lhsT=wc[b][:].bitcast(FP8X4),
@@ -236,23 +266,24 @@ def tile_attend_silu_seg_kernel(tc, qT, k_words, k_scales, vT, vs, offs, out):
             cast_v(b, j)
             gather_v(b, j)
         gather_k(0)
-        gather_k(1)
-        cast_q(0)
-        cast_q(1)
         order_ks(listed_scales)
+        cast_q(0)
         quant_q(0)
-        quant_q(1)
         empty_v(0, [0, 1])
+        nc.scalar.copy(held[:], token_scales(0))
         empty_v(1, [0])
+        gather_k(1)
+        cast_q(1)
+        quant_q(1)
         scores(0)
+        weigh(0)
         scores(1)
         turned_last = gather_last()
-        quant_v(0, [0, 1])
-        empty_last(turned_last)
-        weigh(0)
-        quant_v(1, [0])
-        quant_w(0)
         weigh(1)
+        empty_last(turned_last)
+        quant_v(0, [0, 1])
+        quant_w(0)
+        quant_v(1, [0])
         quant_w(1)
         quant_v(1, [1])
         finish(0)

@@ -28,7 +28,8 @@ VQ0 = VB0 + 1024
 QRAW = [4608, 7168]
 QB1 = 9216
 PW1 = 11008
-VC = [PW1 - 768, PW1 + 768]
+VC = {(0, 0): QRAW[0], (0, 1): PW1 - 256, (1, 0): PW1 + 768, (1, 1): PW1 + 1280}
+RAW = {(0, 1): 24576, (1, 0): 16384}
 
 
 def by_slot(t):
@@ -50,7 +51,11 @@ def tile_attend_silu_seg_kernel(tc, qT, k_words, k_scales, vT, vs, offs, out):
             shared.tile([P, T], BF16, name="vb0", offset=VB0, align_bytes=64),
             sb.tile([P, SEG], BF16, name="vb1", align_bytes=64),
         ]
-        vf = [sb.tile([P, T], F32, name="vf%d" % j, align_bytes=64) for j in range(PLANES)]
+        vf = sb.tile([P, T], F32, name="vf", align_bytes=64)
+        vraw = {(0, 0): vf[:, 0:SEG], (1, 1): vf[:, SEG:T]}
+        for b, j in RAW:
+            staged = shared.tile([P, SEG], F32, name="vraw%d%d" % (b, j), offset=RAW[b, j], align_bytes=64)
+            vraw[b, j] = staged[:]
         qraw = [shared.tile([P, PACK, NQ], F32, name="qraw%d" % b, offset=QRAW[b], align_bytes=64) for b in range(B)]
         ident = sb.tile([P, P], F32, name="ident", align_bytes=64)
         warm = sb.tile([P, 8], F32, name="warm")
@@ -65,13 +70,11 @@ def tile_attend_silu_seg_kernel(tc, qT, k_words, k_scales, vT, vs, offs, out):
 
         words = k_words[0].rearrange("p n t -> p (n t)").bitcast(I32)
         scale_rows = k_scales[0].bitcast(I32)
-        vraw = {}
 
         def seg(b):
             return slice(b * SEG, (b + 1) * SEG)
 
         def load_v(b, j):
-            vraw[b, j] = vf[j][:, seg(b)]
             nc.sync.dma_start(out=vraw[b, j], in_=vT[j * P : (j + 1) * P, seg(b)])
 
         def load_k(b):
@@ -117,7 +120,7 @@ def tile_attend_silu_seg_kernel(tc, qT, k_words, k_scales, vT, vs, offs, out):
             return listed
 
         def order_ks(listed):
-            both = shared.tile([P, PACK, B * P], U8, name="ksg", offset=QRAW[0] - 512, align_bytes=64)
+            both = shared.tile([P, PACK, B * P], U8, name="ksg", offset=RAW[1, 0], align_bytes=64)
             nc.vector.tensor_copy(
                 both[:].bitcast(I32).rearrange("x t (a i) -> x a t i", i=4),
                 listed[:].bitcast(I32).rearrange("x (a i t) -> x a t i", i=4, t=PACK),
@@ -135,14 +138,14 @@ def tile_attend_silu_seg_kernel(tc, qT, k_words, k_scales, vT, vs, offs, out):
 
         def cast_v(b, j):
             if (b, j) == (0, 0):
-                nc.scalar.activation(vb[j][:, 0:HALF], vf[j][:, 0:HALF], ACT.Copy)
-                nc.gpsimd.tensor_copy(vb[j][:, HALF:SEG], vf[j][:, HALF:SEG])
+                nc.scalar.activation(vb[j][:, 0:HALF], vf[:, 0:HALF], ACT.Copy)
+                nc.gpsimd.tensor_copy(vb[j][:, HALF:SEG], vf[:, HALF:SEG])
             else:
                 nc.gpsimd.tensor_copy(vb[j][:, seg(b)], vraw[b, j])
 
         def gather_last():
             vg = shared.tile([P, N], BF16, name="vglast", offset=QRAW[1], align_bytes=64)
-            nc.vector.tensor_copy(vg[:].rearrange("x (u g r e) -> x g u e r", u=2, r=4, e=2), vf[1][:].indirect(lst(1)))
+            nc.vector.tensor_copy(vg[:].rearrange("x (u g r e) -> x g u e r", u=2, r=4, e=2), vf[:].indirect(lst(1)))
             turned = ps.tile([P, 2, P], F32, name="vtlast", tag="vt0")
             pairs = vg[:].bitcast(F32)
             for u in range(2):
@@ -159,29 +162,24 @@ def tile_attend_silu_seg_kernel(tc, qT, k_words, k_scales, vT, vs, offs, out):
             vg = sb.tile([P, N], BF16, name="vg%d%d" % (b, j), align_bytes=64)
             dealt = vg[:].rearrange("x (g r t) -> x g t r", r=4, t=PACK)
             nc.scalar.activation(dealt, vb[j][:, 0 : end(b)].indirect(lst(b)), ACT.Copy)
-            if j == 0:
-                vt[b] = ps.tile([P, PLANES, 2, P], F32, name="vt%d" % b)
+            vt[b, j] = ps.tile([P, 2, P], F32, name="vt%d%d" % (b, j), tag="vt%d" % b if j == 0 else "y1")
             pairs = vg[:].bitcast(F32)
             for u in range(2):
-                nc.tensor.transpose(vt[b][:, j, u, :], pairs[:, u : N // 2 : 2], ident[:])
+                nc.tensor.transpose(vt[b, j][:, u, :], pairs[:, u : N // 2 : 2], ident[:])
 
-        def empty_v(b, planes):
-            j = planes[0]
+        def empty_v(b, j):
             if b == 0:
-                vq[b, j] = shared.tile([P, len(planes) * P * PACK], BF16, name="vq00", offset=VQ0, align_bytes=64)
+                vq[b, j] = shared.tile([P, P * PACK], BF16, name="vq0%d" % j, offset=(RAW[0, 1], VQ0)[j], align_bytes=64)
             else:
-                vq[b, j] = sb.tile([P, len(planes) * P * PACK], BF16, name="vq10", align_bytes=64)
+                vq[b, j] = sb.tile([P, P * PACK], BF16, name="vq10", align_bytes=64)
             nc.scalar.copy(
-                vq[b, j][:].bitcast(F32).rearrange("p (j e u) -> p j e u", j=len(planes), u=2),
-                vt[b][:, planes[0] : planes[-1] + 1, :, :].rearrange("p j u e -> p j e u"),
+                vq[b, j][:].bitcast(F32).rearrange("p (e u) -> p e u", u=2), vt[b, j][:].rearrange("p u e -> p e u")
             )
 
-        def quant_v(b, planes):
-            if planes[0] == 0:
-                vc[b] = shared.tile([P, DV], U32, name="vc%d" % b, offset=VC[b], align_bytes=64)
-                vsc[b] = sb.tile([P, DV], U8, name="vsc%d" % b, align_bytes=64)
-            cols = slice(planes[0] * P, (planes[-1] + 1) * P)
-            nc.vector.quantize_mx(out=vc[b][:, cols].bitcast(FP8X4), scales=vsc[b][:, cols], in_=vq[b, planes[0]][:])
+        def quant_v(b, j):
+            vc[b, j] = shared.tile([P, P], U32, name="vc%d%d" % (b, j), offset=VC[b, j], align_bytes=64)
+            vsc[b, j] = sb.tile([P, P], U8, name="vsc%d%d" % (b, j), align_bytes=64)
+            nc.vector.quantize_mx(out=vc[b, j][:].bitcast(FP8X4), scales=vsc[b, j][:], in_=vq[b, j][:])
 
         def cast_q(b):
             if b == 0:
@@ -241,37 +239,48 @@ def tile_attend_silu_seg_kernel(tc, qT, k_words, k_scales, vT, vs, offs, out):
 
         def finish(b):
             res = sb.tile([P, DV], F32, name="res%d" % b, align_bytes=64)
-            width = DV // (b + 1)
-            for h in range(b + 1):
-                cols = slice(h * width, (h + 1) * width)
-                y = ps.tile([P, width], F32, name="y%d%d" % (b, h), tag="y%d" % b if h == 0 else "z%d" % b)
+            if b == 0:
+                whole = ps.tile([P, DV], F32, name="y0", tag="y0")
+            for j in range(PLANES):
+                cols = slice(j * P, (j + 1) * P)
+                if b == 0:
+                    y = whole[:, cols]
+                else:
+                    bank = ps.tile([P, P], F32, name="y1%d" % j, tag=("y1", "z1")[j])
+                    y = bank[:]
                 nc.tensor.matmul_mx(
-                    out=y[:],
+                    out=y,
                     lhsT=wc[b][:].bitcast(FP8X4),
                     lhsT_scale=wsc[b][:],
-                    rhs=vc[b][:, cols].bitcast(FP8X4),
-                    rhs_scale=vsc[b][:, cols],
+                    rhs=vc[b, j][:].bitcast(FP8X4),
+                    rhs_scale=vsc[b, j][:],
                     start=True,
                     stop=True,
                 )
-                if h == 0:
-                    nc.scalar.activation(res[:, cols], y[:], ACT.Copy, scale=1.0 / 16.0)
-                else:
-                    nc.vector.tensor_scalar(res[:, cols], y[:], 1.0 / 16.0, None, MULT)
+                if (b, j) == (1, 0):
+                    nc.scalar.activation(res[:, cols], y, ACT.Copy, scale=1.0 / 16.0)
+                if (b, j) == (1, 1):
+                    nc.vector.tensor_scalar(res[:, cols], y, 1.0 / 16.0, None, MULT)
+            if b == 0:
+                nc.scalar.activation(res[:], whole[:], ACT.Copy, scale=1.0 / 16.0)
             nc.sync.dma_start(out=out[b], in_=res[:])
 
         gather_vs()
         listed_scales = gather_ks()
-        for b, j in ((0, 0), (0, 1), (1, 0)):
-            cast_v(b, j)
-            gather_v(b, j)
+        for j in range(PLANES):
+            cast_v(0, j)
+            gather_v(0, j)
+        empty_v(0, 0)
+        cast_v(1, 0)
+        gather_v(1, 0)
         gather_k(0)
         order_ks(listed_scales)
         cast_q(0)
         quant_q(0)
-        empty_v(0, [0, 1])
+        quant_v(0, 0)
+        empty_v(0, 1)
         nc.scalar.copy(held[:], token_scales(0))
-        empty_v(1, [0])
+        empty_v(1, 0)
         gather_k(1)
         cast_q(1)
         quant_q(1)
@@ -281,10 +290,10 @@ def tile_attend_silu_seg_kernel(tc, qT, k_words, k_scales, vT, vs, offs, out):
         turned_last = gather_last()
         weigh(1)
         empty_last(turned_last)
-        quant_v(0, [0, 1])
+        quant_v(0, 1)
         quant_w(0)
-        quant_v(1, [0])
+        quant_v(1, 0)
         quant_w(1)
-        quant_v(1, [1])
+        quant_v(1, 1)
         finish(0)
         finish(1)

@@ -25,10 +25,10 @@ PLANES = DV // P
 HALF = SEG // 2
 VB0 = 0
 VQ0 = VB0 + 1024
-QRAW = [4608, 7168]
-QB1 = 9216
+QRAW = [4608, 32768]
+QB1 = VB0 + 2048
 PW1 = 11008
-VC = {(0, 0): QRAW[0], (0, 1): PW1 - 256, (1, 0): PW1 + 768, (1, 1): PW1 + 1280}
+VC = {(0, 0): QRAW[0], (0, 1): QRAW[1] + 1088, (1, 0): PW1 + 768, (1, 1): PW1 + 1280}
 RAW = {(0, 1): 24576, (1, 0): 16384}
 
 
@@ -84,7 +84,7 @@ def tile_attend_silu_seg_kernel(tc, qT, k_words, k_scales, vT, vs, offs, out):
             nc.sync.dma_start(out=qraw[b][:], in_=qT[b].rearrange("(p j) n -> p j n", j=PACK))
 
         nc.sync.dma_start(offsets[:], offs)
-        nc.sync.dma_start(out=vsw[P - 1 : P, :], in_=vs[0:1, :])
+        nc.scalar.dma_start(out=vsw[P - 1 : P, :], in_=vs[0:1, :])
         nc.scalar.activation(warm2[:], warm[:], ACT.Silu)
         load_v(0, 0)
         load_v(0, 1)
@@ -144,7 +144,7 @@ def tile_attend_silu_seg_kernel(tc, qT, k_words, k_scales, vT, vs, offs, out):
                 nc.gpsimd.tensor_copy(vb[j][:, seg(b)], vraw[b, j])
 
         def gather_last():
-            vg = shared.tile([P, N], BF16, name="vglast", offset=QRAW[1], align_bytes=64)
+            vg = shared.tile([P, N], BF16, name="vglast", offset=QRAW[1] - 960, align_bytes=64)
             nc.vector.tensor_copy(vg[:].rearrange("x (u g r e) -> x g u e r", u=2, r=4, e=2), vf[:].indirect(lst(1)))
             turned = ps.tile([P, 2, P], F32, name="vtlast", tag="vt0")
             pairs = vg[:].bitcast(F32)
@@ -171,7 +171,7 @@ def tile_attend_silu_seg_kernel(tc, qT, k_words, k_scales, vT, vs, offs, out):
             if b == 0:
                 vq[b, j] = shared.tile([P, P * PACK], BF16, name="vq0%d" % j, offset=(RAW[0, 1], VQ0)[j], align_bytes=64)
             else:
-                vq[b, j] = sb.tile([P, P * PACK], BF16, name="vq10", align_bytes=64)
+                vq[b, j] = shared.tile([P, P * PACK], BF16, name="vq10", offset=QRAW[1] + 64, align_bytes=64)
             nc.scalar.copy(
                 vq[b, j][:].bitcast(F32).rearrange("p (e u) -> p e u", u=2), vt[b, j][:].rearrange("p u e -> p e u")
             )
@@ -186,7 +186,12 @@ def tile_attend_silu_seg_kernel(tc, qT, k_words, k_scales, vT, vs, offs, out):
                 qb[b] = sb.tile([P, NQ, PACK], BF16, name="qb0", align_bytes=64)
             else:
                 qb[b] = shared.tile([P, NQ, PACK], BF16, name="qb1", offset=QB1, align_bytes=64)
-            nc.gpsimd.tensor_copy(qb[b][:], qraw[b][:].rearrange("p j n -> p n j"))
+            rows = qraw[b][:].rearrange("p j n -> p n j")
+            if b == 0:
+                nc.gpsimd.tensor_copy(qb[b][:], rows)
+            else:
+                nc.gpsimd.tensor_copy(qb[b][:, 0 : NQ // 2, :], rows[:, 0 : NQ // 2, :])
+                nc.scalar.copy(qb[b][:, NQ // 2 : NQ, :], rows[:, NQ // 2 : NQ, :])
 
         def quant_q(b):
             qc[b] = sb.tile([P, NQ], U32, name="qc%d" % b, align_bytes=64)
@@ -209,6 +214,8 @@ def tile_attend_silu_seg_kernel(tc, qT, k_words, k_scales, vT, vs, offs, out):
             for h in range(b + 1):
                 if (b, h) == (1, 0):
                     pw[b, h] = shared.tile([P, width, PACK], F32, name="pw10", offset=PW1, align_bytes=64)
+                elif b == 0:
+                    pw[b, h] = shared.tile([P, width, PACK], F32, name="pw00", offset=QRAW[1] + 1984, align_bytes=64)
                 else:
                     pw[b, h] = sb.tile([P, width, PACK], F32, name="pw%d%d" % (b, h), align_bytes=64)
                 scored = z[b][:, :, h * width : (h + 1) * width]
@@ -217,7 +224,7 @@ def tile_attend_silu_seg_kernel(tc, qT, k_words, k_scales, vT, vs, offs, out):
         def token_scales(b):
             return vst[b][:, :, P - 1 : P].rearrange("p t o -> p o t")
 
-        held = shared.tile([P, 1, PACK], F32, name="held", offset=VQ0 + 2048, align_bytes=64)
+        held = shared.tile([P, 1, PACK], F32, name="held", offset=RAW[0, 1] + 1024, align_bytes=64)
 
         def weigh(b):
             if b == 0:
@@ -271,6 +278,7 @@ def tile_attend_silu_seg_kernel(tc, qT, k_words, k_scales, vT, vs, offs, out):
             cast_v(0, j)
             gather_v(0, j)
         empty_v(0, 0)
+        nc.scalar.copy(held[:], token_scales(0))
         cast_v(1, 0)
         gather_v(1, 0)
         gather_k(0)
@@ -279,18 +287,17 @@ def tile_attend_silu_seg_kernel(tc, qT, k_words, k_scales, vT, vs, offs, out):
         quant_q(0)
         quant_v(0, 0)
         empty_v(0, 1)
-        nc.scalar.copy(held[:], token_scales(0))
-        empty_v(1, 0)
         gather_k(1)
         cast_q(1)
         quant_q(1)
+        quant_v(0, 1)
         scores(0)
+        empty_v(1, 0)
         weigh(0)
         scores(1)
         turned_last = gather_last()
         weigh(1)
         empty_last(turned_last)
-        quant_v(0, 1)
         quant_w(0)
         quant_v(1, 0)
         quant_w(1)

@@ -23,7 +23,7 @@ SEG = T // B
 COLS = N // 16
 PLANES = DV // P
 HALF = SEG // 2
-VB0 = 0
+VB0 = 40960
 VQ0 = VB0 + 1024
 QRAW = [4608, 32768]
 QB1 = VB0 + 2048
@@ -103,7 +103,7 @@ def tile_attend_silu_seg_kernel(tc, qT, k_words, k_scales, vT, vs, offs, out):
         def end(b):
             return (b + 1) * SEG
 
-        kg, ksg, qb, vq = {}, {}, {}, {}
+        kg, ksg, qb, vq, gathered = {}, {}, {}, {}, {}
         z, vst, vt, pw, wq = {}, {}, {}, {}, {}
         wc, wsc, vc, vsc, qc, qsc = {}, {}, {}, {}, {}, {}
 
@@ -154,15 +154,22 @@ def tile_attend_silu_seg_kernel(tc, qT, k_words, k_scales, vT, vs, offs, out):
 
         def empty_last(turned):
             vq[1, 1] = sb.tile([P, P * PACK], BF16, name="vq11", align_bytes=64)
-            nc.scalar.copy(
-                vq[1, 1][:].bitcast(F32).rearrange("p (e u) -> p e u", u=2), turned[:].rearrange("p u e -> p e u")
-            )
+            for h in range(2):
+                part = slice(h * (P // 2), (h + 1) * (P // 2))
+                nc.scalar.copy(
+                    vq[1, 1][:].bitcast(F32).rearrange("p (e u) -> p e u", u=2)[:, part, :],
+                    turned[:].rearrange("p u e -> p e u")[:, part, :],
+                )
 
         def gather_v(b, j):
             vg = sb.tile([P, N], BF16, name="vg%d%d" % (b, j), align_bytes=64)
             dealt = vg[:].rearrange("x (g r t) -> x g t r", r=4, t=PACK)
             nc.scalar.activation(dealt, vb[j][:, 0 : end(b)].indirect(lst(b)), ACT.Copy)
-            vt[b, j] = ps.tile([P, 2, P], F32, name="vt%d%d" % (b, j), tag="vt%d" % b if j == 0 else "y1")
+            gathered[b, j] = vg
+
+        def turn_v(b, j):
+            vg = gathered[b, j]
+            vt[b, j] = ps.tile([P, 2, P], F32, name="vt%d%d" % (b, j), tag={(0, 0): "vt0", (0, 1): "y1", (1, 0): "y1"}[b, j])
             pairs = vg[:].bitcast(F32)
             for u in range(2):
                 nc.tensor.transpose(vt[b, j][:, u, :], pairs[:, u : N // 2 : 2], ident[:])
@@ -179,7 +186,15 @@ def tile_attend_silu_seg_kernel(tc, qT, k_words, k_scales, vT, vs, offs, out):
         def quant_v(b, j):
             vc[b, j] = shared.tile([P, P], U32, name="vc%d%d" % (b, j), offset=VC[b, j], align_bytes=64)
             vsc[b, j] = sb.tile([P, P], U8, name="vsc%d%d" % (b, j), align_bytes=64)
-            nc.vector.quantize_mx(out=vc[b, j][:].bitcast(FP8X4), scales=vsc[b, j][:], in_=vq[b, j][:])
+            parts = 2 if (b, j) == (1, 1) else 1
+            width = P // parts
+            for h in range(parts):
+                cols = slice(h * width, (h + 1) * width)
+                nc.vector.quantize_mx(
+                    out=vc[b, j][:, cols].bitcast(FP8X4),
+                    scales=vsc[b, j][:, cols],
+                    in_=vq[b, j][:, h * width * PACK : (h + 1) * width * PACK],
+                )
 
         def cast_q(b):
             if b == 0:
@@ -199,7 +214,7 @@ def tile_attend_silu_seg_kernel(tc, qT, k_words, k_scales, vT, vs, offs, out):
             nc.vector.quantize_mx(out=qc[b][:].bitcast(FP8X4), scales=qsc[b][:], in_=qb[b][:].rearrange("p n j -> p (n j)"))
 
         def scores(b):
-            z[b] = ps.tile([P, PACK, NQ], F32, name="z%d" % b)
+            z[b] = ps.tile([P, PACK, NQ], F32, name="z%d" % b, tag="z%d" % b)
             for t in range(PACK):
                 nc.tensor.matmul_mx(
                     out=z[b][:, t, :],
@@ -215,7 +230,7 @@ def tile_attend_silu_seg_kernel(tc, qT, k_words, k_scales, vT, vs, offs, out):
                 if (b, h) == (1, 0):
                     pw[b, h] = shared.tile([P, width, PACK], F32, name="pw10", offset=PW1, align_bytes=64)
                 elif b == 0:
-                    pw[b, h] = shared.tile([P, width, PACK], F32, name="pw00", offset=QRAW[1] + 1984, align_bytes=64)
+                    pw[b, h] = shared.tile([P, width, PACK], F32, name="pw00", offset=VB0 - 1024, align_bytes=64)
                 else:
                     pw[b, h] = sb.tile([P, width, PACK], F32, name="pw%d%d" % (b, h), align_bytes=64)
                 scored = z[b][:, :, h * width : (h + 1) * width]
@@ -228,7 +243,7 @@ def tile_attend_silu_seg_kernel(tc, qT, k_words, k_scales, vT, vs, offs, out):
 
         def weigh(b):
             if b == 0:
-                wq[b] = shared.tile([P, NQ, PACK], BF16, name="wq0", offset=QB1, align_bytes=64)
+                wq[b] = shared.tile([P, NQ, PACK], BF16, name="wq0", offset=QB1 - 512, align_bytes=64)
                 nc.gpsimd.tensor_tensor(wq[b][:], pw[b, 0][:], held[:].to_broadcast([P, NQ, PACK]), MULT)
             else:
                 wq[b] = sb.tile([P, NQ, PACK], BF16, name="wq1", align_bytes=64)
@@ -244,32 +259,36 @@ def tile_attend_silu_seg_kernel(tc, qT, k_words, k_scales, vT, vs, offs, out):
             wsc[b] = sb.tile([P, NQ], U8, name="wsc%d" % b, align_bytes=64)
             nc.vector.quantize_mx(out=wc[b][:].bitcast(FP8X4), scales=wsc[b][:], in_=wq[b][:].rearrange("p q t -> p (q t)"))
 
+        def product(y, b, j, cols):
+            nc.tensor.matmul_mx(
+                out=y,
+                lhsT=wc[b][:].bitcast(FP8X4),
+                lhsT_scale=wsc[b][:],
+                rhs=vc[b, j][:, cols].bitcast(FP8X4),
+                rhs_scale=vsc[b, j][:, cols],
+                start=True,
+                stop=True,
+            )
+
         def finish(b):
             res = sb.tile([P, DV], F32, name="res%d" % b, align_bytes=64)
             if b == 0:
-                whole = ps.tile([P, DV], F32, name="y0", tag="y0")
-            for j in range(PLANES):
-                cols = slice(j * P, (j + 1) * P)
-                if b == 0:
-                    y = whole[:, cols]
-                else:
-                    bank = ps.tile([P, P], F32, name="y1%d" % j, tag=("y1", "z1")[j])
-                    y = bank[:]
-                nc.tensor.matmul_mx(
-                    out=y,
-                    lhsT=wc[b][:].bitcast(FP8X4),
-                    lhsT_scale=wsc[b][:],
-                    rhs=vc[b, j][:].bitcast(FP8X4),
-                    rhs_scale=vsc[b, j][:],
-                    start=True,
-                    stop=True,
-                )
-                if (b, j) == (1, 0):
-                    nc.scalar.activation(res[:, cols], y, ACT.Copy, scale=1.0 / 16.0)
-                if (b, j) == (1, 1):
-                    nc.vector.tensor_scalar(res[:, cols], y, 1.0 / 16.0, None, MULT)
-            if b == 0:
-                nc.scalar.activation(res[:], whole[:], ACT.Copy, scale=1.0 / 16.0)
+                low = ps.tile([P, P], F32, name="y00", tag="y0")
+                product(low[:], b, 0, slice(0, P))
+                nc.scalar.activation(res[:, 0:P], low[:], ACT.Copy, scale=1.0 / 16.0)
+                high = ps.tile([P, P], F32, name="y01", tag="vst0")
+                product(high[:], b, 1, slice(0, P))
+                nc.vector.tensor_scalar(res[:, P:DV], high[:], 1.0 / 16.0, None, MULT)
+            else:
+                early = ps.tile([P, P], F32, name="y1", tag="y1")
+                product(early[:], b, 0, slice(0, P))
+                nc.scalar.activation(res[:, 0:P], early[:], ACT.Copy, scale=1.0 / 16.0)
+                for h in range(2):
+                    late = ps.tile([P, P // 2], F32, name="ylate%d" % h, tag=("vt1", "z1")[h])
+                    product(late[:], b, 1, slice(h * (P // 2), (h + 1) * (P // 2)))
+                    nc.vector.tensor_scalar(
+                        res[:, P + h * (P // 2) : P + (h + 1) * (P // 2)], late[:], 1.0 / 16.0, None, MULT
+                    )
             nc.sync.dma_start(out=out[b], in_=res[:])
 
         gather_vs()
@@ -277,6 +296,7 @@ def tile_attend_silu_seg_kernel(tc, qT, k_words, k_scales, vT, vs, offs, out):
         for j in range(PLANES):
             cast_v(0, j)
             gather_v(0, j)
+            turn_v(0, j)
         empty_v(0, 0)
         nc.scalar.copy(held[:], token_scales(0))
         cast_v(1, 0)
@@ -292,6 +312,7 @@ def tile_attend_silu_seg_kernel(tc, qT, k_words, k_scales, vT, vs, offs, out):
         quant_q(1)
         quant_v(0, 1)
         scores(0)
+        turn_v(1, 0)
         empty_v(1, 0)
         weigh(0)
         scores(1)

@@ -22,18 +22,17 @@ PACK = 4
 SEG = T // B
 COLS = N // 16
 PLANES = DV // P
-HALF = SEG // 2
-VB0 = 40960
-VQ0 = VB0 + 1024
-QRAW = [4608, 32768]
-QB1 = VB0 + 2048
-PW1 = 11008
-VC = {(0, 0): QRAW[0], (0, 1): QRAW[1] + 1088, (1, 0): PW1 + 768, (1, 1): PW1 + 1280}
-RAW = {(0, 1): 24576, (1, 0): 16384}
+
+AT_VWIN00 = 0
+AT_PW0 = AT_VWIN00 + 2048
+AT_VG01 = AT_PW0 + 2048
+AT_VG00 = AT_VG01 + 512
+AT_PW1 = AT_VG00 + 512
+AT_QRAW = [8192, 10240]
 
 
-def by_slot(t):
-    return t.rearrange("x t (j r) -> x j t r", r=4)
+def dealt(t):
+    return t.rearrange("x t p -> x p t")
 
 
 def tile_attend_silu_seg_kernel(tc, qT, k_words, k_scales, vT, vs, offs, out):
@@ -43,27 +42,27 @@ def tile_attend_silu_seg_kernel(tc, qT, k_words, k_scales, vT, vs, offs, out):
         shared = ctx.enter_context(tc.tile_pool(name="shared", bufs=1))
         ps = ctx.enter_context(tc.psum_pool(name="ps", bufs=1))
 
+        def place(shape, dtype, name, at=None):
+            if at is None:
+                return sb.tile(shape, dtype, name=name, align_bytes=64)
+            return shared.tile(shape, dtype, name=name, offset=at, align_bytes=64)
+
         offsets = sb.tile([P, B * COLS], U16, name="offsets")
-        kw = sb.tile([P, T], I32, name="kw", align_bytes=64)
-        ksc = sb.tile([P, T], U8, name="ksc", align_bytes=64)
-        vsw = sb.tile([P, T], F32, name="vsw", align_bytes=64)
-        vb = [
-            shared.tile([P, T], BF16, name="vb0", offset=VB0, align_bytes=64),
-            sb.tile([P, SEG], BF16, name="vb1", align_bytes=64),
-        ]
-        vf = sb.tile([P, T], F32, name="vf", align_bytes=64)
-        vraw = {(0, 0): vf[:, 0:SEG], (1, 1): vf[:, SEG:T]}
-        for b, j in RAW:
-            staged = shared.tile([P, SEG], F32, name="vraw%d%d" % (b, j), offset=RAW[b, j], align_bytes=64)
-            vraw[b, j] = staged[:]
-        qraw = [shared.tile([P, PACK, NQ], F32, name="qraw%d" % b, offset=QRAW[b], align_bytes=64) for b in range(B)]
-        ident = sb.tile([P, P], F32, name="ident", align_bytes=64)
+        kw = place([P, T], I32, "kw")
+        ksc = place([P, T], U8, "ksc")
+        vsw = place([P, T], F32, "vsw")
+        vwin = {}
+        for b in range(B):
+            for j in range(PLANES):
+                vwin[b, j] = place([P, (b + 1) * SEG], F32, "vwin%d%d" % (b, j), AT_VWIN00 if (b, j) == (0, 0) else None)
+        qraw = [place([P, PACK, NQ], F32, "qraw%d" % b, AT_QRAW[b]) for b in range(B)]
+        ident = place([P, P], F32, "ident")
         warm = sb.tile([P, 8], F32, name="warm")
         warm2 = sb.tile([P, 8], F32, name="warm2")
 
-        nc.gpsimd.memset(warm[:], 0.0)
         nc.vector.memset(ksc[:, 0:SEG].bitcast(I32), 0)
         nc.gpsimd.memset(ksc[:, SEG:T].bitcast(I32), 0)
+        nc.vector.memset(warm[:], 0.0)
         nc.vector.memset(vsw[0 : P - 1, 0:SEG], 0.0)
         nc.gpsimd.memset(vsw[0 : P - 1, SEG:T], 0.0)
         make_identity(nc, ident[:])
@@ -75,7 +74,7 @@ def tile_attend_silu_seg_kernel(tc, qT, k_words, k_scales, vT, vs, offs, out):
             return slice(b * SEG, (b + 1) * SEG)
 
         def load_v(b, j):
-            nc.sync.dma_start(out=vraw[b, j], in_=vT[j * P : (j + 1) * P, seg(b)])
+            nc.sync.dma_start(out=vwin[b, j][:, seg(b)], in_=vT[j * P : (j + 1) * P, seg(b)])
 
         def load_k(b):
             nc.sync.dma_start(out=kw[:, seg(b)], in_=words[:, seg(b)])
@@ -86,138 +85,86 @@ def tile_attend_silu_seg_kernel(tc, qT, k_words, k_scales, vT, vs, offs, out):
         nc.sync.dma_start(offsets[:], offs)
         nc.scalar.dma_start(out=vsw[P - 1 : P, :], in_=vs[0:1, :])
         nc.scalar.activation(warm2[:], warm[:], ACT.Silu)
-        load_v(0, 0)
-        load_v(0, 1)
+        load_k(0)
         for r in range(4):
             nc.sync.dma_start(out=ksc[r:P:32, :].bitcast(I32), in_=scale_rows[r:16:4, :])
-        load_v(1, 0)
-        load_k(0)
         load_q(0)
-        load_k(1)
+        load_v(0, 0)
         load_q(1)
+        load_k(1)
+        load_v(0, 1)
+        load_v(1, 0)
         load_v(1, 1)
 
-        def lst(b):
-            return offsets[:, b * COLS : (b + 1) * COLS]
+        def lst(b, part=0, parts=1):
+            width = COLS // parts
+            return offsets[:, b * COLS + part * width : b * COLS + (part + 1) * width]
 
-        def end(b):
-            return (b + 1) * SEG
+        kg, ksg, qb, vg, vt, vst, vq = {}, {}, {}, {}, {}, {}, {}
+        held, pw, wq = {}, {}, {}
+        wc, wsc, qc, qsc, vc, vsc = {}, {}, {}, {}, {}, {}
 
-        kg, ksg, qb, vq, gathered = {}, {}, {}, {}, {}
-        z, vst, vt, pw, wq = {}, {}, {}, {}, {}
-        wc, wsc, vc, vsc, qc, qsc = {}, {}, {}, {}, {}, {}
+        def gather_vs(b):
+            listed = place([P, N], F32, "vsg%d" % b)
+            nc.scalar.activation(listed[:], vsw[:].indirect(lst(b)), ACT.Copy)
+            vst[b] = ps.tile([P, PACK, P], F32, name="vst%d" % b)
+            for t in range(PACK):
+                nc.tensor.transpose(vst[b][:, t, :], listed[:, t:N:PACK], ident[:])
 
-        def gather_k(b):
-            if b == 0:
-                kg[b] = sb.tile([P, PACK, P], U32, name="kg0", align_bytes=64)
-            else:
-                kg[b] = shared.tile([P, PACK, P], U32, name="kg1", offset=QRAW[0] + 512, align_bytes=64)
-            nc.vector.tensor_copy(by_slot(kg[b][:]), kw[:, 0 : end(b)].bitcast(U32).indirect(lst(b)))
+        def hold_vs(b, at=None):
+            held[b] = place([P, 1, PACK], F32, "held%d" % b, at)
+            nc.scalar.copy(held[b][:], vst[b][:, :, P - 1 : P].rearrange("p t o -> p o t"))
 
-        def gather_ks():
-            listed = sb.tile([P, B * N], U8, name="kslisted", align_bytes=64)
-            nc.vector.tensor_copy(listed[:], ksc[:].indirect(offsets[:]))
-            return listed
+        def gather_ks(b, at=None):
+            ksg[b] = place([P, PACK, P], U8, "ksg%d" % b, at)
+            nc.vector.tensor_copy(dealt(ksg[b][:]), ksc[:].indirect(lst(b)))
 
-        def order_ks(listed):
-            both = shared.tile([P, PACK, B * P], U8, name="ksg", offset=RAW[1, 0], align_bytes=64)
-            nc.vector.tensor_copy(
-                both[:].bitcast(I32).rearrange("x t (a i) -> x a t i", i=4),
-                listed[:].bitcast(I32).rearrange("x (a i t) -> x a t i", i=4, t=PACK),
-            )
-            for b in range(B):
-                ksg[b] = both[:, :, b * P : (b + 1) * P]
+        def gather_k(b, at=None):
+            kg[b] = place([P, PACK, P], U32, "kg%d" % b, at)
+            nc.vector.tensor_copy(dealt(kg[b][:]), kw[:, 0 : (b + 1) * SEG].bitcast(U32).indirect(lst(b)))
 
-        def gather_vs():
-            both = sb.tile([P, PACK, B * P], U32, name="vsg", align_bytes=64)
-            nc.vector.tensor_copy(by_slot(both[:]), vsw[:].bitcast(U32).indirect(offsets[:]))
-            for b in range(B):
-                vst[b] = ps.tile([P, PACK, P], F32, name="vst%d" % b)
-                for t in range(PACK):
-                    nc.tensor.transpose(vst[b][:, t, :], both[:, t, b * P : (b + 1) * P].bitcast(F32), ident[:])
-
-        def cast_v(b, j):
-            if (b, j) == (0, 0):
-                nc.scalar.activation(vb[j][:, 0:HALF], vf[:, 0:HALF], ACT.Copy)
-                nc.gpsimd.tensor_copy(vb[j][:, HALF:SEG], vf[:, HALF:SEG])
-            else:
-                nc.gpsimd.tensor_copy(vb[j][:, seg(b)], vraw[b, j])
-
-        def gather_last():
-            vg = shared.tile([P, N], BF16, name="vglast", offset=QRAW[1] - 960, align_bytes=64)
-            nc.vector.tensor_copy(vg[:].rearrange("x (u g r e) -> x g u e r", u=2, r=4, e=2), vf[:].indirect(lst(1)))
-            turned = ps.tile([P, 2, P], F32, name="vtlast", tag="vt0")
-            pairs = vg[:].bitcast(F32)
-            for u in range(2):
-                nc.tensor.transpose(turned[:, u, :], pairs[:, u * P : (u + 1) * P], ident[:])
-            return turned
-
-        def empty_last(turned):
-            vq[1, 1] = sb.tile([P, P * PACK], BF16, name="vq11", align_bytes=64)
-            for h in range(2):
-                part = slice(h * (P // 2), (h + 1) * (P // 2))
-                nc.scalar.copy(
-                    vq[1, 1][:].bitcast(F32).rearrange("p (e u) -> p e u", u=2)[:, part, :],
-                    turned[:].rearrange("p u e -> p e u")[:, part, :],
-                )
-
-        def gather_v(b, j):
-            vg = sb.tile([P, N], BF16, name="vg%d%d" % (b, j), align_bytes=64)
-            dealt = vg[:].rearrange("x (g r t) -> x g t r", r=4, t=PACK)
-            nc.scalar.activation(dealt, vb[j][:, 0 : end(b)].indirect(lst(b)), ACT.Copy)
-            gathered[b, j] = vg
+        def gather_v(b, j, who, at):
+            vg[b, j] = place([P, N], BF16, "vg%d%d" % (b, j), at)
+            width = N // len(who)
+            for h, engine in enumerate(who):
+                part = vg[b, j][:, h * width : (h + 1) * width]
+                listed = vwin[b, j][:].indirect(lst(b, h, len(who)))
+                if engine == "vector":
+                    nc.vector.tensor_copy(part, listed)
+                else:
+                    nc.scalar.activation(part, listed, ACT.Copy)
 
         def turn_v(b, j):
-            vg = gathered[b, j]
-            vt[b, j] = ps.tile([P, 2, P], F32, name="vt%d%d" % (b, j), tag={(0, 0): "vt0", (0, 1): "y1", (1, 0): "y1"}[b, j])
-            pairs = vg[:].bitcast(F32)
+            vt[b, j] = ps.tile([P, 2, P], F32, name="vt%d%d" % (b, j))
+            pairs = vg[b, j][:].bitcast(F32)
             for u in range(2):
                 nc.tensor.transpose(vt[b, j][:, u, :], pairs[:, u : N // 2 : 2], ident[:])
 
         def empty_v(b, j):
-            if b == 0:
-                vq[b, j] = shared.tile([P, P * PACK], BF16, name="vq0%d" % j, offset=(RAW[0, 1], VQ0)[j], align_bytes=64)
-            else:
-                vq[b, j] = shared.tile([P, P * PACK], BF16, name="vq10", offset=QRAW[1] + 64, align_bytes=64)
+            vq[b, j] = place([P, P * PACK], BF16, "vq%d%d" % (b, j))
             nc.scalar.copy(
                 vq[b, j][:].bitcast(F32).rearrange("p (e u) -> p e u", u=2), vt[b, j][:].rearrange("p u e -> p e u")
             )
 
-        def quant_v(b, j):
-            vc[b, j] = shared.tile([P, P], U32, name="vc%d%d" % (b, j), offset=VC[b, j], align_bytes=64)
-            vsc[b, j] = sb.tile([P, P], U8, name="vsc%d%d" % (b, j), align_bytes=64)
-            parts = 2 if (b, j) == (1, 1) else 1
-            width = P // parts
-            for h in range(parts):
-                cols = slice(h * width, (h + 1) * width)
-                nc.vector.quantize_mx(
-                    out=vc[b, j][:, cols].bitcast(FP8X4),
-                    scales=vsc[b, j][:, cols],
-                    in_=vq[b, j][:, h * width * PACK : (h + 1) * width * PACK],
-                )
+        def quant_v(b, j, at):
+            vc[b, j] = place([P, P], U32, "vc%d%d" % (b, j), at)
+            vsc[b, j] = place([P, P], U8, "vsc%d%d" % (b, j))
+            nc.vector.quantize_mx(out=vc[b, j][:].bitcast(FP8X4), scales=vsc[b, j][:], in_=vq[b, j][:])
 
         def cast_q(b):
-            if b == 0:
-                qb[b] = sb.tile([P, NQ, PACK], BF16, name="qb0", align_bytes=64)
-            else:
-                qb[b] = shared.tile([P, NQ, PACK], BF16, name="qb1", offset=QB1, align_bytes=64)
-            rows = qraw[b][:].rearrange("p j n -> p n j")
-            if b == 0:
-                nc.gpsimd.tensor_copy(qb[b][:], rows)
-            else:
-                nc.gpsimd.tensor_copy(qb[b][:, 0 : NQ // 2, :], rows[:, 0 : NQ // 2, :])
-                nc.scalar.copy(qb[b][:, NQ // 2 : NQ, :], rows[:, NQ // 2 : NQ, :])
+            qb[b] = place([P, NQ, PACK], BF16, "qb%d" % b)
+            nc.gpsimd.tensor_copy(qb[b][:], qraw[b][:].rearrange("p j n -> p n j"))
 
         def quant_q(b):
-            qc[b] = sb.tile([P, NQ], U32, name="qc%d" % b, align_bytes=64)
-            qsc[b] = sb.tile([P, NQ], U8, name="qsc%d" % b, align_bytes=64)
+            qc[b] = place([P, NQ], U32, "qc%d" % b)
+            qsc[b] = place([P, NQ], U8, "qsc%d" % b)
             nc.vector.quantize_mx(out=qc[b][:].bitcast(FP8X4), scales=qsc[b][:], in_=qb[b][:].rearrange("p n j -> p (n j)"))
 
-        def scores(b):
-            z[b] = ps.tile([P, PACK, NQ], F32, name="z%d" % b, tag="z%d" % b)
+        def scores(b, at):
+            z = ps.tile([P, PACK, NQ], F32, name="z%d" % b)
             for t in range(PACK):
                 nc.tensor.matmul_mx(
-                    out=z[b][:, t, :],
+                    out=z[:, t, :],
                     lhsT=kg[b][:, t, :].bitcast(FP8X4),
                     lhsT_scale=ksg[b][:, t, :],
                     rhs=qc[b][:].bitcast(FP8X4),
@@ -225,103 +172,74 @@ def tile_attend_silu_seg_kernel(tc, qT, k_words, k_scales, vT, vs, offs, out):
                     start=True,
                     stop=True,
                 )
-            width = NQ // (b + 1)
-            for h in range(b + 1):
-                if (b, h) == (1, 0):
-                    pw[b, h] = shared.tile([P, width, PACK], F32, name="pw10", offset=PW1, align_bytes=64)
-                elif b == 0:
-                    pw[b, h] = shared.tile([P, width, PACK], F32, name="pw00", offset=VB0 - 1024, align_bytes=64)
-                else:
-                    pw[b, h] = sb.tile([P, width, PACK], F32, name="pw%d%d" % (b, h), align_bytes=64)
-                scored = z[b][:, :, h * width : (h + 1) * width]
-                nc.scalar.activation(pw[b, h][:], scored.rearrange("p t q -> p q t"), ACT.Silu)
-
-        def token_scales(b):
-            return vst[b][:, :, P - 1 : P].rearrange("p t o -> p o t")
-
-        held = shared.tile([P, 1, PACK], F32, name="held", offset=RAW[0, 1] + 1024, align_bytes=64)
+            pw[b] = place([P, NQ, PACK], F32, "pw%d" % b, at)
+            nc.scalar.activation(pw[b][:], z[:].rearrange("p t q -> p q t"), ACT.Silu)
 
         def weigh(b):
-            if b == 0:
-                wq[b] = shared.tile([P, NQ, PACK], BF16, name="wq0", offset=QB1 - 512, align_bytes=64)
-                nc.gpsimd.tensor_tensor(wq[b][:], pw[b, 0][:], held[:].to_broadcast([P, NQ, PACK]), MULT)
-            else:
-                wq[b] = sb.tile([P, NQ, PACK], BF16, name="wq1", align_bytes=64)
-                for h in range(2):
-                    scale = token_scales(b).to_broadcast([P, NQ // 2, PACK])
-                    nc.vector.tensor_tensor(wq[b][:, h * (NQ // 2) : (h + 1) * (NQ // 2), :], pw[b, h][:], scale, MULT)
+            wq[b] = place([P, NQ, PACK], BF16, "wq%d" % b)
+            nc.gpsimd.tensor_tensor(wq[b][:], pw[b][:], held[b][:].to_broadcast([P, NQ, PACK]), MULT)
 
         def quant_w(b):
-            if b == 0:
-                wc[b] = shared.tile([P, NQ], U32, name="wc0", offset=PW1 + 256, align_bytes=64)
-            else:
-                wc[b] = sb.tile([P, NQ], U32, name="wc1", align_bytes=64)
-            wsc[b] = sb.tile([P, NQ], U8, name="wsc%d" % b, align_bytes=64)
+            wc[b] = place([P, NQ], U32, "wc%d" % b)
+            wsc[b] = place([P, NQ], U8, "wsc%d" % b)
             nc.vector.quantize_mx(out=wc[b][:].bitcast(FP8X4), scales=wsc[b][:], in_=wq[b][:].rearrange("p q t -> p (q t)"))
 
-        def product(y, b, j, cols):
+        res = [place([P, DV], F32, "res%d" % b) for b in range(B)]
+
+        def finish(b, j, tag):
+            y = ps.tile([P, P], F32, name="y%d%d" % (b, j), tag=tag)
             nc.tensor.matmul_mx(
-                out=y,
+                out=y[:],
                 lhsT=wc[b][:].bitcast(FP8X4),
                 lhsT_scale=wsc[b][:],
-                rhs=vc[b, j][:, cols].bitcast(FP8X4),
-                rhs_scale=vsc[b, j][:, cols],
+                rhs=vc[b, j][:].bitcast(FP8X4),
+                rhs_scale=vsc[b, j][:],
                 start=True,
                 stop=True,
             )
-
-        def finish(b):
-            res = sb.tile([P, DV], F32, name="res%d" % b, align_bytes=64)
-            if b == 0:
-                low = ps.tile([P, P], F32, name="y00", tag="y0")
-                product(low[:], b, 0, slice(0, P))
-                nc.scalar.activation(res[:, 0:P], low[:], ACT.Copy, scale=1.0 / 16.0)
-                high = ps.tile([P, P], F32, name="y01", tag="vst0")
-                product(high[:], b, 1, slice(0, P))
-                nc.vector.tensor_scalar(res[:, P:DV], high[:], 1.0 / 16.0, None, MULT)
+            part = res[b][:, j * P : (j + 1) * P]
+            if (b, j) == (1, 1):
+                nc.vector.tensor_scalar(part, y[:], 1.0 / 16.0, None, MULT)
             else:
-                early = ps.tile([P, P], F32, name="y1", tag="y1")
-                product(early[:], b, 0, slice(0, P))
-                nc.scalar.activation(res[:, 0:P], early[:], ACT.Copy, scale=1.0 / 16.0)
-                for h in range(2):
-                    late = ps.tile([P, P // 2], F32, name="ylate%d" % h, tag=("vt1", "z1")[h])
-                    product(late[:], b, 1, slice(h * (P // 2), (h + 1) * (P // 2)))
-                    nc.vector.tensor_scalar(
-                        res[:, P + h * (P // 2) : P + (h + 1) * (P // 2)], late[:], 1.0 / 16.0, None, MULT
-                    )
-            nc.sync.dma_start(out=out[b], in_=res[:])
+                nc.scalar.activation(part, y[:], ACT.Copy, scale=1.0 / 16.0)
+            if j == 1:
+                nc.sync.dma_start(out=out[b], in_=res[b][:])
 
-        gather_vs()
-        listed_scales = gather_ks()
-        for j in range(PLANES):
-            cast_v(0, j)
-            gather_v(0, j)
-            turn_v(0, j)
-        empty_v(0, 0)
-        nc.scalar.copy(held[:], token_scales(0))
-        cast_v(1, 0)
-        gather_v(1, 0)
+        gather_vs(0)
+        gather_vs(1)
+        hold_vs(0)
         gather_k(0)
-        order_ks(listed_scales)
+        gather_ks(0)
         cast_q(0)
         quant_q(0)
-        quant_v(0, 0)
-        empty_v(0, 1)
-        gather_k(1)
+        gather_ks(1, AT_QRAW[0])
+        gather_v(0, 0, ["scalar"], AT_VG00)
+        hold_vs(1, AT_VWIN00)
+        scores(0, AT_PW0)
+        turn_v(0, 0)
+        empty_v(0, 0)
         cast_q(1)
         quant_q(1)
-        quant_v(0, 1)
-        scores(0)
-        turn_v(1, 0)
-        empty_v(1, 0)
+        gather_k(1, AT_QRAW[1])
         weigh(0)
-        scores(1)
-        turned_last = gather_last()
-        weigh(1)
-        empty_last(turned_last)
+        gather_v(0, 1, ["scalar"], AT_VG01)
+        scores(1, AT_PW1)
+        turn_v(0, 1)
+        empty_v(0, 1)
+        quant_v(0, 0, AT_PW0 - 448)
         quant_w(0)
-        quant_v(1, 0)
+        gather_v(1, 0, ["vector"], AT_PW0 + 64)
+        turn_v(1, 0)
+        weigh(1)
+        gather_v(1, 1, ["vector", "scalar"], AT_VG01 - 512)
+        turn_v(1, 1)
+        finish(0, 0, "vst0")
+        empty_v(1, 0)
+        empty_v(1, 1)
+        quant_v(0, 1, AT_PW1 + 512)
         quant_w(1)
-        quant_v(1, 1)
-        finish(0)
-        finish(1)
+        quant_v(1, 0, AT_PW1 + 1024)
+        quant_v(1, 1, AT_PW1 + 1536)
+        finish(0, 1, "vst1")
+        finish(1, 0, "z0")
+        finish(1, 1, "vt00")

@@ -23,12 +23,19 @@ SEG = T // B
 COLS = N // 16
 PLANES = DV // P
 
-AT_VWIN00 = 0
-AT_PW0 = AT_VWIN00 + 2048
-AT_VG01 = AT_PW0 + 2048
-AT_VG00 = AT_VG01 + 512
-AT_PW1 = AT_VG00 + 512
-AT_QRAW = [8192, 10240]
+AT_KG0 = 0
+AT_VWIN = {(0, 0): 2048}
+AT_VG01 = AT_VWIN[0, 0] - 512
+AT_PW0 = AT_VWIN[0, 0] + 4096 - 64
+AT_VC0 = AT_PW0 - 960
+AT_PW10 = AT_PW0 + 1024
+AT_PW11 = AT_PW10 + 2624
+AT_VG11 = AT_PW11 + 1024
+AT_KG1 = 12288
+AT_QRAW = [AT_KG1 + 5056 - 64, AT_KG1 + 2048 - 64]
+AT_VG00 = AT_QRAW[1] + 2048
+HALF = NQ // 2
+SHARE = {0: 288, 1: 384}
 
 
 def dealt(t):
@@ -54,7 +61,7 @@ def tile_attend_silu_seg_kernel(tc, qT, k_words, k_scales, vT, vs, offs, out):
         vwin = {}
         for b in range(B):
             for j in range(PLANES):
-                vwin[b, j] = place([P, (b + 1) * SEG], F32, "vwin%d%d" % (b, j), AT_VWIN00 if (b, j) == (0, 0) else None)
+                vwin[b, j] = place([P, (b + 1) * SEG], F32, "vwin%d%d" % (b, j), AT_VWIN.get((b, j)))
         qraw = [place([P, PACK, NQ], F32, "qraw%d" % b, AT_QRAW[b]) for b in range(B)]
         ident = place([P, P], F32, "ident")
         warm = sb.tile([P, 8], F32, name="warm")
@@ -96,9 +103,8 @@ def tile_attend_silu_seg_kernel(tc, qT, k_words, k_scales, vT, vs, offs, out):
         load_v(1, 0)
         load_v(1, 1)
 
-        def lst(b, part=0, parts=1):
-            width = COLS // parts
-            return offsets[:, b * COLS + part * width : b * COLS + (part + 1) * width]
+        def lst(b, first=0, last=N):
+            return offsets[:, b * COLS + first // 16 : b * COLS + last // 16]
 
         kg, ksg, qb, vg, vt, vst, vq = {}, {}, {}, {}, {}, {}, {}
         held, pw, wq = {}, {}, {}
@@ -111,7 +117,7 @@ def tile_attend_silu_seg_kernel(tc, qT, k_words, k_scales, vT, vs, offs, out):
             for t in range(PACK):
                 nc.tensor.transpose(vst[b][:, t, :], listed[:, t:N:PACK], ident[:])
 
-        def hold_vs(b, at=None):
+        def hold_vs(b, at):
             held[b] = place([P, 1, PACK], F32, "held%d" % b, at)
             nc.scalar.copy(held[b][:], vst[b][:, :, P - 1 : P].rearrange("p t o -> p o t"))
 
@@ -125,31 +131,26 @@ def tile_attend_silu_seg_kernel(tc, qT, k_words, k_scales, vT, vs, offs, out):
 
         def gather_v(b, j, who, at):
             vg[b, j] = place([P, N], BF16, "vg%d%d" % (b, j), at)
-            width = N // len(who)
-            for h, engine in enumerate(who):
-                part = vg[b, j][:, h * width : (h + 1) * width]
-                listed = vwin[b, j][:].indirect(lst(b, h, len(who)))
+            for engine, first, last in who:
+                part = vg[b, j][:, first:last]
+                listed = vwin[b, j][:].indirect(lst(b, first, last))
                 if engine == "vector":
                     nc.vector.tensor_copy(part, listed)
                 else:
                     nc.scalar.activation(part, listed, ACT.Copy)
 
-        def turn_v(b, j):
-            vt[b, j] = ps.tile([P, 2, P], F32, name="vt%d%d" % (b, j))
+        def turn_v(b, j, tag):
+            vt[b, j] = ps.tile([P, 2, P], F32, name="vt%d%d" % (b, j), tag=tag)
             pairs = vg[b, j][:].bitcast(F32)
             for u in range(2):
                 nc.tensor.transpose(vt[b, j][:, u, :], pairs[:, u : N // 2 : 2], ident[:])
 
-        def empty_v(b, j):
-            vq[b, j] = place([P, P * PACK], BF16, "vq%d%d" % (b, j))
-            nc.scalar.copy(
-                vq[b, j][:].bitcast(F32).rearrange("p (e u) -> p e u", u=2), vt[b, j][:].rearrange("p u e -> p e u")
-            )
+        def empty_v(b, j, at=None, copy=nc.scalar.copy):
+            vq[b, j] = place([P, P * PACK], BF16, "vq%d%d" % (b, j), at)
+            copy(vq[b, j][:].bitcast(F32).rearrange("p (e u) -> p e u", u=2), vt[b, j][:].rearrange("p u e -> p e u"))
 
-        def quant_v(b, j, at):
-            vc[b, j] = place([P, P], U32, "vc%d%d" % (b, j), at)
-            vsc[b, j] = place([P, P], U8, "vsc%d%d" % (b, j))
-            nc.vector.quantize_mx(out=vc[b, j][:].bitcast(FP8X4), scales=vsc[b, j][:], in_=vq[b, j][:])
+        def quantise(codes, scales, values):
+            nc.vector.quantize_mx(out=codes.bitcast(FP8X4), scales=scales, in_=values)
 
         def cast_q(b):
             qb[b] = place([P, NQ, PACK], BF16, "qb%d" % b)
@@ -158,7 +159,7 @@ def tile_attend_silu_seg_kernel(tc, qT, k_words, k_scales, vT, vs, offs, out):
         def quant_q(b):
             qc[b] = place([P, NQ], U32, "qc%d" % b)
             qsc[b] = place([P, NQ], U8, "qsc%d" % b)
-            nc.vector.quantize_mx(out=qc[b][:].bitcast(FP8X4), scales=qsc[b][:], in_=qb[b][:].rearrange("p n j -> p (n j)"))
+            quantise(qc[b][:], qsc[b][:], qb[b][:].rearrange("p n j -> p (n j)"))
 
         def scores(b, at):
             z = ps.tile([P, PACK, NQ], F32, name="z%d" % b)
@@ -172,74 +173,86 @@ def tile_attend_silu_seg_kernel(tc, qT, k_words, k_scales, vT, vs, offs, out):
                     start=True,
                     stop=True,
                 )
-            pw[b] = place([P, NQ, PACK], F32, "pw%d" % b, at)
-            nc.scalar.activation(pw[b][:], z[:].rearrange("p t q -> p q t"), ACT.Silu)
+            width = NQ // len(at)
+            for h in range(len(at)):
+                room = place([P, at[h][1], PACK], F32, "pw%d%d" % (b, h), at[h][0])
+                pw[b, h] = room[:, 0:width, :]
+                scored = z[:, :, h * width : (h + 1) * width]
+                nc.scalar.activation(pw[b, h], scored.rearrange("p t q -> p q t"), ACT.Silu)
 
-        def weigh(b):
-            wq[b] = place([P, NQ, PACK], BF16, "wq%d" % b)
-            nc.gpsimd.tensor_tensor(wq[b][:], pw[b][:], held[b][:].to_broadcast([P, NQ, PACK]), MULT)
+        def weigh(b, h, width, engine, at=None):
+            wq[b, h] = place([P, width, PACK], BF16, "wq%d%d" % (b, h), at)
+            engine.tensor_tensor(wq[b, h][:], pw[b, h], held[b][:].to_broadcast([P, width, PACK]), MULT)
 
-        def quant_w(b):
-            wc[b] = place([P, NQ], U32, "wc%d" % b)
-            wsc[b] = place([P, NQ], U8, "wsc%d" % b)
-            nc.vector.quantize_mx(out=wc[b][:].bitcast(FP8X4), scales=wsc[b][:], in_=wq[b][:].rearrange("p q t -> p (q t)"))
+        def quant_w(b, h, width):
+            cols = slice(h * width, (h + 1) * width)
+            quantise(wc[b][:, cols], wsc[b][:, cols], wq[b, h][:].rearrange("p q t -> p (q t)"))
 
-        res = [place([P, DV], F32, "res%d" % b) for b in range(B)]
+        def quant_v(b, j):
+            cols = slice(j * P, (j + 1) * P)
+            quantise(vc[b][:, cols], vsc[b][:, cols], vq[b, j][:])
 
-        def finish(b, j, tag):
-            y = ps.tile([P, P], F32, name="y%d%d" % (b, j), tag=tag)
+        def product(b, cols, name, tag):
+            y = ps.tile([P, cols.stop - cols.start], F32, name=name, tag=tag)
             nc.tensor.matmul_mx(
                 out=y[:],
                 lhsT=wc[b][:].bitcast(FP8X4),
                 lhsT_scale=wsc[b][:],
-                rhs=vc[b, j][:].bitcast(FP8X4),
-                rhs_scale=vsc[b, j][:],
+                rhs=vc[b][:, cols].bitcast(FP8X4),
+                rhs_scale=vsc[b][:, cols],
                 start=True,
                 stop=True,
             )
-            part = res[b][:, j * P : (j + 1) * P]
-            if (b, j) == (1, 1):
-                nc.vector.tensor_scalar(part, y[:], 1.0 / 16.0, None, MULT)
-            else:
-                nc.scalar.activation(part, y[:], ACT.Copy, scale=1.0 / 16.0)
-            if j == 1:
-                nc.sync.dma_start(out=out[b], in_=res[b][:])
+            return y
 
+        for b in range(B):
+            wc[b] = place([P, NQ], U32, "wc%d" % b, (AT_VG11 + 1024, AT_PW10 + 576)[b])
+            wsc[b] = place([P, NQ], U8, "wsc%d" % b)
+            vc[b] = place([P, DV], U32, "vc%d" % b, (AT_VC0, None)[b])
+            vsc[b] = place([P, DV], U8, "vsc%d" % b)
+        res = [place([P, DV], F32, "res%d" % b, (AT_VG11, None)[b]) for b in range(B)]
+
+        gather_k(0, AT_KG0)
         gather_vs(0)
         gather_vs(1)
-        hold_vs(0)
-        gather_k(0)
         gather_ks(0)
         cast_q(0)
         quant_q(0)
-        gather_ks(1, AT_QRAW[0])
-        gather_v(0, 0, ["scalar"], AT_VG00)
-        hold_vs(1, AT_VWIN00)
-        scores(0, AT_PW0)
-        turn_v(0, 0)
-        empty_v(0, 0)
+        gather_ks(1, AT_QRAW[0] + 64)
+        gather_v(0, 0, [("scalar", 0, N)], AT_VG00)
+        hold_vs(0, AT_VWIN[0, 0] + 512)
+        hold_vs(1, AT_VWIN[0, 0] + 576)
+        scores(0, [(AT_PW0, 3 * NQ)])
+        turn_v(0, 0, "vt00")
         cast_q(1)
         quant_q(1)
-        gather_k(1, AT_QRAW[1])
-        weigh(0)
-        gather_v(0, 1, ["scalar"], AT_VG01)
-        scores(1, AT_PW1)
-        turn_v(0, 1)
-        empty_v(0, 1)
-        quant_v(0, 0, AT_PW0 - 448)
-        quant_w(0)
-        gather_v(1, 0, ["vector"], AT_PW0 + 64)
-        turn_v(1, 0)
-        weigh(1)
-        gather_v(1, 1, ["vector", "scalar"], AT_VG01 - 512)
-        turn_v(1, 1)
-        finish(0, 0, "vst0")
-        empty_v(1, 0)
+        gather_k(1, AT_KG1)
+        empty_v(0, 0, AT_KG1 + 2048, nc.vector.tensor_copy)
+        weigh(0, 0, NQ, nc.gpsimd)
+        gather_v(0, 1, [("scalar", 0, N)], AT_VG01)
+        gather_v(1, 0, [("vector", 0, SHARE[0]), ("scalar", SHARE[0], N)], AT_VG00 - 512)
+        quant_v(0, 0)
+        quant_w(0, 0, NQ)
+        scores(1, [(AT_PW10, NQ), (AT_PW11, HALF)])
+        turn_v(0, 1, "vt00")
+        turn_v(1, 0, "vt10")
+        weigh(1, 0, HALF, nc.gpsimd)
+        gather_v(1, 1, [("vector", 0, SHARE[1]), ("scalar", SHARE[1], N)], AT_VG11)
+        turn_v(1, 1, "vt11")
+        weigh(1, 1, HALF, nc.vector, AT_PW10 + 1088)
+        empty_v(0, 1, AT_PW10 - 960)
+        empty_v(1, 0, AT_PW10 + 1600)
         empty_v(1, 1)
-        quant_v(0, 1, AT_PW1 + 512)
-        quant_w(1)
-        quant_v(1, 0, AT_PW1 + 1024)
-        quant_v(1, 1, AT_PW1 + 1536)
-        finish(0, 1, "vst1")
-        finish(1, 0, "z0")
-        finish(1, 1, "vt00")
+        quant_w(1, 0, HALF)
+        quant_v(0, 1)
+        quant_w(1, 1, HALF)
+        quant_v(1, 0)
+        quant_v(1, 1)
+        y0 = product(0, slice(0, DV), "y0", "vst0")
+        nc.scalar.activation(res[0][:], y0[:], ACT.Copy, scale=1.0 / 16.0)
+        nc.sync.dma_start(out=out[0], in_=res[0][:])
+        y10 = product(1, slice(0, P), "y10", "vst1")
+        nc.scalar.activation(res[1][:, 0:P], y10[:], ACT.Copy, scale=1.0 / 16.0)
+        y11 = product(1, slice(P, DV), "y11", "z0")
+        nc.vector.tensor_scalar(res[1][:, P:DV], y11[:], 1.0 / 16.0, None, MULT)
+        nc.sync.dma_start(out=out[1], in_=res[1][:])

@@ -23,19 +23,15 @@ SEG = T // B
 COLS = N // 16
 PLANES = DV // P
 
-AT_KG0 = 0
-AT_VWIN = {(0, 0): 2048}
-AT_VG01 = AT_VWIN[0, 0] - 512
+AT_VWIN = {(0, 0): 0, (1, 1): 20480}
 AT_PW0 = AT_VWIN[0, 0] + 4096 - 64
-AT_VC0 = AT_PW0 - 960
-AT_PW10 = AT_PW0 + 1024
-AT_PW11 = AT_PW10 + 2624
-AT_VG11 = AT_PW11 + 1024
-AT_KG1 = 12288
-AT_QRAW = [AT_KG1 + 5056 - 64, AT_KG1 + 2048 - 64]
-AT_VG00 = AT_QRAW[1] + 2048
+AT_PW1 = AT_PW0 + 64
+AT_VG10 = AT_PW1 + 2048
+AT_VG11 = AT_VG10 + 1024
+AT_QRAW = [15360, 10240]
+AT_VG00 = AT_QRAW[0] - 960
+AT_LATE = AT_VWIN[1, 1]
 HALF = NQ // 2
-SHARE = {0: 288, 1: 384}
 
 
 def dealt(t):
@@ -119,7 +115,7 @@ def tile_attend_silu_seg_kernel(tc, qT, k_words, k_scales, vT, vs, offs, out):
 
         def hold_vs(b, at):
             held[b] = place([P, 1, PACK], F32, "held%d" % b, at)
-            nc.scalar.copy(held[b][:], vst[b][:, :, P - 1 : P].rearrange("p t o -> p o t"))
+            nc.scalar.copy(held[b][:], token_scales(b))
 
         def gather_ks(b, at=None):
             ksg[b] = place([P, PACK, P], U8, "ksg%d" % b, at)
@@ -145,9 +141,11 @@ def tile_attend_silu_seg_kernel(tc, qT, k_words, k_scales, vT, vs, offs, out):
             for u in range(2):
                 nc.tensor.transpose(vt[b, j][:, u, :], pairs[:, u : N // 2 : 2], ident[:])
 
-        def empty_v(b, j, at=None, copy=nc.scalar.copy):
+        def empty_v(b, j, at=None):
             vq[b, j] = place([P, P * PACK], BF16, "vq%d%d" % (b, j), at)
-            copy(vq[b, j][:].bitcast(F32).rearrange("p (e u) -> p e u", u=2), vt[b, j][:].rearrange("p u e -> p e u"))
+            nc.scalar.copy(
+                vq[b, j][:].bitcast(F32).rearrange("p (e u) -> p e u", u=2), vt[b, j][:].rearrange("p u e -> p e u")
+            )
 
         def quantise(codes, scales, values):
             nc.vector.quantize_mx(out=codes.bitcast(FP8X4), scales=scales, in_=values)
@@ -180,39 +178,42 @@ def tile_attend_silu_seg_kernel(tc, qT, k_words, k_scales, vT, vs, offs, out):
                 scored = z[:, :, h * width : (h + 1) * width]
                 nc.scalar.activation(pw[b, h], scored.rearrange("p t q -> p q t"), ACT.Silu)
 
-        def weigh(b, h, width, engine, at=None):
-            wq[b, h] = place([P, width, PACK], BF16, "wq%d%d" % (b, h), at)
-            engine.tensor_tensor(wq[b, h][:], pw[b, h], held[b][:].to_broadcast([P, width, PACK]), MULT)
+        def token_scales(b):
+            return vst[b][:, :, P - 1 : P].rearrange("p t o -> p o t")
 
-        def quant_w(b, h, width):
-            cols = slice(h * width, (h + 1) * width)
-            quantise(wc[b][:, cols], wsc[b][:, cols], wq[b, h][:].rearrange("p q t -> p (q t)"))
+        def weigh(engine, weights, silu, scales):
+            engine.tensor_tensor(weights, silu, scales.to_broadcast([P, HALF, PACK]), MULT)
+
+        def quant_w(b, cols, weights):
+            quantise(wc[b][:, cols], wsc[b][:, cols], weights.rearrange("p q t -> p (q t)"))
 
         def quant_v(b, j):
-            cols = slice(j * P, (j + 1) * P)
-            quantise(vc[b][:, cols], vsc[b][:, cols], vq[b, j][:])
+            vc[b, j] = place([P, P], U32, "vc%d%d" % (b, j))
+            vsc[b, j] = place([P, P], U8, "vsc%d%d" % (b, j))
+            quantise(vc[b, j][:], vsc[b, j][:], vq[b, j][:])
 
-        def product(b, cols, name, tag):
-            y = ps.tile([P, cols.stop - cols.start], F32, name=name, tag=tag)
+        def product(b, j, tag):
+            y = ps.tile([P, P], F32, name="y%d%d" % (b, j), tag=tag)
             nc.tensor.matmul_mx(
                 out=y[:],
                 lhsT=wc[b][:].bitcast(FP8X4),
                 lhsT_scale=wsc[b][:],
-                rhs=vc[b][:, cols].bitcast(FP8X4),
-                rhs_scale=vsc[b][:, cols],
+                rhs=vc[b, j][:].bitcast(FP8X4),
+                rhs_scale=vsc[b, j][:],
                 start=True,
                 stop=True,
             )
             return y
 
         for b in range(B):
-            wc[b] = place([P, NQ], U32, "wc%d" % b, (AT_VG11 + 1024, AT_PW10 + 576)[b])
+            wc[b] = place([P, NQ], U32, "wc%d" % b, (None, AT_LATE)[b])
             wsc[b] = place([P, NQ], U8, "wsc%d" % b)
-            vc[b] = place([P, DV], U32, "vc%d" % b, (AT_VC0, None)[b])
-            vsc[b] = place([P, DV], U8, "vsc%d" % b)
         res = [place([P, DV], F32, "res%d" % b, (AT_VG11, None)[b]) for b in range(B)]
+        low, high = slice(0, HALF), slice(HALF, NQ)
+        wq0 = place([P, NQ, PACK], BF16, "wq0")
+        wq1 = [place([P, HALF, PACK], BF16, "wq1%d" % h, (None, AT_LATE + 512)[h]) for h in range(2)]
 
-        gather_k(0, AT_KG0)
+        gather_k(0)
         gather_vs(0)
         gather_vs(1)
         gather_ks(0)
@@ -220,39 +221,42 @@ def tile_attend_silu_seg_kernel(tc, qT, k_words, k_scales, vT, vs, offs, out):
         quant_q(0)
         gather_ks(1, AT_QRAW[0] + 64)
         gather_v(0, 0, [("scalar", 0, N)], AT_VG00)
-        hold_vs(0, AT_VWIN[0, 0] + 512)
-        hold_vs(1, AT_VWIN[0, 0] + 576)
+        hold_vs(0, AT_VWIN[0, 0])
+        hold_vs(1, AT_VWIN[0, 0] + 64)
         scores(0, [(AT_PW0, 3 * NQ)])
         turn_v(0, 0, "vt00")
+        empty_v(0, 0)
         cast_q(1)
         quant_q(1)
-        gather_k(1, AT_KG1)
-        empty_v(0, 0, AT_KG1 + 2048, nc.vector.tensor_copy)
-        weigh(0, 0, NQ, nc.gpsimd)
-        gather_v(0, 1, [("scalar", 0, N)], AT_VG01)
-        gather_v(1, 0, [("vector", 0, SHARE[0]), ("scalar", SHARE[0], N)], AT_VG00 - 512)
+        gather_k(1, AT_QRAW[1])
+        weigh(nc.gpsimd, wq0[:, low, :], pw[0, 0][:, low, :], held[0][:])
+        weigh(nc.vector, wq0[:, high, :], pw[0, 0][:, high, :], token_scales(0))
+        gather_v(0, 1, [("scalar", 0, N)], AT_VG00 - 960)
         quant_v(0, 0)
-        quant_w(0, 0, NQ)
-        scores(1, [(AT_PW10, NQ), (AT_PW11, HALF)])
+        quant_w(0, slice(0, NQ), wq0[:])
+        gather_v(1, 0, [("vector", 0, N)], AT_VG10)
+        scores(1, [(AT_PW1, HALF), (AT_PW1 + 1024, HALF)])
         turn_v(0, 1, "vt00")
+        y00 = product(0, 0, "y00")
         turn_v(1, 0, "vt10")
-        weigh(1, 0, HALF, nc.gpsimd)
-        gather_v(1, 1, [("vector", 0, SHARE[1]), ("scalar", SHARE[1], N)], AT_VG11)
+        weigh(nc.gpsimd, wq1[0][:], pw[1, 0], held[1][:])
+        gather_v(1, 1, [("vector", 0, N // 2), ("scalar", N // 2, N)], AT_VG11)
         turn_v(1, 1, "vt11")
-        weigh(1, 1, HALF, nc.vector, AT_PW10 + 1088)
-        empty_v(0, 1, AT_PW10 - 960)
-        empty_v(1, 0, AT_PW10 + 1600)
+        weigh(nc.vector, wq1[1][:], pw[1, 1], token_scales(1))
+        empty_v(0, 1, AT_LATE + 1024)
+        empty_v(1, 0, AT_LATE + 2048)
         empty_v(1, 1)
-        quant_w(1, 0, HALF)
+        quant_w(1, low, wq1[0][:])
         quant_v(0, 1)
-        quant_w(1, 1, HALF)
+        quant_w(1, high, wq1[1][:])
         quant_v(1, 0)
         quant_v(1, 1)
-        y0 = product(0, slice(0, DV), "y0", "vst0")
-        nc.scalar.activation(res[0][:], y0[:], ACT.Copy, scale=1.0 / 16.0)
+        y01 = product(0, 1, "vst0")
+        y10 = product(1, 0, "z0")
+        y11 = product(1, 1, "z1")
+        nc.scalar.activation(res[0][:, 0:P], y00[:], ACT.Copy, scale=1.0 / 16.0)
+        nc.scalar.activation(res[0][:, P:DV], y01[:], ACT.Copy, scale=1.0 / 16.0)
         nc.sync.dma_start(out=out[0], in_=res[0][:])
-        y10 = product(1, slice(0, P), "y10", "vst1")
         nc.scalar.activation(res[1][:, 0:P], y10[:], ACT.Copy, scale=1.0 / 16.0)
-        y11 = product(1, slice(P, DV), "y11", "z0")
         nc.vector.tensor_scalar(res[1][:, P:DV], y11[:], 1.0 / 16.0, None, MULT)
         nc.sync.dma_start(out=out[1], in_=res[1][:])

@@ -187,8 +187,8 @@ def tile_attend_silu_seg_kernel(tc, qT, k_words, k_scales, vT, vs, offs, out):
         def quant_w(b, cols, weights):
             quantise(wc[b][:, cols], wsc[b][:, cols], weights.rearrange("p q t -> p (q t)"))
 
-        def quant_v(b, j):
-            vc[b, j] = place([P, P], U32, "vc%d%d" % (b, j))
+        def quant_v(b, j, at=None):
+            vc[b, j] = place([P, P], U32, "vc%d%d" % (b, j), at)
             vsc[b, j] = place([P, P], U8, "vsc%d%d" % (b, j))
             quantise(vc[b, j][:], vsc[b, j][:], vq[b, j][:])
 
@@ -237,17 +237,17 @@ def tile_attend_silu_seg_kernel(tc, qT, k_words, k_scales, vT, vs, offs, out):
         gather_v(1, 0, [("vector", 0, N)], AT_VG10)
         scores(1, [(AT_PW1, HALF), (AT_PW1 + 1024, HALF)])
         turn_v(0, 1, "vt00")
+        empty_v(0, 1, AT_VG11 + 1024)
         y00 = product(0, 0, "y00")
         turn_v(1, 0, "vt10")
         weigh(nc.gpsimd, wq1[0][:], pw[1, 0], held[1][:])
         gather_v(1, 1, [("vector", 0, N // 2), ("scalar", N // 2, N)], AT_VG11)
         turn_v(1, 1, "vt11")
         weigh(nc.vector, wq1[1][:], pw[1, 1], token_scales(1))
-        empty_v(0, 1, AT_LATE + 1024)
         empty_v(1, 0, AT_LATE + 2048)
         empty_v(1, 1)
         quant_w(1, low, wq1[0][:])
-        quant_v(0, 1)
+        quant_v(0, 1, AT_LATE + 1024)
         quant_w(1, high, wq1[1][:])
         quant_v(1, 0)
         quant_v(1, 1)

@@ -32,6 +32,11 @@ AT_QRAW = [15360, 10240]
 AT_VG00 = AT_QRAW[0] - 960
 AT_LATE = AT_VWIN[1, 1]
 HALF = NQ // 2
+EARLY = NQ // 4
+
+
+def cuts(parts):
+    return [slice(h * P // parts, (h + 1) * P // parts) for h in range(parts)]
 
 
 def dealt(t):
@@ -141,11 +146,11 @@ def tile_attend_silu_seg_kernel(tc, qT, k_words, k_scales, vT, vs, offs, out):
             for u in range(2):
                 nc.tensor.transpose(vt[b, j][:, u, :], pairs[:, u : N // 2 : 2], ident[:])
 
-        def empty_v(b, j, at=None):
+        def empty_v(b, j, at=None, parts=1):
             vq[b, j] = place([P, P * PACK], BF16, "vq%d%d" % (b, j), at)
-            nc.scalar.copy(
-                vq[b, j][:].bitcast(F32).rearrange("p (e u) -> p e u", u=2), vt[b, j][:].rearrange("p u e -> p e u")
-            )
+            words = vq[b, j][:].bitcast(F32).rearrange("p (e u) -> p e u", u=2)
+            for part in cuts(parts):
+                nc.scalar.copy(words[:, part, :], vt[b, j][:].rearrange("p u e -> p e u")[:, part, :])
 
         def quantise(codes, scales, values):
             nc.vector.quantize_mx(out=codes.bitcast(FP8X4), scales=scales, in_=values)
@@ -159,7 +164,7 @@ def tile_attend_silu_seg_kernel(tc, qT, k_words, k_scales, vT, vs, offs, out):
             qsc[b] = place([P, NQ], U8, "qsc%d" % b)
             quantise(qc[b][:], qsc[b][:], qb[b][:].rearrange("p n j -> p (n j)"))
 
-        def scores(b, at):
+        def scores(b, parts):
             z = ps.tile([P, PACK, NQ], F32, name="z%d" % b)
             for t in range(PACK):
                 nc.tensor.matmul_mx(
@@ -171,47 +176,47 @@ def tile_attend_silu_seg_kernel(tc, qT, k_words, k_scales, vT, vs, offs, out):
                     start=True,
                     stop=True,
                 )
-            width = NQ // len(at)
-            for h in range(len(at)):
-                room = place([P, at[h][1], PACK], F32, "pw%d%d" % (b, h), at[h][0])
-                pw[b, h] = room[:, 0:width, :]
-                scored = z[:, :, h * width : (h + 1) * width]
+            for h, (at, rows, part) in enumerate(parts):
+                room = place([P, rows, PACK], F32, "pw%d%d" % (b, h), at)
+                pw[b, h] = room[:, 0 : part.stop - part.start, :]
+                scored = z[:, :, part]
                 nc.scalar.activation(pw[b, h], scored.rearrange("p t q -> p q t"), ACT.Silu)
 
         def token_scales(b):
             return vst[b][:, :, P - 1 : P].rearrange("p t o -> p o t")
 
         def weigh(engine, weights, silu, scales):
-            engine.tensor_tensor(weights, silu, scales.to_broadcast([P, HALF, PACK]), MULT)
+            engine.tensor_tensor(weights, silu, scales.to_broadcast(list(weights.shape)), MULT)
 
-        def quant_w(b, cols, weights):
-            quantise(wc[b][:, cols], wsc[b][:, cols], weights.rearrange("p q t -> p (q t)"))
+        def quant_w(b):
+            quantise(wc[b][:], wsc[b][:], wq[b][:].rearrange("p q t -> p (q t)"))
 
-        def quant_v(b, j, at=None):
+        def quant_v(b, j, at=None, parts=1):
             vc[b, j] = place([P, P], U32, "vc%d%d" % (b, j), at)
             vsc[b, j] = place([P, P], U8, "vsc%d%d" % (b, j))
-            quantise(vc[b, j][:], vsc[b, j][:], vq[b, j][:])
+            for part in cuts(parts):
+                quantise(vc[b, j][:, part], vsc[b, j][:, part], vq[b, j][:, part.start * PACK : part.stop * PACK])
 
-        def product(b, j, tag):
-            y = ps.tile([P, P], F32, name="y%d%d" % (b, j), tag=tag)
+        def product(b, j, tag, part=slice(0, P)):
+            y = ps.tile([P, part.stop - part.start], F32, name="y%d%d%d" % (b, j, part.start), tag=tag)
             nc.tensor.matmul_mx(
                 out=y[:],
                 lhsT=wc[b][:].bitcast(FP8X4),
                 lhsT_scale=wsc[b][:],
-                rhs=vc[b, j][:].bitcast(FP8X4),
-                rhs_scale=vsc[b, j][:],
+                rhs=vc[b, j][:, part].bitcast(FP8X4),
+                rhs_scale=vsc[b, j][:, part],
                 start=True,
                 stop=True,
             )
             return y
 
         for b in range(B):
+            wq[b] = place([P, NQ, PACK], BF16, "wq%d" % b)
             wc[b] = place([P, NQ], U32, "wc%d" % b, (None, AT_LATE)[b])
             wsc[b] = place([P, NQ], U8, "wsc%d" % b)
         res = [place([P, DV], F32, "res%d" % b, (AT_VG11, None)[b]) for b in range(B)]
-        low, high = slice(0, HALF), slice(HALF, NQ)
-        wq0 = place([P, NQ, PACK], BF16, "wq0")
-        wq1 = [place([P, HALF, PACK], BF16, "wq1%d" % h, (None, AT_LATE + 512)[h]) for h in range(2)]
+        low, high = cuts(2)
+        early, rest = slice(0, EARLY), slice(EARLY, NQ)
 
         gather_k(0)
         gather_vs(0)
@@ -223,40 +228,40 @@ def tile_attend_silu_seg_kernel(tc, qT, k_words, k_scales, vT, vs, offs, out):
         gather_v(0, 0, [("scalar", 0, N)], AT_VG00)
         hold_vs(0, AT_VWIN[0, 0])
         hold_vs(1, AT_VWIN[0, 0] + 64)
-        scores(0, [(AT_PW0, 3 * NQ)])
+        scores(0, [(AT_PW0, 3 * NQ, slice(0, NQ))])
         turn_v(0, 0, "vt00")
         empty_v(0, 0)
         cast_q(1)
         quant_q(1)
         gather_k(1, AT_QRAW[1])
-        weigh(nc.gpsimd, wq0[:, low, :], pw[0, 0][:, low, :], held[0][:])
-        weigh(nc.vector, wq0[:, high, :], pw[0, 0][:, high, :], token_scales(0))
+        weigh(nc.gpsimd, wq[0][:, low, :], pw[0, 0][:, low, :], held[0][:])
+        weigh(nc.vector, wq[0][:, high, :], pw[0, 0][:, high, :], token_scales(0))
         gather_v(0, 1, [("scalar", 0, N)], AT_VG00 - 960)
         quant_v(0, 0)
-        quant_w(0, slice(0, NQ), wq0[:])
+        quant_w(0)
         gather_v(1, 0, [("vector", 0, N)], AT_VG10)
-        scores(1, [(AT_PW1, HALF), (AT_PW1 + 1024, HALF)])
+        scores(1, [(AT_PW1, EARLY, early), (AT_PW1 + 512, NQ - EARLY, rest)])
         turn_v(0, 1, "vt00")
         empty_v(0, 1, AT_VG11 + 1024)
         y00 = product(0, 0, "y00")
         turn_v(1, 0, "vt10")
-        weigh(nc.gpsimd, wq1[0][:], pw[1, 0], held[1][:])
+        weigh(nc.gpsimd, wq[1][:, early, :], pw[1, 0], held[1][:])
+        weigh(nc.gpsimd, wq[1][:, rest, :], pw[1, 1], held[1][:])
         gather_v(1, 1, [("vector", 0, N // 2), ("scalar", N // 2, N)], AT_VG11)
         turn_v(1, 1, "vt11")
-        weigh(nc.vector, wq1[1][:], pw[1, 1], token_scales(1))
         empty_v(1, 0, AT_LATE + 2048)
-        empty_v(1, 1)
-        quant_w(1, low, wq1[0][:])
+        empty_v(1, 1, None, 2)
         quant_v(0, 1, AT_LATE + 1024)
-        quant_w(1, high, wq1[1][:])
+        quant_w(1)
         quant_v(1, 0)
-        quant_v(1, 1)
+        quant_v(1, 1, None, 2)
         y01 = product(0, 1, "vst0")
         y10 = product(1, 0, "z0")
-        y11 = product(1, 1, "z1")
+        last = [product(1, 1, tag, part) for tag, part in zip(("z1", "vst1"), cuts(2))]
         nc.scalar.activation(res[0][:, 0:P], y00[:], ACT.Copy, scale=1.0 / 16.0)
         nc.scalar.activation(res[0][:, P:DV], y01[:], ACT.Copy, scale=1.0 / 16.0)
         nc.sync.dma_start(out=out[0], in_=res[0][:])
         nc.scalar.activation(res[1][:, 0:P], y10[:], ACT.Copy, scale=1.0 / 16.0)
-        nc.vector.tensor_scalar(res[1][:, P:DV], y11[:], 1.0 / 16.0, None, MULT)
+        for y, part in zip(last, cuts(2)):
+            nc.vector.tensor_scalar(res[1][:, P + part.start : P + part.stop], y[:], 1.0 / 16.0, None, MULT)
         nc.sync.dma_start(out=out[1], in_=res[1][:])

@@ -262,6 +262,7 @@ def tile_attend_silu_seg_kernel(tc, qT, k_words, k_scales, vT, vs, offs, out):
         nc.scalar.activation(res[0][:, P:DV], y01[:], ACT.Copy, scale=1.0 / 16.0)
         nc.sync.dma_start(out=out[0], in_=res[0][:])
         nc.scalar.activation(res[1][:, 0:P], y10[:], ACT.Copy, scale=1.0 / 16.0)
+        nc.sync.dma_start(out=out[1][:, 0:P], in_=res[1][:, 0:P])
         for y, part in zip(last, cuts(2)):
             nc.vector.tensor_scalar(res[1][:, P + part.start : P + part.stop], y[:], 1.0 / 16.0, None, MULT)
-        nc.sync.dma_start(out=out[1], in_=res[1][:])
+        nc.sync.dma_start(out=out[1][:, P:DV], in_=res[1][:, P:DV])

@@ -91,7 +91,8 @@ def tile_attend_silu_seg_kernel(tc, qT, k_words, k_scales, vT, vs, offs, out):
             nc.sync.dma_start(out=qraw[b][:], in_=qT[b].rearrange("(p j) n -> p j n", j=PACK))
 
         nc.sync.dma_start(offsets[:], offs)
-        nc.scalar.dma_start(out=vsw[P - 1 : P, :], in_=vs[0:1, :])
+        for b in range(B):
+            nc.scalar.dma_start(out=vsw[P - 1 : P, seg(b)], in_=vs[0:1, seg(b)])
         nc.scalar.activation(warm2[:], warm[:], ACT.Silu)
         load_k(0)
         for r in range(4):
@@ -113,7 +114,7 @@ def tile_attend_silu_seg_kernel(tc, qT, k_words, k_scales, vT, vs, offs, out):
 
         def gather_vs(b):
             listed = place([P, N], F32, "vsg%d" % b)
-            nc.scalar.activation(listed[:], vsw[:].indirect(lst(b)), ACT.Copy)
+            nc.scalar.activation(listed[:], vsw[:, 0 : (b + 1) * SEG].indirect(lst(b)), ACT.Copy)
             vst[b] = ps.tile([P, PACK, P], F32, name="vst%d" % b)
             for t in range(PACK):
                 nc.tensor.transpose(vst[b][:, t, :], listed[:, t:N:PACK], ident[:])

@@ -22,25 +22,27 @@ PACK = 4
 SEG = T // B
 COLS = N // 16
 PLANES = DV // P
-
-AT_VWIN = {(0, 0): 0, (1, 1): 20480}
-AT_PW0 = AT_VWIN[0, 0] + 4096 - 64
-AT_PW1 = AT_PW0 + 64
-AT_VG10 = AT_PW1 + 2048
-AT_VG11 = AT_VG10 + 1024
-AT_QRAW = [15360, 10240]
-AT_VG00 = AT_QRAW[0] - 960
-AT_LATE = AT_VWIN[1, 1]
-HALF = NQ // 2
+ALIGN = 256
 EARLY = NQ // 4
+
+AT_KSC = 0
+AT_KW = AT_KSC + T
+AT_V10 = AT_KW + 4 * T
+AT_V11 = AT_V10 + 4 * T
+AT_VSW = AT_V11 + 4 * T
+AT_V00 = AT_VSW + 4 * T
+AT_V01 = AT_V00 + 4 * SEG
+AT_QRAW = [AT_V01 + 4 * SEG, AT_V01 + 4 * SEG + 4 * PACK * NQ]
+AT_VC00 = AT_KW
+AT_VG10 = AT_KW + 512
+AT_VG01 = AT_VSW + 512
+AT_P0 = AT_V00 + 1024
+AT_VWIN = {(0, 0): AT_V00, (0, 1): AT_V01, (1, 0): AT_V10, (1, 1): AT_V11}
+AT_LATE = AT_V11
 
 
 def cuts(parts):
     return [slice(h * P // parts, (h + 1) * P // parts) for h in range(parts)]
-
-
-def dealt(t):
-    return t.rearrange("x t p -> x p t")
 
 
 def tile_attend_silu_seg_kernel(tc, qT, k_words, k_scales, vT, vs, offs, out):
@@ -53,17 +55,17 @@ def tile_attend_silu_seg_kernel(tc, qT, k_words, k_scales, vT, vs, offs, out):
         def place(shape, dtype, name, at=None):
             if at is None:
                 return sb.tile(shape, dtype, name=name, align_bytes=64)
-            return shared.tile(shape, dtype, name=name, offset=at, align_bytes=64)
+            return shared.tile(shape, dtype, name=name, offset=at, align_bytes=ALIGN)
 
         offsets = sb.tile([P, B * COLS], U16, name="offsets")
-        kw = place([P, T], I32, "kw")
-        ksc = place([P, T], U8, "ksc")
-        vsw = place([P, T], F32, "vsw")
+        kw = place([P, T], I32, "kw", AT_KW)
+        ksc = place([P, T], U8, "ksc", AT_KSC)
+        vsw = place([P, T], F32, "vsw", AT_VSW)
+        qraw = [place([P, PACK, NQ], F32, "qraw%d" % b, AT_QRAW[b])[:] for b in range(B)]
         vwin = {}
         for b in range(B):
             for j in range(PLANES):
-                vwin[b, j] = place([P, (b + 1) * SEG], F32, "vwin%d%d" % (b, j), AT_VWIN.get((b, j)))
-        qraw = [place([P, PACK, NQ], F32, "qraw%d" % b, AT_QRAW[b]) for b in range(B)]
+                vwin[b, j] = place([P, (b + 1) * SEG], F32, "vwin%d%d" % (b, j), AT_VWIN[b, j])
         ident = place([P, P], F32, "ident")
         warm = sb.tile([P, 8], F32, name="warm")
         warm2 = sb.tile([P, 8], F32, name="warm2")
@@ -88,16 +90,15 @@ def tile_attend_silu_seg_kernel(tc, qT, k_words, k_scales, vT, vs, offs, out):
             nc.sync.dma_start(out=kw[:, seg(b)], in_=words[:, seg(b)])
 
         def load_q(b):
-            nc.sync.dma_start(out=qraw[b][:], in_=qT[b].rearrange("(p j) n -> p j n", j=PACK))
+            nc.sync.dma_start(out=qraw[b], in_=qT[b].rearrange("(p j) n -> p j n", j=PACK))
 
         nc.sync.dma_start(offsets[:], offs)
-        for b in range(B):
-            nc.scalar.dma_start(out=vsw[P - 1 : P, seg(b)], in_=vs[0:1, seg(b)])
+        nc.scalar.dma_start(out=vsw[P - 1 : P, :], in_=vs[0:1, :])
         nc.scalar.activation(warm2[:], warm[:], ACT.Silu)
         load_k(0)
+        load_q(0)
         for r in range(4):
             nc.sync.dma_start(out=ksc[r:P:32, :].bitcast(I32), in_=scale_rows[r:16:4, :])
-        load_q(0)
         load_v(0, 0)
         load_q(1)
         load_k(1)
@@ -108,38 +109,42 @@ def tile_attend_silu_seg_kernel(tc, qT, k_words, k_scales, vT, vs, offs, out):
         def lst(b, first=0, last=N):
             return offsets[:, b * COLS + first // 16 : b * COLS + last // 16]
 
-        kg, ksg, qb, vg, vt, vst, vq = {}, {}, {}, {}, {}, {}, {}
-        held, pw, wq = {}, {}, {}
-        wc, wsc, qc, qsc, vc, vsc = {}, {}, {}, {}, {}, {}
+        kg, qb, vg, vt, vst, vq = {}, {}, {}, {}, {}, {}
+        qc, qsc, vc, vsc, z, ksg = {}, {}, {}, {}, {}, {}
 
-        def gather_vs(b):
+        def gather(engine, dense, listed):
+            if engine == "vector":
+                nc.vector.tensor_copy(dense, listed)
+            else:
+                nc.scalar.activation(dense, listed, ACT.Copy)
+
+        def gather_vs(b, engine):
             listed = place([P, N], F32, "vsg%d" % b)
-            nc.scalar.activation(listed[:], vsw[:, 0 : (b + 1) * SEG].indirect(lst(b)), ACT.Copy)
+            gather(engine, listed[:], vsw[:, 0 : (b + 1) * SEG].indirect(lst(b)))
             vst[b] = ps.tile([P, PACK, P], F32, name="vst%d" % b)
             for t in range(PACK):
                 nc.tensor.transpose(vst[b][:, t, :], listed[:, t:N:PACK], ident[:])
 
-        def hold_vs(b, at):
-            held[b] = place([P, 1, PACK], F32, "held%d" % b, at)
-            nc.scalar.copy(held[b][:], token_scales(b))
+        def token_scales(b):
+            return vst[b][:, :, P - 1 : P].rearrange("p t o -> p o t")
 
-        def gather_ks(b, at=None):
+        def hold_vs(b, copy, at=None):
+            column = place([P, 1, PACK], F32, "held%d" % b, at)
+            copy(column[:], token_scales(b))
+            return column[:]
+
+        def gather_ks(b, at):
             ksg[b] = place([P, PACK, P], U8, "ksg%d" % b, at)
-            nc.vector.tensor_copy(dealt(ksg[b][:]), ksc[:].indirect(lst(b)))
+            nc.vector.tensor_copy(ksg[b][:].rearrange("x t p -> x p t"), ksc[:].indirect(lst(b)))
 
-        def gather_k(b, at=None):
+        def gather_k(b, at):
             kg[b] = place([P, PACK, P], U32, "kg%d" % b, at)
-            nc.vector.tensor_copy(dealt(kg[b][:]), kw[:, 0 : (b + 1) * SEG].bitcast(U32).indirect(lst(b)))
+            nc.vector.tensor_copy(kg[b][:].rearrange("x t p -> x p t"), kw[:, 0 : (b + 1) * SEG].bitcast(U32).indirect(lst(b)))
 
         def gather_v(b, j, who, at):
             vg[b, j] = place([P, N], BF16, "vg%d%d" % (b, j), at)
             for engine, first, last in who:
-                part = vg[b, j][:, first:last]
-                listed = vwin[b, j][:].indirect(lst(b, first, last))
-                if engine == "vector":
-                    nc.vector.tensor_copy(part, listed)
-                else:
-                    nc.scalar.activation(part, listed, ACT.Copy)
+                gather(engine, vg[b, j][:, first:last], vwin[b, j][:].indirect(lst(b, first, last)))
 
         def turn_v(b, j, tag):
             vt[b, j] = ps.tile([P, 2, P], F32, name="vt%d%d" % (b, j), tag=tag)
@@ -147,29 +152,31 @@ def tile_attend_silu_seg_kernel(tc, qT, k_words, k_scales, vT, vs, offs, out):
             for u in range(2):
                 nc.tensor.transpose(vt[b, j][:, u, :], pairs[:, u : N // 2 : 2], ident[:])
 
-        def empty_v(b, j, at=None, parts=1):
+        def empty_v(b, j, copy, at=None, parts=1):
             vq[b, j] = place([P, P * PACK], BF16, "vq%d%d" % (b, j), at)
-            words = vq[b, j][:].bitcast(F32).rearrange("p (e u) -> p e u", u=2)
+            pair_words = vq[b, j][:].bitcast(F32).rearrange("p (e u) -> p e u", u=2)
             for part in cuts(parts):
-                nc.scalar.copy(words[:, part, :], vt[b, j][:].rearrange("p u e -> p e u")[:, part, :])
+                copy(pair_words[:, part, :], vt[b, j][:].rearrange("p u e -> p e u")[:, part, :])
 
         def quantise(codes, scales, values):
             nc.vector.quantize_mx(out=codes.bitcast(FP8X4), scales=scales, in_=values)
 
-        def cast_q(b):
-            qb[b] = place([P, NQ, PACK], BF16, "qb%d" % b)
-            nc.gpsimd.tensor_copy(qb[b][:], qraw[b][:].rearrange("p j n -> p n j"))
+        def cast_q(b, who, at=None, rows=NQ):
+            room = place([P, rows, PACK], BF16, "qb%d" % b, at)
+            qb[b] = room[:, 0:NQ, :]
+            for copy, part in who:
+                copy(qb[b][:, part, :], qraw[b].rearrange("p j n -> p n j")[:, part, :])
 
-        def quant_q(b):
-            qc[b] = place([P, NQ], U32, "qc%d" % b)
+        def quant_q(b, at):
+            qc[b] = place([P, NQ], U32, "qc%d" % b, at)
             qsc[b] = place([P, NQ], U8, "qsc%d" % b)
-            quantise(qc[b][:], qsc[b][:], qb[b][:].rearrange("p n j -> p (n j)"))
+            quantise(qc[b][:], qsc[b][:], qb[b].rearrange("p n j -> p (n j)"))
 
-        def scores(b, parts):
-            z = ps.tile([P, PACK, NQ], F32, name="z%d" % b)
+        def scores(b, tag):
+            z[b] = ps.tile([P, PACK, NQ], F32, name="z%d" % b, tag=tag)
             for t in range(PACK):
                 nc.tensor.matmul_mx(
-                    out=z[:, t, :],
+                    out=z[b][:, t, :],
                     lhsT=kg[b][:, t, :].bitcast(FP8X4),
                     lhsT_scale=ksg[b][:, t, :],
                     rhs=qc[b][:].bitcast(FP8X4),
@@ -177,20 +184,16 @@ def tile_attend_silu_seg_kernel(tc, qT, k_words, k_scales, vT, vs, offs, out):
                     start=True,
                     stop=True,
                 )
-            for h, (at, rows, part) in enumerate(parts):
-                room = place([P, rows, PACK], F32, "pw%d%d" % (b, h), at)
-                pw[b, h] = room[:, 0 : part.stop - part.start, :]
-                scored = z[:, :, part]
-                nc.scalar.activation(pw[b, h], scored.rearrange("p t q -> p q t"), ACT.Silu)
 
-        def token_scales(b):
-            return vst[b][:, :, P - 1 : P].rearrange("p t o -> p o t")
+        def silu(b, part, p):
+            nc.scalar.activation(p, z[b][:, :, part].rearrange("p t q -> p q t"), ACT.Silu)
+            return p
 
-        def weigh(engine, weights, silu, scales):
-            engine.tensor_tensor(weights, silu, scales.to_broadcast(list(weights.shape)), MULT)
+        def weigh(engine, weights, p, scales):
+            engine.tensor_tensor(weights, p, scales.to_broadcast(list(weights.shape)), MULT)
 
-        def quant_w(b):
-            quantise(wc[b][:], wsc[b][:], wq[b][:].rearrange("p q t -> p (q t)"))
+        def quant_w(b, weights, part):
+            quantise(wc[b][:, part], wsc[b][:, part], weights.rearrange("p q t -> p (q t)"))
 
         def quant_v(b, j, at=None, parts=1):
             vc[b, j] = place([P, P], U32, "vc%d%d" % (b, j), at)
@@ -211,54 +214,60 @@ def tile_attend_silu_seg_kernel(tc, qT, k_words, k_scales, vT, vs, offs, out):
             )
             return y
 
-        for b in range(B):
-            wq[b] = place([P, NQ, PACK], BF16, "wq%d" % b)
-            wc[b] = place([P, NQ], U32, "wc%d" % b, (None, AT_LATE)[b])
-            wsc[b] = place([P, NQ], U8, "wsc%d" % b)
-        res = [place([P, DV], F32, "res%d" % b, (AT_VG11, None)[b]) for b in range(B)]
+        wq0 = place([P, NQ, PACK], BF16, "wq0")
+        wq1 = place([P, NQ, PACK], BF16, "wq1")
+        wc = [place([P, NQ], U32, "wc%d" % b, AT_LATE + 512 * b) for b in range(B)]
+        wsc = [place([P, NQ], U8, "wsc%d" % b) for b in range(B)]
+        res = [place([P, DV], F32, "res%d" % b, (AT_LATE + 3072, None)[b]) for b in range(B)]
         low, high = cuts(2)
         early, rest = slice(0, EARLY), slice(EARLY, NQ)
 
-        gather_k(0)
-        gather_vs(0)
-        gather_vs(1)
-        gather_ks(0)
-        cast_q(0)
-        quant_q(0)
-        gather_ks(1, AT_QRAW[0] + 64)
-        gather_v(0, 0, [("scalar", 0, N)], AT_VG00)
-        hold_vs(0, AT_VWIN[0, 0])
-        hold_vs(1, AT_VWIN[0, 0] + 64)
-        scores(0, [(AT_PW0, 3 * NQ, slice(0, NQ))])
+        whole = slice(0, NQ)
+        gather_k(0, None)
+        gather_ks(0, None)
+        gather_vs(0, "scalar")
+        gather_vs(1, "scalar")
+        cast_q(0, [(nc.gpsimd.tensor_copy, whole)])
+        quant_q(0, None)
+        gather_ks(1, AT_QRAW[0])
+        scores(0, "z0")
+        gather_v(0, 0, [("scalar", 0, N)], AT_VSW + 512)
         turn_v(0, 0, "vt00")
-        empty_v(0, 0)
-        cast_q(1)
-        quant_q(1)
+        held0 = hold_vs(0, nc.scalar.copy, AT_V00)
+        held1 = hold_vs(1, nc.scalar.copy, AT_V00 + 256)
+        p0 = place([P, NQ, PACK], F32, "p0", AT_P0)
+        silu(0, whole, p0[:])
+        empty_v(0, 0, nc.scalar.copy)
+        cast_q(1, [(nc.gpsimd.tensor_copy, whole)])
+        quant_q(1, None)
         gather_k(1, AT_QRAW[1])
-        weigh(nc.gpsimd, wq[0][:, low, :], pw[0, 0][:, low, :], held[0][:])
-        weigh(nc.vector, wq[0][:, high, :], pw[0, 0][:, high, :], token_scales(0))
-        gather_v(0, 1, [("scalar", 0, N)], AT_VG00 - 960)
-        quant_v(0, 0)
-        quant_w(0)
+        quant_v(0, 0, AT_VC00)
+        scores(1, "z1")
+        weigh(nc.gpsimd, wq0[:], p0[:], held0)
+        gather_v(0, 1, [("scalar", 0, N)], AT_VG01)
+        p1a = place([P, EARLY, PACK], F32, "p1a", AT_V01)
+        p1b = place([P, NQ - EARLY, PACK], F32, "p1b", AT_V01 + 512)
+        silu(1, early, p1a[:])
+        silu(1, rest, p1b[:])
+        turn_v(0, 1, "vt01")
+        weigh(nc.gpsimd, wq1[:, early, :], p1a[:], held1)
+        weigh(nc.gpsimd, wq1[:, rest, :], p1b[:], held1)
         gather_v(1, 0, [("vector", 0, N)], AT_VG10)
-        scores(1, [(AT_PW1, EARLY, early), (AT_PW1 + 512, NQ - EARLY, rest)])
-        turn_v(0, 1, "vt00")
-        empty_v(0, 1, AT_VG11 + 1024)
-        y00 = product(0, 0, "y00")
-        turn_v(1, 0, "vt10")
-        weigh(nc.gpsimd, wq[1][:, early, :], pw[1, 0], held[1][:])
-        weigh(nc.gpsimd, wq[1][:, rest, :], pw[1, 1], held[1][:])
-        gather_v(1, 1, [("vector", 0, N // 2), ("scalar", N // 2, N)], AT_VG11)
+        turn_v(1, 0, "z1")
+        gather_v(1, 1, [("vector", 0, N // 2), ("scalar", N // 2, N)], AT_VG01)
         turn_v(1, 1, "vt11")
-        empty_v(1, 0, AT_LATE + 2048)
-        empty_v(1, 1, None, 2)
-        quant_v(0, 1, AT_LATE + 1024)
-        quant_w(1)
-        quant_v(1, 0)
-        quant_v(1, 1, None, 2)
+        empty_v(0, 1, nc.scalar.copy, AT_LATE + 4096)
+        empty_v(1, 0, nc.scalar.copy, AT_LATE + 2048)
+        empty_v(1, 1, nc.scalar.copy, None, 2)
+        quant_w(0, wq0[:], whole)
+        quant_v(0, 1)
+        quant_w(1, wq1[:], whole)
+        quant_v(1, 0, AT_V01 + 512)
+        quant_v(1, 1, AT_V01 + 1024, 2)
+        y00 = product(0, 0, "vt00")
         y01 = product(0, 1, "vst0")
         y10 = product(1, 0, "z0")
-        last = [product(1, 1, tag, part) for tag, part in zip(("z1", "vst1"), cuts(2))]
+        last = [product(1, 1, tag, part) for tag, part in zip(("y11a", "vst1"), cuts(2))]
         nc.scalar.activation(res[0][:, 0:P], y00[:], ACT.Copy, scale=1.0 / 16.0)
         nc.scalar.activation(res[0][:, P:DV], y01[:], ACT.Copy, scale=1.0 / 16.0)
         nc.sync.dma_start(out=out[0], in_=res[0][:])

@@ -23,7 +23,6 @@ SEG = T // B
 COLS = N // 16
 PLANES = DV // P
 ALIGN = 256
-EARLY = NQ // 4
 
 AT_KSC = 0
 AT_KW = AT_KSC + T
@@ -172,11 +171,12 @@ def tile_attend_silu_seg_kernel(tc, qT, k_words, k_scales, vT, vs, offs, out):
             qsc[b] = place([P, NQ], U8, "qsc%d" % b)
             quantise(qc[b][:], qsc[b][:], qb[b].rearrange("p n j -> p (n j)"))
 
-        def scores(b, tag):
-            z[b] = ps.tile([P, PACK, NQ], F32, name="z%d" % b, tag=tag)
+        def scores(b, tags):
+            share = PACK // len(tags)
+            z[b] = [ps.tile([P, share, NQ], F32, name="z%d_%d" % (b, h), tag=tag) for h, tag in enumerate(tags)]
             for t in range(PACK):
                 nc.tensor.matmul_mx(
-                    out=z[b][:, t, :],
+                    out=z[b][t // share][:, t % share, :],
                     lhsT=kg[b][:, t, :].bitcast(FP8X4),
                     lhsT_scale=ksg[b][:, t, :],
                     rhs=qc[b][:].bitcast(FP8X4),
@@ -184,10 +184,6 @@ def tile_attend_silu_seg_kernel(tc, qT, k_words, k_scales, vT, vs, offs, out):
                     start=True,
                     stop=True,
                 )
-
-        def silu(b, part, p):
-            nc.scalar.activation(p, z[b][:, :, part].rearrange("p t q -> p q t"), ACT.Silu)
-            return p
 
         def weigh(engine, weights, p, scales):
             engine.tensor_tensor(weights, p, scales.to_broadcast(list(weights.shape)), MULT)
@@ -215,12 +211,11 @@ def tile_attend_silu_seg_kernel(tc, qT, k_words, k_scales, vT, vs, offs, out):
             return y
 
         wq0 = place([P, NQ, PACK], BF16, "wq0")
-        wq1 = place([P, NQ, PACK], BF16, "wq1")
+        wq1 = [place([P, NQ // 2, PACK], BF16, "wq1_%d" % h, (None, AT_LATE + 5120)[h]) for h in range(2)]
         wc = [place([P, NQ], U32, "wc%d" % b, AT_LATE + 512 * b) for b in range(B)]
         wsc = [place([P, NQ], U8, "wsc%d" % b) for b in range(B)]
         res = [place([P, DV], F32, "res%d" % b, (AT_LATE + 3072, None)[b]) for b in range(B)]
         low, high = cuts(2)
-        early, rest = slice(0, EARLY), slice(EARLY, NQ)
 
         whole = slice(0, NQ)
         gather_k(0, None)
@@ -230,40 +225,41 @@ def tile_attend_silu_seg_kernel(tc, qT, k_words, k_scales, vT, vs, offs, out):
         cast_q(0, [(nc.gpsimd.tensor_copy, whole)])
         quant_q(0, None)
         gather_ks(1, AT_QRAW[0])
-        scores(0, "z0")
+        scores(0, ["z0"])
         gather_v(0, 0, [("scalar", 0, N)], AT_VSW + 512)
         turn_v(0, 0, "vt00")
         held0 = hold_vs(0, nc.scalar.copy, AT_V00)
         held1 = hold_vs(1, nc.scalar.copy, AT_V00 + 256)
         p0 = place([P, NQ, PACK], F32, "p0", AT_P0)
-        silu(0, whole, p0[:])
+        nc.scalar.activation(p0[:], z[0][0][:].rearrange("p t q -> p q t"), ACT.Silu)
         empty_v(0, 0, nc.scalar.copy)
         cast_q(1, [(nc.gpsimd.tensor_copy, whole)])
         quant_q(1, None)
         gather_k(1, AT_QRAW[1])
-        quant_v(0, 0, AT_VC00)
-        scores(1, "z1")
+        scores(1, ["vst0", "z1"])
         weigh(nc.gpsimd, wq0[:], p0[:], held0)
         gather_v(0, 1, [("scalar", 0, N)], AT_VG01)
-        p1a = place([P, EARLY, PACK], F32, "p1a", AT_V01)
-        p1b = place([P, NQ - EARLY, PACK], F32, "p1b", AT_V01 + 512)
-        silu(1, early, p1a[:])
-        silu(1, rest, p1b[:])
+        p1 = place([P, PACK, NQ], F32, "p1", AT_V01)
+        for h in range(2):
+            nc.scalar.activation(p1[:, 2 * h : 2 * h + 2, :], z[1][h][:], ACT.Silu)
+        p1_by_query = p1[:].rearrange("p t q -> p q t")
         turn_v(0, 1, "vt01")
-        weigh(nc.gpsimd, wq1[:, early, :], p1a[:], held1)
-        weigh(nc.gpsimd, wq1[:, rest, :], p1b[:], held1)
-        gather_v(1, 0, [("vector", 0, N)], AT_VG10)
+        weigh(nc.gpsimd, wq1[0][:], p1_by_query[:, low, :], held1)
+        gather_v(1, 0, [("vector", 0, N)], None)
         turn_v(1, 0, "z1")
-        gather_v(1, 1, [("vector", 0, N // 2), ("scalar", N // 2, N)], AT_VG01)
+        gather_v(1, 1, [("vector", 0, N // 2), ("scalar", N // 2, N)], AT_QRAW[1])
         turn_v(1, 1, "vt11")
         empty_v(0, 1, nc.scalar.copy, AT_LATE + 4096)
         empty_v(1, 0, nc.scalar.copy, AT_LATE + 2048)
         empty_v(1, 1, nc.scalar.copy, None, 2)
+        weigh(nc.vector, wq1[1][:], p1_by_query[:, high, :], token_scales(1))
         quant_w(0, wq0[:], whole)
+        quant_v(0, 0, AT_LATE + 1024)
         quant_v(0, 1)
-        quant_w(1, wq1[:], whole)
-        quant_v(1, 0, AT_V01 + 512)
-        quant_v(1, 1, AT_V01 + 1024, 2)
+        quant_w(1, wq1[0][:], low)
+        quant_w(1, wq1[1][:], high)
+        quant_v(1, 0)
+        quant_v(1, 1, None, 2)
         y00 = product(0, 0, "vt00")
         y01 = product(0, 1, "vst0")
         y10 = product(1, 0, "z0")

@@ -60,7 +60,8 @@ def tile_attend_silu_seg_kernel(tc, qT, k_words, k_scales, vT, vs, offs, out):
         kw = place([P, T], I32, "kw", AT_KW)
         ksc = place([P, T], U8, "ksc", AT_KSC)
         vsw = place([P, T], F32, "vsw", AT_VSW)
-        qraw = [place([P, PACK, NQ], F32, "qraw%d" % b, AT_QRAW[b])[:] for b in range(B)]
+        qboth = place([P, B, PACK, NQ], F32, "qraw", AT_QRAW[0])
+        qraw = [qboth[:, b, :, :] for b in range(B)]
         vwin = {}
         for b in range(B):
             for j in range(PLANES):
@@ -88,18 +89,14 @@ def tile_attend_silu_seg_kernel(tc, qT, k_words, k_scales, vT, vs, offs, out):
         def load_k(b):
             nc.sync.dma_start(out=kw[:, seg(b)], in_=words[:, seg(b)])
 
-        def load_q(b):
-            nc.sync.dma_start(out=qraw[b], in_=qT[b].rearrange("(p j) n -> p j n", j=PACK))
-
         nc.sync.dma_start(offsets[:], offs)
         nc.scalar.dma_start(out=vsw[P - 1 : P, :], in_=vs[0:1, :])
         nc.scalar.activation(warm2[:], warm[:], ACT.Silu)
         load_k(0)
-        load_q(0)
+        nc.sync.dma_start(out=qboth[:], in_=qT.rearrange("b (p j) n -> p b j n", j=PACK))
         for r in range(4):
             nc.sync.dma_start(out=ksc[r:P:32, :].bitcast(I32), in_=scale_rows[r:16:4, :])
         load_v(0, 0)
-        load_q(1)
         load_k(1)
         load_v(0, 1)
         load_v(1, 0)
@@ -108,8 +105,8 @@ def tile_attend_silu_seg_kernel(tc, qT, k_words, k_scales, vT, vs, offs, out):
         def lst(b, first=0, last=N):
             return offsets[:, b * COLS + first // 16 : b * COLS + last // 16]
 
-        kg, qb, vg, vt, vst, vq = {}, {}, {}, {}, {}, {}
-        qc, qsc, vc, vsc, z, ksg = {}, {}, {}, {}, {}, {}
+        kg, vg, vt, vst, vq = {}, {}, {}, {}, {}
+        vc, vsc, z, ksg = {}, {}, {}, {}
 
         def gather(engine, dense, listed):
             if engine == "vector":
@@ -160,16 +157,8 @@ def tile_attend_silu_seg_kernel(tc, qT, k_words, k_scales, vT, vs, offs, out):
         def quantise(codes, scales, values):
             nc.vector.quantize_mx(out=codes.bitcast(FP8X4), scales=scales, in_=values)
 
-        def cast_q(b, who, at=None, rows=NQ):
-            room = place([P, rows, PACK], BF16, "qb%d" % b, at)
-            qb[b] = room[:, 0:NQ, :]
-            for copy, part in who:
-                copy(qb[b][:, part, :], qraw[b].rearrange("p j n -> p n j")[:, part, :])
-
-        def quant_q(b, at):
-            qc[b] = place([P, NQ], U32, "qc%d" % b, at)
-            qsc[b] = place([P, NQ], U8, "qsc%d" % b)
-            quantise(qc[b][:], qsc[b][:], qb[b].rearrange("p n j -> p (n j)"))
+        def cast_q(copy, b, part):
+            copy(qb[:, b, part, :], qraw[b].rearrange("p j n -> p n j")[:, part, :])
 
         def scores(b, tags):
             share = PACK // len(tags)
@@ -179,8 +168,8 @@ def tile_attend_silu_seg_kernel(tc, qT, k_words, k_scales, vT, vs, offs, out):
                     out=z[b][t // share][:, t % share, :],
                     lhsT=kg[b][:, t, :].bitcast(FP8X4),
                     lhsT_scale=ksg[b][:, t, :],
-                    rhs=qc[b][:].bitcast(FP8X4),
-                    rhs_scale=qsc[b][:],
+                    rhs=qc[:, b, :].bitcast(FP8X4),
+                    rhs_scale=qsc[:, b, :],
                     start=True,
                     stop=True,
                 )
@@ -216,29 +205,31 @@ def tile_attend_silu_seg_kernel(tc, qT, k_words, k_scales, vT, vs, offs, out):
         wsc = [place([P, NQ], U8, "wsc%d" % b) for b in range(B)]
         res = [place([P, DV], F32, "res%d" % b, (AT_LATE + 3072, None)[b]) for b in range(B)]
         low, high = cuts(2)
+        qb = place([P, B, NQ, PACK], BF16, "qb", AT_VSW + 2048)
+        qc = place([P, B, NQ], U32, "qc")
+        qsc = place([P, B, NQ], U8, "qsc")
 
         whole = slice(0, NQ)
         gather_k(0, None)
         gather_ks(0, None)
         gather_vs(0, "scalar")
         gather_vs(1, "scalar")
-        cast_q(0, [(nc.gpsimd.tensor_copy, whole)])
-        quant_q(0, None)
+        cast_q(nc.gpsimd.tensor_copy, 0, whole)
+        cast_q(nc.scalar.copy, 1, whole)
+        quantise(qc[:].rearrange("p b n -> p (b n)"), qsc[:].rearrange("p b n -> p (b n)"), qb[:].rearrange("p b n j -> p (b n j)"))
+        held0 = hold_vs(0, nc.scalar.copy, AT_VSW)
+        held1 = hold_vs(1, nc.scalar.copy, AT_VSW + 256)
         gather_ks(1, AT_QRAW[0])
         scores(0, ["z0"])
         gather_v(0, 0, [("scalar", 0, N)], AT_VSW + 512)
         turn_v(0, 0, "vt00")
-        held0 = hold_vs(0, nc.scalar.copy, AT_V00)
-        held1 = hold_vs(1, nc.scalar.copy, AT_V00 + 256)
         p0 = place([P, NQ, PACK], F32, "p0", AT_P0)
         nc.scalar.activation(p0[:], z[0][0][:].rearrange("p t q -> p q t"), ACT.Silu)
-        empty_v(0, 0, nc.scalar.copy)
-        cast_q(1, [(nc.gpsimd.tensor_copy, whole)])
-        quant_q(1, None)
         gather_k(1, AT_QRAW[1])
         scores(1, ["vst0", "z1"])
         weigh(nc.gpsimd, wq0[:], p0[:], held0)
-        gather_v(0, 1, [("scalar", 0, N)], AT_VG01)
+        gather_v(0, 1, [("vector", 0, N // 4), ("scalar", N // 4, N)], AT_VG01)
+        empty_v(0, 0, nc.scalar.copy, AT_V01 + 2048)
         p1 = place([P, PACK, NQ], F32, "p1", AT_V01)
         for h in range(2):
             nc.scalar.activation(p1[:, 2 * h : 2 * h + 2, :], z[1][h][:], ACT.Silu)

from contextlib import ExitStack

import concourse.mybir as mybir
from concourse.masks import make_identity

B, N, T, D, DV, NQ = 2, 512, 2048, 512, 256, 128
FLOPS = 2 * B * NQ * N * (D + DV)
BYTES = 4 * B * D * NQ + 4 * 128 * T + 16 * T + 4 * DV * T + 4 * T + 2 * 128 * 64 + 4 * B * NQ * DV

F32 = mybir.dt.float32
BF16 = mybir.dt.bfloat16
I32 = mybir.dt.int32
U32 = mybir.dt.uint32
U16 = mybir.dt.uint16
U8 = mybir.dt.uint8
FP8X4 = mybir.dt.float8_e4m3fn_x4
ACT = mybir.ActivationFunctionType
MULT = mybir.AluOpType.mult

P = 128
PACK = 4
SEG = T // B
COLS = N // 16
PLANES = DV // P
ALIGN = 256

AT_KSC = 0
AT_KW = AT_KSC + T
AT_V10 = AT_KW + 4 * T
AT_V11 = AT_V10 + 4 * T
AT_VSW = AT_V11 + 4 * T
AT_V00 = AT_VSW + 4 * T
AT_V01 = AT_V00 + 4 * SEG
AT_QRAW = [AT_V01 + 4 * SEG, AT_V01 + 4 * SEG + 4 * PACK * NQ]
AT_VC00 = AT_KW
AT_VG10 = AT_KW + 512
AT_VG01 = AT_VSW + 512
AT_P0 = AT_V00 + 1024
AT_VWIN = {(0, 0): AT_V00, (0, 1): AT_V01, (1, 0): AT_V10, (1, 1): AT_V11}
AT_LATE = AT_V11


def cuts(parts):
    return [slice(h * P // parts, (h + 1) * P // parts) for h in range(parts)]


def tile_attend_silu_seg_kernel(tc, qT, k_words, k_scales, vT, vs, offs, out):
    nc = tc.nc
    with ExitStack() as ctx:
        sb = ctx.enter_context(tc.tile_pool(name="sb", bufs=1))
        shared = ctx.enter_context(tc.tile_pool(name="shared", bufs=1))
        ps = ctx.enter_context(tc.psum_pool(name="ps", bufs=1))

        def place(shape, dtype, name, at=None):
            if at is None:
                return sb.tile(shape, dtype, name=name, align_bytes=64)
            return shared.tile(shape, dtype, name=name, offset=at, align_bytes=ALIGN)

        offsets = sb.tile([P, B * COLS], U16, name="offsets")
        kw = place([P, T], I32, "kw", AT_KW)
        ksc = place([P, T], U8, "ksc", AT_KSC)
        vsw = place([P, T], F32, "vsw", AT_VSW)
        qboth = place([P, B, PACK, NQ], F32, "qraw", AT_QRAW[0])
        qraw = [qboth[:, b, :, :] for b in range(B)]
        vwin = {}
        for b in range(B):
            for j in range(PLANES):
                vwin[b, j] = place([P, (b + 1) * SEG], F32, "vwin%d%d" % (b, j), AT_VWIN[b, j])
        ident = place([P, P], F32, "ident")
        warm = sb.tile([P, 8], F32, name="warm")
        warm2 = sb.tile([P, 8], F32, name="warm2")

        nc.vector.memset(ksc[:, 0:SEG].bitcast(I32), 0)
        nc.gpsimd.memset(ksc[:, SEG:T].bitcast(I32), 0)
        nc.vector.memset(warm[:], 0.0)
        nc.vector.memset(vsw[0 : P - 1, 0:SEG], 0.0)
        nc.gpsimd.memset(vsw[0 : P - 1, SEG:T], 0.0)
        make_identity(nc, ident[:])

        words = k_words[0].rearrange("p n t -> p (n t)").bitcast(I32)
        scale_rows = k_scales[0].bitcast(I32)

        def seg(b):
            return slice(b * SEG, (b + 1) * SEG)

        def load_v(b, j):
            nc.sync.dma_start(out=vwin[b, j][:, seg(b)], in_=vT[j * P : (j + 1) * P, seg(b)])

        def load_k(b):
            nc.sync.dma_start(out=kw[:, seg(b)], in_=words[:, seg(b)])

        nc.sync.dma_start(offsets[:], offs)
        nc.scalar.dma_start(out=vsw[P - 1 : P, :], in_=vs[0:1, :])
        nc.scalar.activation(warm2[:], warm[:], ACT.Silu)
        load_k(0)
        nc.sync.dma_start(out=qboth[:], in_=qT.rearrange("b (p j) n -> p b j n", j=PACK))
        for r in range(4):
            nc.sync.dma_start(out=ksc[r:P:32, :].bitcast(I32), in_=scale_rows[r:16:4, :])
        load_v(0, 0)
        load_k(1)
        load_v(0, 1)
        load_v(1, 0)
        load_v(1, 1)

        def lst(b, first=0, last=N):
            return offsets[:, b * COLS + first // 16 : b * COLS + last // 16]

        kg, vg, vt, vst, vq = {}, {}, {}, {}, {}
        vc, vsc, z, ksg = {}, {}, {}, {}

        def gather(engine, dense, listed):
            if engine == "vector":
                nc.vector.tensor_copy(dense, listed)
            else:
                nc.scalar.activation(dense, listed, ACT.Copy)

        def gather_vs(b, engine):
            listed = place([P, N], F32, "vsg%d" % b)
            gather(engine, listed[:], vsw[:, 0 : (b + 1) * SEG].indirect(lst(b)))
            vst[b] = ps.tile([P, PACK, P], F32, name="vst%d" % b)
            for t in range(PACK):
                nc.tensor.transpose(vst[b][:, t, :], listed[:, t:N:PACK], ident[:])

        def token_scales(b):
            return vst[b][:, :, P - 1 : P].rearrange("p t o -> p o t")

        def hold_vs(b, copy, at=None):
            column = place([P, 1, PACK], F32, "held%d" % b, at)
            copy(column[:], token_scales(b))
            return column[:]

        def gather_ks(b, at):
            ksg[b] = place([P, PACK, P], U8, "ksg%d" % b, at)
            nc.vector.tensor_copy(ksg[b][:].rearrange("x t p -> x p t"), ksc[:].indirect(lst(b)))

        def gather_k(b, at):
            kg[b] = place([P, PACK, P], U32, "kg%d" % b, at)
            nc.vector.tensor_copy(kg[b][:].rearrange("x t p -> x p t"), kw[:, 0 : (b + 1) * SEG].bitcast(U32).indirect(lst(b)))

        def gather_v(b, j, who, at):
            vg[b, j] = place([P, N], BF16, "vg%d%d" % (b, j), at)
            for engine, first, last in who:
                gather(engine, vg[b, j][:, first:last], vwin[b, j][:].indirect(lst(b, first, last)))

        def turn_v(b, j, tag):
            vt[b, j] = ps.tile([P, 2, P], F32, name="vt%d%d" % (b, j), tag=tag)
            pairs = vg[b, j][:].bitcast(F32)
            for u in range(2):
                nc.tensor.transpose(vt[b, j][:, u, :], pairs[:, u : N // 2 : 2], ident[:])

        def empty_v(b, j, copy, at=None, parts=1):
            vq[b, j] = place([P, P * PACK], BF16, "vq%d%d" % (b, j), at)
            pair_words = vq[b, j][:].bitcast(F32).rearrange("p (e u) -> p e u", u=2)
            for part in cuts(parts):
                copy(pair_words[:, part, :], vt[b, j][:].rearrange("p u e -> p e u")[:, part, :])

        def quantise(codes, scales, values):
            nc.vector.quantize_mx(out=codes.bitcast(FP8X4), scales=scales, in_=values)

        def cast_q(copy, b, part):
            copy(qb[:, b, part, :], qraw[b].rearrange("p j n -> p n j")[:, part, :])

        def scores(b, tags):
            share = PACK // len(tags)
            z[b] = [ps.tile([P, share, NQ], F32, name="z%d_%d" % (b, h), tag=tag) for h, tag in enumerate(tags)]
            for t in range(PACK):
                nc.tensor.matmul_mx(
                    out=z[b][t // share][:, t % share, :],
                    lhsT=kg[b][:, t, :].bitcast(FP8X4),
                    lhsT_scale=ksg[b][:, t, :],
                    rhs=qc[:, b, :].bitcast(FP8X4),
                    rhs_scale=qsc[:, b, :],
                    start=True,
                    stop=True,
                )

        def weigh(engine, weights, p, scales):
            engine.tensor_tensor(weights, p, scales.to_broadcast(list(weights.shape)), MULT)

        def quant_w(b, weights, part):
            quantise(wc[b][:, part], wsc[b][:, part], weights.rearrange("p q t -> p (q t)"))

        def quant_v(b, j, at=None, parts=1):
            vc[b, j] = place([P, P], U32, "vc%d%d" % (b, j), at)
            vsc[b, j] = place([P, P], U8, "vsc%d%d" % (b, j))
            for part in cuts(parts):
                quantise(vc[b, j][:, part], vsc[b, j][:, part], vq[b, j][:, part.start * PACK : part.stop * PACK])

        def product(b, j, tag, part=slice(0, P)):
            y = ps.tile([P, part.stop - part.start], F32, name="y%d%d%d" % (b, j, part.start), tag=tag)
            nc.tensor.matmul_mx(
                out=y[:],
                lhsT=wc[b][:].bitcast(FP8X4),
                lhsT_scale=wsc[b][:],
                rhs=vc[b, j][:, part].bitcast(FP8X4),
                rhs_scale=vsc[b, j][:, part],
                start=True,
                stop=True,
            )
            return y

        wq0 = place([P, NQ, PACK], BF16, "wq0")
        wq1 = [place([P, NQ // 2, PACK], BF16, "wq1_%d" % h, (None, AT_LATE + 5120)[h]) for h in range(2)]
        wc = [place([P, NQ], U32, "wc%d" % b, AT_LATE + 512 * b) for b in range(B)]
        wsc = [place([P, NQ], U8, "wsc%d" % b) for b in range(B)]
        res = [place([P, DV], F32, "res%d" % b, (AT_LATE + 3072, None)[b]) for b in range(B)]
        low, high = cuts(2)
        qb = place([P, B, NQ, PACK], BF16, "qb", AT_VSW + 2048)
        qc = place([P, B, NQ], U32, "qc")
        qsc = place([P, B, NQ], U8, "qsc")

        whole = slice(0, NQ)
        gather_k(0, None)
        gather_ks(0, None)
        gather_vs(0, "scalar")
        gather_vs(1, "scalar")
        cast_q(nc.gpsimd.tensor_copy, 0, whole)
        cast_q(nc.scalar.copy, 1, whole)
        quantise(qc[:].rearrange("p b n -> p (b n)"), qsc[:].rearrange("p b n -> p (b n)"), qb[:].rearrange("p b n j -> p (b n j)"))
        held0 = hold_vs(0, nc.scalar.copy, AT_VSW)
        held1 = hold_vs(1, nc.scalar.copy, AT_VSW + 256)
        gather_ks(1, AT_QRAW[0])
        scores(0, ["z0"])
        gather_v(0, 0, [("scalar", 0, N)], AT_VSW + 512)
        turn_v(0, 0, "vt00")
        p0 = place([P, NQ, PACK], F32, "p0", AT_P0)
        nc.scalar.activation(p0[:], z[0][0][:].rearrange("p t q -> p q t"), ACT.Silu)
        gather_k(1, AT_QRAW[1])
        scores(1, ["vst0", "z1"])
        weigh(nc.gpsimd, wq0[:], p0[:], held0)
        gather_v(0, 1, [("vector", 0, N // 4), ("scalar", N // 4, N)], AT_VG01)
        empty_v(0, 0, nc.scalar.copy, AT_V01 + 2048)
        p1 = place([P, PACK, NQ], F32, "p1", AT_V01)
        for h in range(2):
            nc.scalar.activation(p1[:, 2 * h : 2 * h + 2, :], z[1][h][:], ACT.Silu)
        p1_by_query = p1[:].rearrange("p t q -> p q t")
        turn_v(0, 1, "vt01")
        weigh(nc.gpsimd, wq1[0][:], p1_by_query[:, low, :], held1)
        gather_v(1, 0, [("vector", 0, N)], None)
        turn_v(1, 0, "z1")
        gather_v(1, 1, [("vector", 0, N // 2), ("scalar", N // 2, N)], AT_QRAW[1])
        turn_v(1, 1, "vt11")
        empty_v(0, 1, nc.scalar.copy, AT_LATE + 4096)
        empty_v(1, 0, nc.scalar.copy, AT_LATE + 2048)
        empty_v(1, 1, nc.scalar.copy, None, 2)
        weigh(nc.vector, wq1[1][:], p1_by_query[:, high, :], token_scales(1))
        quant_w(0, wq0[:], whole)
        quant_v(0, 0, AT_LATE + 1024)
        quant_v(0, 1)
        quant_w(1, wq1[0][:], low)
        quant_w(1, wq1[1][:], high)
        quant_v(1, 0)
        quant_v(1, 1, None, 2)
        y00 = product(0, 0, "vt00")
        y01 = product(0, 1, "vst0")
        y10 = product(1, 0, "z0")
        last = [product(1, 1, tag, part) for tag, part in zip(("y11a", "vst1"), cuts(2))]
        nc.scalar.activation(res[0][:, 0:P], y00[:], ACT.Copy, scale=1.0 / 16.0)
        nc.scalar.activation(res[0][:, P:DV], y01[:], ACT.Copy, scale=1.0 / 16.0)
        nc.sync.dma_start(out=out[0], in_=res[0][:])
        nc.scalar.activation(res[1][:, 0:P], y10[:], ACT.Copy, scale=1.0 / 16.0)
        nc.sync.dma_start(out=out[1][:, 0:P], in_=res[1][:, 0:P])
        for y, part in zip(last, cuts(2)):
            nc.vector.tensor_scalar(res[1][:, P + part.start : P + part.stop], y[:], 1.0 / 16.0, None, MULT)
        nc.sync.dma_start(out=out[1][:, P:DV], in_=res[1][:, P:DV])
